import numpy as np
import ml_dtypes


def mxq(x, axis, fmt="e4m3"):
    dtype, down = {"e4m3": (ml_dtypes.float8_e4m3fn, 7), "e5m2": (ml_dtypes.float8_e5m2, 14)}[fmt]
    v = np.moveaxis(np.asarray(x, np.float32).astype(ml_dtypes.bfloat16).astype(np.float64), axis, -1)
    blocks = v.reshape(v.shape[:-1] + (-1, 32))
    amax = np.abs(blocks).max(-1, keepdims=True)
    byte = np.maximum(np.where(amax > 0, np.frexp(amax)[1] - 1 + 127, 0) - down, 1)
    scale = np.exp2(byte - 127.0)
    codes = (blocks / scale).astype(np.float32).astype(dtype).astype(np.float64)
    return np.moveaxis((codes * scale).reshape(v.shape), -1, axis)


WIDE = False


def mx_kscale(k):
    if not WIDE:
        return np.ones(k)
    levels = np.array([10, -10, 5, -5, 0])
    if k % 512:
        return np.exp2(np.random.permutation(np.resize(levels, k // 32))).repeat(32)
    a = np.empty((k // 512, 16))
    for p in range(k // 512):
        a[p, :8] = np.random.permutation(np.resize(levels, 8))
        for g in range(8):
            far = levels[np.abs(levels - a[p, g]) >= 10]
            a[p, g + 8] = far[np.random.randint(len(far))]
    return np.exp2(a.ravel()).repeat(32)


def f64(x):
    return np.asarray(x).astype(np.float64)


def striped(idx):
    return np.tile(idx.reshape(-1, 16).T, (8, 1)).astype(np.uint16)


def unstriped(offs):
    return offs[:16].T.reshape(-1).astype(np.int64)


E2M1 = np.array([0.0, 0.5, 1.0, 1.5, 2.0, 3.0, 4.0, 6.0, -0.0, -0.5, -1.0, -1.5, -2.0, -3.0, -4.0, -6.0])


def pack_weight(w, fmt):
    k, n = w.shape
    w = f64(np.asarray(w, np.float32).astype(ml_dtypes.bfloat16)).reshape(k // 32, 32, n)
    amax = np.abs(w).max(1)
    if fmt == "e4m3":
        byte = np.frexp(amax)[1] - 1 + 127 - 7
    else:
        mant, ex = np.frexp(amax / 6.0)
        byte = np.where(mant > 0.5, ex, ex - 1) + 127
    byte = np.clip(np.where(amax > 0, byte, 1), 1, 254)
    scaled = (w * np.exp2(127.0 - byte)[:, None, :]).reshape(k, n).astype(np.float32)
    by_word = np.ascontiguousarray(scaled.reshape(k // 512, 128, 4, n).transpose(0, 1, 3, 2))
    if fmt == "e4m3":
        words = by_word.astype(ml_dtypes.float8_e4m3fn).view(np.uint8)
    else:
        c = by_word.astype(ml_dtypes.float4_e2m1fn).view(np.uint8) & 0xF
        words = (c[..., 0::2] | (c[..., 1::2] << 4)).reshape(k // 512, 128, 2 * n)
    return np.ascontiguousarray(words), np.ascontiguousarray(byte.astype(np.uint8).reshape(k // 512, 16, n))


def unpack_weight(words, scales, fmt):
    g, _, n = scales.shape
    words = np.ascontiguousarray(words).reshape(g, 128, n, -1)
    if fmt == "e4m3":
        vals = words.view(ml_dtypes.float8_e4m3fn).astype(np.float64)
    else:
        nib = np.empty((g, 128, n, 4), np.uint8)
        nib[..., 0::2] = words & 0xF
        nib[..., 1::2] = words >> 4
        vals = E2M1[nib]
    vals = vals * np.repeat(np.exp2(scales.astype(np.float64) - 127.0), 8, axis=1)[..., None]
    return vals.transpose(0, 1, 3, 2).reshape(g * 512, n)


def gelu(v):
    return 0.5 * v * (1.0 + np.tanh(np.sqrt(2.0 / np.pi) * (v + 0.044715 * v**3)))


def bf(x):
    return np.asarray(x, np.float32).astype(ml_dtypes.bfloat16)


def planes(Y):
    n, m = Y.shape
    b = f64(bf(Y)).reshape(n // 32, 32, m)
    amax = np.abs(b).max(1)
    byte = np.clip(np.where(amax > 0, np.frexp(amax)[1] - 1 + 127 - 7, 1), 1, 254)
    codes = (b * np.exp2(127.0 - byte)[:, None, :]).reshape(n, m).astype(np.float32).astype(ml_dtypes.float8_e4m3fn).view(np.uint8)
    words = codes.reshape(n // 512, 128, 4, m).transpose(0, 1, 3, 2)
    return np.ascontiguousarray(words), np.ascontiguousarray(byte.astype(np.uint8).reshape(n // 512, 16, m))


K, H, N, T, S = 512, 1024, 768, 4096, 1024

def setup_inputs():
    n = np.random.standard_normal
    s = mx_kscale(K)[:, None]
    u = mx_kscale(H)[:, None]
    tab_words, tab_scales = pack_weight(n((K, T)) * s, "e4m3")
    offs = striped(np.random.permutation(T)[:S])
    w1 = 0.7 * n((K, H)) / np.sqrt(K) / s * u.T
    w4_words, w4_scales = pack_weight(0.7 * n((K, H)) / np.sqrt(K) / s * u.T, "e2m1")
    cub = np.random.uniform(0.05, 0.15, H) / u[:, 0] ** 2
    w3 = n((H, N)) / np.sqrt(H) / u
    drive = n((N, S))
    w8_words, w8_scales = pack_weight(0.7 * n((K, N)) / np.sqrt(K) / s, "e4m3")
    return {"tab_words": tab_words, "tab_scales": tab_scales, "offs": offs,
            "w1": w1.astype(np.float32),
            "w4_words": w4_words, "w4_scales": w4_scales,
            "cub": cub.astype(np.float32),
            "w3": w3.astype(np.float32),
            "drive": drive.astype(np.float32),
            "w8_words": w8_words, "w8_scales": w8_scales}

def reference(tab_words, tab_scales, offs, w1, w4_words, w4_scales, cub, w3, drive, w8_words, w8_scales):
    v = unpack_weight(tab_words, tab_scales, "e4m3")[:, unstriped(offs)]
    w1q = mxq(f64(w1), 0, "e4m3")
    w4 = unpack_weight(w4_words, w4_scales, "e2m1")
    w8 = unpack_weight(w8_words, w8_scales, "e4m3")
    e = w1q.T @ v + w4.T @ v
    h = e - f64(cub)[:, None] * e * e * e
    hq = mxq(h, 0, "e4m3")
    w3q = mxq(f64(w3), 0, "e4m3")
    y = f64(drive) * (w3q.T @ hq) + (w8.T @ v)
    words, scales = planes(h)
    return y, h, words, scales

@@ -1,0 +1,221 @@
+from contextlib import ExitStack
+
+import concourse.mybir as mybir
+
+K, H, N, T, S = 512, 1024, 768, 4096, 1024
+FLOPS = 2 * S * (2 * K * H + H * N + K * N)
+
+F32 = mybir.dt.float32
+BF16 = mybir.dt.bfloat16
+I32 = mybir.dt.int32
+U32 = mybir.dt.uint32
+U16 = mybir.dt.uint16
+U8 = mybir.dt.uint8
+FP8X4 = mybir.dt.float8_e4m3fn_x4
+FP4X4 = mybir.dt.float4_e2m1fn_x4
+MULT = mybir.AluOpType.mult
+ADD = mybir.AluOpType.add
+SQUARE = mybir.ActivationFunctionType.Square
+
+P = 128
+PACK = 4
+PASS = P * PACK
+GROUPS = H // PASS
+J = 512
+HALVES = S // J
+NTILES = N // P
+W3_CHUNK = 256
+
+
+def load_scale_rows(queues, plane, rows):
+    for q in range(4):
+        queues[q].dma_start(out=plane[32 * q : 32 * q + 4, :].bitcast(I32), in_=rows[4 * q : 4 * q + 4, :].bitcast(I32))
+
+
+def tile_list_cavity_pulse_shaping_kernel(
+    tc, tab_words, tab_scales, offs, w1, w4_words, w4_scales, cub, w3, drive, w8_words, w8_scales, out_0, out_1, out_2, out_3
+):
+    nc = tc.nc
+    with ExitStack() as ctx:
+        held = ctx.enter_context(tc.tile_pool(name="held", bufs=1))
+        ring = ctx.enter_context(tc.tile_pool(name="ring", bufs=4))
+        pair = ctx.enter_context(tc.tile_pool(name="pair", bufs=2))
+        psum_e = ctx.enter_context(tc.psum_pool(name="psum_e", bufs=4))
+        psum_y = ctx.enter_context(tc.psum_pool(name="psum_y", bufs=2))
+
+        def keep(name, shape, dtype, tag=None):
+            return held.tile(shape, dtype, name=name, tag=tag or name, align_bytes=64)
+
+        offsets = held.tile([P, S // 16], U16, name="offsets")
+        tab_s = keep("tab_s", [P, T], U8)
+        w4_raw = keep("w4_raw", [P, 2 * H], U8, "w4_tab_drive")
+        w4_s_raw = keep("w4_s_raw", [P, H], U8, "w4s_then_floats")
+        w8_s = keep("w8_s", [P, N], U8)
+
+        nc.gpsimd.memset(w4_s_raw[:].bitcast(I32), 0)
+        nc.vector.memset(tab_s[:].bitcast(I32), 0)
+        nc.vector.memset(w8_s[:].bitcast(I32), 0)
+        nc.sync.dma_start(offsets[:], offs)
+        nc.sync.dma_start(out=w4_raw[:].bitcast(I32), in_=w4_words[0].bitcast(I32))
+        w1_rows = w1.rearrange("(p i) r -> p i r", i=PACK)
+        w1_first = keep("w1_first", [P, PACK, PASS], F32, "w1_then_w8")
+        nc.sync.dma_start(out=w1_first[:], in_=w1_rows[:, :, 0:PASS])
+
+        load_scale_rows([nc.gpsimd, nc.gpsimd, nc.scalar, nc.scalar], w4_s_raw, w4_scales[0])
+        load_scale_rows([nc.scalar] * 4, tab_s, tab_scales[0])
+        load_scale_rows([nc.gpsimd] * 4, w8_s, w8_scales[0])
+
+        w4_w = keep("w4_w", [P, 2 * H], U8)
+        w4_s = keep("w4_s", [P, H], U8)
+        nc.vector.tensor_copy(
+            out=w4_w[:].bitcast(U16).rearrange("p (g t m) -> p g m t", g=GROUPS, t=PACK),
+            in_=w4_raw[:].bitcast(U16).rearrange("p (g m t) -> p g m t", g=GROUPS, t=PACK),
+        )
+        tab_w = keep("tab_w", [P, T], U32, "w4_tab_drive")
+        nc.sync.dma_start(out=tab_w[:].bitcast(I32), in_=tab_words[0].rearrange("p n t -> p (n t)").bitcast(I32))
+        v_s = keep("v_s", [P, S], U8)
+        v_w = [keep("v_w%d" % jh, [P, J], U32) for jh in range(HALVES)]
+
+        def gather_words(jh):
+            nc.vector.tensor_copy(v_w[jh][:], tab_w[:].indirect(offsets[:, jh * (J // 16) : (jh + 1) * (J // 16)]))
+
+        nc.vector.tensor_copy(v_s[:], tab_s[:].indirect(offsets[:]))
+        nc.vector.tensor_copy(
+            out=w4_s[:].rearrange("p (g t m) -> p g m t", g=GROUPS, t=PACK),
+            in_=w4_s_raw[:].rearrange("p (g m t) -> p g m t", g=GROUPS, t=PACK),
+        )
+
+        w3_at = PACK * PASS
+        cub_at = w3_at + GROUPS * PACK * N
+        floats = keep("floats", [P, cub_at + GROUPS * PACK], F32, "w4s_then_floats")
+        cub_t = floats[:, cub_at:].rearrange("p (g t) -> p g t", g=GROUPS)
+        nc.gpsimd.dma_start(out=cub_t, in_=cub.rearrange("(g p t) -> p g t", g=GROUPS, t=PACK))
+        w1_raw = [w1_first[:], floats[:, 0:w3_at].rearrange("p (i r) -> p i r", i=PACK)]
+        w3_raw = [
+            floats[:, w3_at + g * PACK * N : w3_at + (g + 1) * PACK * N].rearrange("p (i n) -> p i n", i=PACK) for g in range(GROUPS)
+        ]
+        nc.sync.dma_start(out=w1_raw[1], in_=w1_rows[:, :, PASS : 2 * PASS])
+        for g in range(GROUPS):
+            nc.sync.dma_start(out=w3_raw[g], in_=w3[g * PASS : (g + 1) * PASS, :].rearrange("(p i) n -> p i n", i=PACK))
+
+        w1_w = [keep("w1_w%d" % g, [P, PASS], U32) for g in range(GROUPS)]
+        w1_s = [keep("w1_s%d" % g, [P, PASS], U8) for g in range(GROUPS)]
+
+        def quantise_w1(g, copy):
+            rounded = keep("w1_bf%d" % g, [P, PASS * PACK], BF16)
+            copy(
+                out=rounded[:].rearrange("p (t m i) -> p m i t", t=PACK, i=PACK),
+                in_=w1_raw[g].rearrange("p i (m t) -> p m i t", t=PACK),
+            )
+            nc.vector.quantize_mx(out=w1_w[g][:].bitcast(FP8X4), scales=w1_s[g][:], in_=rounded[:])
+
+        h_w = [keep("h_w%d" % g, [P, S], U32) for g in range(GROUPS)]
+        h_s = keep("h_s", [P, GROUPS * S], U8)
+        h_t = {}
+
+        def shape(g, jh):
+            cols = slice(jh * J, (jh + 1) * J)
+            h = keep("h%d%d" % (g, jh), [P, PACK, J], F32)
+            h_t[g, jh] = h
+            for t in range(PACK):
+                e = psum_e.tile([P, J], F32, name="e")
+                m0 = t * P
+                nc.tensor.matmul_mx(
+                    out=e[:], lhsT=w1_w[g][:, m0 : m0 + P].bitcast(FP8X4), lhsT_scale=w1_s[g][:, m0 : m0 + P],
+                    rhs=v_w[jh][:].bitcast(FP8X4), rhs_scale=v_s[:, cols], start=True, stop=False,
+                )
+                c0 = g * PASS + m0
+                nc.tensor.matmul_mx(
+                    out=e[:], lhsT=w4_w[:, 2 * c0 : 2 * (c0 + P)].bitcast(FP4X4), lhsT_scale=w4_s[:, c0 : c0 + P],
+                    rhs=v_w[jh][:].bitcast(FP8X4), rhs_scale=v_s[:, cols], start=False, stop=True,
+                )
+                u = ring.tile([P, J], F32, name="u")
+                nc.scalar.activation(u[:], e[:], SQUARE)
+                nc.gpsimd.tensor_scalar(u[:], u[:], cub_t[:, g, t : t + 1], -1.0, MULT, ADD)
+                nc.vector.scalar_tensor_tensor(h[:, t, :], e[:], -1.0, u[:], MULT, MULT)
+            nc.sync.dma_start(
+                out=out_1[g * PASS : (g + 1) * PASS, cols].rearrange("(p t) j -> p t j", t=PACK), in_=h[:]
+            )
+
+        def quantise_h(g, jh):
+            rounded = pair.tile([P, J * PACK], BF16, name="h_bf", align_bytes=64)
+            nc.scalar.copy(
+                out=rounded[:].rearrange("p (c i t) -> p c t i", i=4, t=PACK),
+                in_=h_t[g, jh][:].rearrange("p t (c i) -> p c t i", i=4),
+            )
+            nc.vector.quantize_mx(
+                out=h_w[g][:, jh * J : (jh + 1) * J].bitcast(FP8X4),
+                scales=h_s[:, g * S + jh * J : g * S + (jh + 1) * J],
+                in_=rounded[:],
+            )
+
+        w3_w = [keep("w3_w%d" % g, [P, N], U32) for g in range(GROUPS)]
+        w3_s = [keep("w3_s%d" % g, [P, N], U8) for g in range(GROUPS)]
+
+        def quantise_w3(g):
+            for n0 in range(0, N, W3_CHUNK):
+                rounded = ring.tile([P, W3_CHUNK * PACK], BF16, name="w3_bf", align_bytes=64)
+                nc.gpsimd.tensor_scalar(
+                    rounded[:].rearrange("p (c i t) -> p c t i", i=4, t=PACK),
+                    w3_raw[g][:, :, n0 : n0 + W3_CHUNK].rearrange("p t (c i) -> p c t i", i=4),
+                    1.0, 0.0, MULT, ADD,
+                )
+                nc.vector.quantize_mx(
+                    out=w3_w[g][:, n0 : n0 + W3_CHUNK].bitcast(FP8X4), scales=w3_s[g][:, n0 : n0 + W3_CHUNK], in_=rounded[:]
+                )
+
+        out_v = out_0.rearrange("(a p) j -> p a j", p=P)
+
+        def read_out(jh):
+            cols = slice(jh * J, (jh + 1) * J)
+            for a in range(NTILES):
+                rows = slice(a * P, (a + 1) * P)
+                shaped = psum_y.tile([P, J], F32, name="shaped")
+                for g in range(GROUPS):
+                    nc.tensor.matmul_mx(
+                        out=shaped[:], lhsT=w3_w[g][:, rows].bitcast(FP8X4), lhsT_scale=w3_s[g][:, rows],
+                        rhs=h_w[g][:, cols].bitcast(FP8X4), rhs_scale=h_s[:, g * S + jh * J : g * S + (jh + 1) * J],
+                        start=(g == 0), stop=(g == GROUPS - 1),
+                    )
+                direct = psum_y.tile([P, J], F32, name="direct")
+                nc.tensor.matmul_mx(
+                    out=direct[:], lhsT=w8_w[:, rows].bitcast(FP8X4), lhsT_scale=w8_s[:, rows],
+                    rhs=v_w[jh][:].bitcast(FP8X4), rhs_scale=v_s[:, cols], start=True, stop=True,
+                )
+                y = y_t[jh][:, a, :]
+                nc.vector.tensor_tensor(y, shaped[:], y, MULT)
+                nc.vector.tensor_tensor(y, direct[:], y, ADD)
+                if a % 2 == 1:
+                    nc.sync.dma_start(out=out_v[:, a - 1 : a + 1, cols], in_=y_t[jh][:, a - 1 : a + 1, :])
+
+        quantise_w1(0, nc.scalar.copy)
+        gather_words(0)
+        gather_words(1)
+        w8_w = keep("w8_w", [P, N], U32, "w1_then_w8")
+        nc.sync.dma_start(out=w8_w[:].bitcast(I32), in_=w8_words[0].rearrange("p n t -> p (n t)").bitcast(I32))
+        y_all = keep("y_all", [P, HALVES * NTILES, J], F32, "w4_tab_drive")
+        y_t = [y_all[:, jh * NTILES : (jh + 1) * NTILES, :] for jh in range(HALVES)]
+        drive_v = drive.rearrange("(a p) j -> p a j", p=P)
+        for jh in range(HALVES):
+            for a0 in range(0, NTILES, 3):
+                nc.sync.dma_start(out=y_t[jh][:, a0 : a0 + 3, :], in_=drive_v[:, a0 : a0 + 3, jh * J : (jh + 1) * J])
+        shape(0, 0)
+        quantise_w1(1, nc.vector.tensor_copy)
+        shape(1, 0)
+        quantise_h(0, 0)
+        quantise_w3(0)
+        quantise_h(1, 0)
+        quantise_w3(1)
+        shape(0, 1)
+        shape(1, 1)
+        read_out(0)
+        quantise_h(0, 1)
+        quantise_h(1, 1)
+        for g in range(GROUPS):
+            nc.sync.dma_start(out=out_2[g].rearrange("p m t -> p (m t)").bitcast(I32), in_=h_w[g][:].bitcast(I32))
+        for q in range(4):
+            nc.scalar.dma_start(
+                out=out_3[:, 4 * q : 4 * q + 4, :].rearrange("g r m -> r g m").bitcast(I32),
+                in_=h_s[32 * q : 32 * q + 4, :].bitcast(I32).rearrange("r (g m) -> r g m", g=GROUPS),
+            )
+        read_out(1)

@@ -16,6 +16,7 @@ FP4X4 = mybir.dt.float4_e2m1fn_x4
 MULT = mybir.AluOpType.mult
 ADD = mybir.AluOpType.add
 SQUARE = mybir.ActivationFunctionType.Square
+COPY = mybir.ActivationFunctionType.Copy
 
 P = 128
 PACK = 4
@@ -47,22 +48,23 @@ def tile_list_cavity_pulse_shaping_kernel(
             return held.tile(shape, dtype, name=name, tag=tag or name, align_bytes=64)
 
         offsets = held.tile([P, S // 16], U16, name="offsets")
+        tab_w = keep("tab_w", [P, T], U32, "tab_then_drive")
         tab_s = keep("tab_s", [P, T], U8)
-        w4_raw = keep("w4_raw", [P, 2 * H], U8, "w4_tab_drive")
-        w4_s_raw = keep("w4_s_raw", [P, H], U8, "w4s_then_floats")
+        w4_raw = keep("w4_raw", [P, 2 * H], U8, "w4_then_floats")
+        w4_s_raw = keep("w4_s_raw", [P, H], U8, "w4s_then_w8")
         w8_s = keep("w8_s", [P, N], U8)
 
-        nc.gpsimd.memset(w4_s_raw[:].bitcast(I32), 0)
+        cub_t = keep("cub_t", [P, GROUPS, PACK], F32)
+
         nc.vector.memset(tab_s[:].bitcast(I32), 0)
-        nc.vector.memset(w8_s[:].bitcast(I32), 0)
+        nc.vector.memset(w4_s_raw[:].bitcast(I32), 0)
+        nc.gpsimd.dma_start(out=cub_t[:], in_=cub.rearrange("(g p t) -> p g t", g=GROUPS, t=PACK))
+        nc.gpsimd.memset(w8_s[:].bitcast(I32), 0)
         nc.sync.dma_start(offsets[:], offs)
         nc.sync.dma_start(out=w4_raw[:].bitcast(I32), in_=w4_words[0].bitcast(I32))
-        w1_rows = w1.rearrange("(p i) r -> p i r", i=PACK)
-        w1_first = keep("w1_first", [P, PACK, PASS], F32, "w1_then_w8")
-        nc.sync.dma_start(out=w1_first[:], in_=w1_rows[:, :, 0:PASS])
-
-        load_scale_rows([nc.gpsimd, nc.gpsimd, nc.scalar, nc.scalar], w4_s_raw, w4_scales[0])
+        nc.sync.dma_start(out=tab_w[:].bitcast(I32), in_=tab_words[0].rearrange("p n t -> p (n t)").bitcast(I32))
         load_scale_rows([nc.scalar] * 4, tab_s, tab_scales[0])
+        load_scale_rows([nc.scalar] * 4, w4_s_raw, w4_scales[0])
         load_scale_rows([nc.gpsimd] * 4, w8_s, w8_scales[0])
 
         w4_w = keep("w4_w", [P, 2 * H], U8)
@@ -71,8 +73,6 @@ def tile_list_cavity_pulse_shaping_kernel(
             out=w4_w[:].bitcast(U16).rearrange("p (g t m) -> p g m t", g=GROUPS, t=PACK),
             in_=w4_raw[:].bitcast(U16).rearrange("p (g m t) -> p g m t", g=GROUPS, t=PACK),
         )
-        tab_w = keep("tab_w", [P, T], U32, "w4_tab_drive")
-        nc.sync.dma_start(out=tab_w[:].bitcast(I32), in_=tab_words[0].rearrange("p n t -> p (n t)").bitcast(I32))
         v_s = keep("v_s", [P, S], U8)
         v_w = [keep("v_w%d" % jh, [P, J], U32) for jh in range(HALVES)]
 
@@ -80,33 +80,44 @@ def tile_list_cavity_pulse_shaping_kernel(
             nc.vector.tensor_copy(v_w[jh][:], tab_w[:].indirect(offsets[:, jh * (J // 16) : (jh + 1) * (J // 16)]))
 
         nc.vector.tensor_copy(v_s[:], tab_s[:].indirect(offsets[:]))
+        gather_words(0)
+        gather_words(1)
         nc.vector.tensor_copy(
             out=w4_s[:].rearrange("p (g t m) -> p g m t", g=GROUPS, t=PACK),
             in_=w4_s_raw[:].rearrange("p (g m t) -> p g m t", g=GROUPS, t=PACK),
         )
 
-        w3_at = PACK * PASS
-        cub_at = w3_at + GROUPS * PACK * N
-        floats = keep("floats", [P, cub_at + GROUPS * PACK], F32, "w4s_then_floats")
-        cub_t = floats[:, cub_at:].rearrange("p (g t) -> p g t", g=GROUPS)
-        nc.gpsimd.dma_start(out=cub_t, in_=cub.rearrange("(g p t) -> p g t", g=GROUPS, t=PACK))
-        w1_raw = [w1_first[:], floats[:, 0:w3_at].rearrange("p (i r) -> p i r", i=PACK)]
+        floats = keep("floats", [P, PACK * H + GROUPS * PACK * N], F32, "w4_then_floats")
+        w1_raw = [floats[:, g * PACK * PASS : (g + 1) * PACK * PASS].rearrange("p (i r) -> p i r", i=PACK) for g in range(GROUPS)]
+        w3_at = PACK * H
         w3_raw = [
             floats[:, w3_at + g * PACK * N : w3_at + (g + 1) * PACK * N].rearrange("p (i n) -> p i n", i=PACK) for g in range(GROUPS)
         ]
-        nc.sync.dma_start(out=w1_raw[1], in_=w1_rows[:, :, PASS : 2 * PASS])
+        w1_rows = w1.rearrange("(p i) r -> p i r", i=PACK)
+        for g in range(GROUPS):
+            nc.sync.dma_start(out=w1_raw[g], in_=w1_rows[:, :, g * PASS : (g + 1) * PASS])
         for g in range(GROUPS):
             nc.sync.dma_start(out=w3_raw[g], in_=w3[g * PASS : (g + 1) * PASS, :].rearrange("(p i) n -> p i n", i=PACK))
+        w8_w = keep("w8_w", [P, N], U32, "w4s_then_w8")
+        nc.sync.dma_start(out=w8_w[:].bitcast(I32), in_=w8_words[0].rearrange("p n t -> p (n t)").bitcast(I32))
+        y_all = keep("y_all", [P, HALVES * NTILES, J], F32, "tab_then_drive")
+        y_t = [y_all[:, jh * NTILES : (jh + 1) * NTILES, :] for jh in range(HALVES)]
+        drive_v = drive.rearrange("(a p) j -> p a j", p=P)
+        for jh in range(HALVES):
+            for a0 in range(0, NTILES, 3):
+                nc.sync.dma_start(out=y_t[jh][:, a0 : a0 + 3, :], in_=drive_v[:, a0 : a0 + 3, jh * J : (jh + 1) * J])
 
         w1_w = [keep("w1_w%d" % g, [P, PASS], U32) for g in range(GROUPS)]
         w1_s = [keep("w1_s%d" % g, [P, PASS], U8) for g in range(GROUPS)]
 
-        def quantise_w1(g, copy):
+        def quantise_w1(g, copies):
             rounded = keep("w1_bf%d" % g, [P, PASS * PACK], BF16)
-            copy(
-                out=rounded[:].rearrange("p (t m i) -> p m i t", t=PACK, i=PACK),
-                in_=w1_raw[g].rearrange("p i (m t) -> p m i t", t=PACK),
-            )
+            share = P // len(copies)
+            for c, copy in enumerate(copies):
+                copy(
+                    out=rounded[:].rearrange("p (t m i) -> p m i t", t=PACK, i=PACK)[:, c * share : (c + 1) * share],
+                    in_=w1_raw[g].rearrange("p i (m t) -> p m i t", t=PACK)[:, c * share : (c + 1) * share],
+                )
             nc.vector.quantize_mx(out=w1_w[g][:].bitcast(FP8X4), scales=w1_s[g][:], in_=rounded[:])
 
         h_w = [keep("h_w%d" % g, [P, S], U32) for g in range(GROUPS)]
@@ -117,6 +128,7 @@ def tile_list_cavity_pulse_shaping_kernel(
             cols = slice(jh * J, (jh + 1) * J)
             h = keep("h%d%d" % (g, jh), [P, PACK, J], F32)
             h_t[g, jh] = h
+            pending = []
             for t in range(PACK):
                 e = psum_e.tile([P, J], F32, name="e")
                 m0 = t * P
@@ -131,8 +143,15 @@ def tile_list_cavity_pulse_shaping_kernel(
                 )
                 u = ring.tile([P, J], F32, name="u")
                 nc.scalar.activation(u[:], e[:], SQUARE)
-                nc.gpsimd.tensor_scalar(u[:], u[:], cub_t[:, g, t : t + 1], -1.0, MULT, ADD)
-                nc.vector.scalar_tensor_tensor(h[:, t, :], e[:], -1.0, u[:], MULT, MULT)
+                if jh == 0:
+                    nc.vector.tensor_scalar(u[:], u[:], cub_t[:, g, t : t + 1], -1.0, MULT, ADD)
+                else:
+                    nc.scalar.activation(u[:], u[:], COPY, bias=-1.0, scale=cub_t[:, g, t : t + 1])
+                pending.append((h[:, t, :], e, u))
+                if len(pending) == 2 or t == PACK - 1:
+                    for row, e_done, u_done in pending[: 1 if t < PACK - 1 else 2]:
+                        nc.vector.scalar_tensor_tensor(row, e_done[:], -1.0, u_done[:], MULT, MULT)
+                    pending = pending[1:]
             nc.sync.dma_start(
                 out=out_1[g * PASS : (g + 1) * PASS, cols].rearrange("(p t) j -> p t j", t=PACK), in_=h[:]
             )
@@ -153,22 +172,20 @@ def tile_list_cavity_pulse_shaping_kernel(
         w3_s = [keep("w3_s%d" % g, [P, N], U8) for g in range(GROUPS)]
 
         def quantise_w3(g):
-            for n0 in range(0, N, W3_CHUNK):
-                rounded = ring.tile([P, W3_CHUNK * PACK], BF16, name="w3_bf", align_bytes=64)
-                nc.gpsimd.tensor_scalar(
-                    rounded[:].rearrange("p (c i t) -> p c t i", i=4, t=PACK),
-                    w3_raw[g][:, :, n0 : n0 + W3_CHUNK].rearrange("p t (c i) -> p c t i", i=4),
-                    1.0, 0.0, MULT, ADD,
+            for n0, n1, copy in ((0, W3_CHUNK, nc.vector.tensor_copy), (W3_CHUNK, N, nc.scalar.copy)):
+                rounded = keep("w3_bf%d_%d" % (g, n0), [P, (n1 - n0) * PACK], BF16)
+                copy(
+                    out=rounded[:].rearrange("p (c i t) -> p c t i", i=4, t=PACK),
+                    in_=w3_raw[g][:, :, n0:n1].rearrange("p t (c i) -> p c t i", i=4),
                 )
-                nc.vector.quantize_mx(
-                    out=w3_w[g][:, n0 : n0 + W3_CHUNK].bitcast(FP8X4), scales=w3_s[g][:, n0 : n0 + W3_CHUNK], in_=rounded[:]
-                )
+                nc.vector.quantize_mx(out=w3_w[g][:, n0:n1].bitcast(FP8X4), scales=w3_s[g][:, n0:n1], in_=rounded[:])
 
         out_v = out_0.rearrange("(a p) j -> p a j", p=P)
 
         def read_out(jh):
             cols = slice(jh * J, (jh + 1) * J)
-            for a in range(NTILES):
+
+            def drive_tile(a):
                 rows = slice(a * P, (a + 1) * P)
                 shaped = psum_y.tile([P, J], F32, name="shaped")
                 for g in range(GROUPS):
@@ -177,30 +194,30 @@ def tile_list_cavity_pulse_shaping_kernel(
                         rhs=h_w[g][:, cols].bitcast(FP8X4), rhs_scale=h_s[:, g * S + jh * J : g * S + (jh + 1) * J],
                         start=(g == 0), stop=(g == GROUPS - 1),
                     )
+                nc.vector.tensor_tensor(y_t[jh][:, a, :], shaped[:], y_t[jh][:, a, :], MULT)
+
+            def add_direct(a):
+                rows = slice(a * P, (a + 1) * P)
                 direct = psum_y.tile([P, J], F32, name="direct")
                 nc.tensor.matmul_mx(
                     out=direct[:], lhsT=w8_w[:, rows].bitcast(FP8X4), lhsT_scale=w8_s[:, rows],
                     rhs=v_w[jh][:].bitcast(FP8X4), rhs_scale=v_s[:, cols], start=True, stop=True,
                 )
-                y = y_t[jh][:, a, :]
-                nc.vector.tensor_tensor(y, shaped[:], y, MULT)
-                nc.vector.tensor_tensor(y, direct[:], y, ADD)
-                if a % 2 == 1:
+                nc.vector.tensor_tensor(y_t[jh][:, a, :], direct[:], y_t[jh][:, a, :], ADD)
+                if jh == HALVES - 1:
+                    nc.sync.dma_start(out=out_v[:, a, cols], in_=y_t[jh][:, a, :])
+                elif a % 2 == 1:
                     nc.sync.dma_start(out=out_v[:, a - 1 : a + 1, cols], in_=y_t[jh][:, a - 1 : a + 1, :])
 
-        quantise_w1(0, nc.scalar.copy)
-        gather_words(0)
-        gather_words(1)
-        w8_w = keep("w8_w", [P, N], U32, "w1_then_w8")
-        nc.sync.dma_start(out=w8_w[:].bitcast(I32), in_=w8_words[0].rearrange("p n t -> p (n t)").bitcast(I32))
-        y_all = keep("y_all", [P, HALVES * NTILES, J], F32, "w4_tab_drive")
-        y_t = [y_all[:, jh * NTILES : (jh + 1) * NTILES, :] for jh in range(HALVES)]
-        drive_v = drive.rearrange("(a p) j -> p a j", p=P)
-        for jh in range(HALVES):
-            for a0 in range(0, NTILES, 3):
-                nc.sync.dma_start(out=y_t[jh][:, a0 : a0 + 3, :], in_=drive_v[:, a0 : a0 + 3, jh * J : (jh + 1) * J])
+            drive_tile(0)
+            for a in range(1, NTILES):
+                drive_tile(a)
+                add_direct(a - 1)
+            add_direct(NTILES - 1)
+
+        quantise_w1(0, [nc.scalar.copy, nc.vector.tensor_copy])
         shape(0, 0)
-        quantise_w1(1, nc.vector.tensor_copy)
+        quantise_w1(1, [nc.vector.tensor_copy])
         shape(1, 0)
         quantise_h(0, 0)
         quantise_w3(0)
@@ -208,9 +225,9 @@ def tile_list_cavity_pulse_shaping_kernel(
         quantise_w3(1)
         shape(0, 1)
         shape(1, 1)
-        read_out(0)
         quantise_h(0, 1)
         quantise_h(1, 1)
+        read_out(0)
         for g in range(GROUPS):
             nc.sync.dma_start(out=out_2[g].rearrange("p m t -> p (m t)").bitcast(I32), in_=h_w[g][:].bitcast(I32))
         for q in range(4):

@@ -70,8 +70,8 @@ def tile_list_cavity_pulse_shaping_kernel(
         w4_w = keep("w4_w", [P, 2 * H], U8)
         w4_s = keep("w4_s", [P, H], U8)
         nc.vector.tensor_copy(
-            out=w4_w[:].bitcast(U16).rearrange("p (g t m) -> p g m t", g=GROUPS, t=PACK),
-            in_=w4_raw[:].bitcast(U16).rearrange("p (g m t) -> p g m t", g=GROUPS, t=PACK),
+            out=w4_w[:].bitcast(U16).rearrange("p (g t c m) -> p g c t m", g=GROUPS, t=PACK, m=8),
+            in_=w4_raw[:].bitcast(U16).rearrange("p (g c m t) -> p g c t m", g=GROUPS, t=PACK, m=8),
         )
         v_s = keep("v_s", [P, S], U8)
         v_w = [keep("v_w%d" % jh, [P, J], U32) for jh in range(HALVES)]
@@ -83,8 +83,8 @@ def tile_list_cavity_pulse_shaping_kernel(
         gather_words(0)
         gather_words(1)
         nc.vector.tensor_copy(
-            out=w4_s[:].rearrange("p (g t m) -> p g m t", g=GROUPS, t=PACK),
-            in_=w4_s_raw[:].rearrange("p (g m t) -> p g m t", g=GROUPS, t=PACK),
+            out=w4_s[:].rearrange("p (g t c m) -> p g c t m", g=GROUPS, t=PACK, m=16),
+            in_=w4_s_raw[:].rearrange("p (g c m t) -> p g c t m", g=GROUPS, t=PACK, m=16),
         )
 
         floats = keep("floats", [P, PACK * H + GROUPS * PACK * N], F32, "w4_then_floats")
@@ -115,8 +115,8 @@ def tile_list_cavity_pulse_shaping_kernel(
             share = P // len(copies)
             for c, copy in enumerate(copies):
                 copy(
-                    out=rounded[:].rearrange("p (t m i) -> p m i t", t=PACK, i=PACK)[:, c * share : (c + 1) * share],
-                    in_=w1_raw[g].rearrange("p i (m t) -> p m i t", t=PACK)[:, c * share : (c + 1) * share],
+                    out=rounded[:].rearrange("p (t m i) -> p m t i", t=PACK, i=PACK)[:, c * share : (c + 1) * share],
+                    in_=w1_raw[g].rearrange("p i (m t) -> p m t i", t=PACK)[:, c * share : (c + 1) * share],
                 )
             nc.vector.quantize_mx(out=w1_w[g][:].bitcast(FP8X4), scales=w1_s[g][:], in_=rounded[:])
 
@@ -159,8 +159,8 @@ def tile_list_cavity_pulse_shaping_kernel(
         def quantise_h(g, jh):
             rounded = pair.tile([P, J * PACK], BF16, name="h_bf", align_bytes=64)
             nc.scalar.copy(
-                out=rounded[:].rearrange("p (c i t) -> p c t i", i=4, t=PACK),
-                in_=h_t[g, jh][:].rearrange("p t (c i) -> p c t i", i=4),
+                out=rounded[:].rearrange("p (c i t) -> p c t i", i=2, t=PACK),
+                in_=h_t[g, jh][:].rearrange("p t (c i) -> p c t i", i=2),
             )
             nc.vector.quantize_mx(
                 out=h_w[g][:, jh * J : (jh + 1) * J].bitcast(FP8X4),
@@ -175,8 +175,8 @@ def tile_list_cavity_pulse_shaping_kernel(
             for n0, n1, copy in ((0, W3_CHUNK, nc.vector.tensor_copy), (W3_CHUNK, N, nc.scalar.copy)):
                 rounded = keep("w3_bf%d_%d" % (g, n0), [P, (n1 - n0) * PACK], BF16)
                 copy(
-                    out=rounded[:].rearrange("p (c i t) -> p c t i", i=4, t=PACK),
-                    in_=w3_raw[g][:, :, n0:n1].rearrange("p t (c i) -> p c t i", i=4),
+                    out=rounded[:].rearrange("p (c i t) -> p c t i", i=2, t=PACK),
+                    in_=w3_raw[g][:, :, n0:n1].rearrange("p t (c i) -> p c t i", i=2),
                 )
                 nc.vector.quantize_mx(out=w3_w[g][:, n0:n1].bitcast(FP8X4), scales=w3_s[g][:, n0:n1], in_=rounded[:])
 

@@ -26,6 +26,7 @@ J = 512
 HALVES = S // J
 NTILES = N // P
 W3_CHUNK = 256
+GPSIMD_ADDS = (range(0), range(0, 3))
 
 
 def load_scale_rows(queues, plane, rows):
@@ -39,10 +40,12 @@ def tile_list_cavity_pulse_shaping_kernel(
     nc = tc.nc
     with ExitStack() as ctx:
         held = ctx.enter_context(tc.tile_pool(name="held", bufs=1))
-        ring = ctx.enter_context(tc.tile_pool(name="ring", bufs=4))
+        ring = ctx.enter_context(tc.tile_pool(name="ring", bufs=6))
         pair = ctx.enter_context(tc.tile_pool(name="pair", bufs=2))
-        psum_e = ctx.enter_context(tc.psum_pool(name="psum_e", bufs=4))
-        psum_y = ctx.enter_context(tc.psum_pool(name="psum_y", bufs=2))
+        psum = ctx.enter_context(tc.psum_pool(name="psum", bufs=1))
+
+        def bank(b):
+            return psum.tile([P, J], F32, name="bank%d" % b)
 
         def keep(name, shape, dtype, tag=None):
             return held.tile(shape, dtype, name=name, tag=tag or name, align_bytes=64)
@@ -130,7 +133,7 @@ def tile_list_cavity_pulse_shaping_kernel(
             h_t[g, jh] = h
             pending = []
             for t in range(PACK):
-                e = psum_e.tile([P, J], F32, name="e")
+                e = bank(g * PACK + t if jh == 0 else t)
                 m0 = t * P
                 nc.tensor.matmul_mx(
                     out=e[:], lhsT=w1_w[g][:, m0 : m0 + P].bitcast(FP8X4), lhsT_scale=w1_s[g][:, m0 : m0 + P],
@@ -143,11 +146,9 @@ def tile_list_cavity_pulse_shaping_kernel(
                 )
                 u = ring.tile([P, J], F32, name="u")
                 nc.scalar.activation(u[:], e[:], SQUARE)
-                if jh == 0:
-                    nc.vector.tensor_scalar(u[:], u[:], cub_t[:, g, t : t + 1], -1.0, MULT, ADD)
-                else:
-                    nc.scalar.activation(u[:], u[:], COPY, bias=-1.0, scale=cub_t[:, g, t : t + 1])
-                pending.append((h[:, t, :], e, u))
+                factor = ring.tile([P, J], F32, name="factor")
+                nc.gpsimd.tensor_scalar(factor[:], u[:], cub_t[:, g, t : t + 1], -1.0, MULT, ADD)
+                pending.append((h[:, t, :], e, factor))
                 if len(pending) == 2 or t == PACK - 1:
                     for row, e_done, u_done in pending[: 1 if t < PACK - 1 else 2]:
                         nc.vector.scalar_tensor_tensor(row, e_done[:], -1.0, u_done[:], MULT, MULT)
@@ -167,12 +168,16 @@ def tile_list_cavity_pulse_shaping_kernel(
                 scales=h_s[:, g * S + jh * J : g * S + (jh + 1) * J],
                 in_=rounded[:],
             )
+            nc.sync.dma_start(
+                out=out_2[g].rearrange("p m t -> p (m t)").bitcast(I32)[:, jh * J : (jh + 1) * J],
+                in_=h_w[g][:, jh * J : (jh + 1) * J].bitcast(I32),
+            )
 
         w3_w = [keep("w3_w%d" % g, [P, N], U32) for g in range(GROUPS)]
         w3_s = [keep("w3_s%d" % g, [P, N], U8) for g in range(GROUPS)]
 
         def quantise_w3(g):
-            for n0, n1, copy in ((0, W3_CHUNK, nc.vector.tensor_copy), (W3_CHUNK, N, nc.scalar.copy)):
+            for n0, n1, copy in ((0, W3_CHUNK, nc.vector.tensor_copy), (W3_CHUNK, N, nc.scalar.copy if g else nc.vector.tensor_copy)):
                 rounded = keep("w3_bf%d_%d" % (g, n0), [P, (n1 - n0) * PACK], BF16)
                 copy(
                     out=rounded[:].rearrange("p (c i t) -> p c t i", i=2, t=PACK),
@@ -182,28 +187,40 @@ def tile_list_cavity_pulse_shaping_kernel(
 
         out_v = out_0.rearrange("(a p) j -> p a j", p=P)
 
+        def direct_sum(a, jh):
+            rows = slice(a * P, (a + 1) * P)
+            direct = bank(6 + a % 2 if jh == 0 else 4 + a % 4)
+            nc.tensor.matmul_mx(
+                out=direct[:], lhsT=w8_w[:, rows].bitcast(FP8X4), lhsT_scale=w8_s[:, rows],
+                rhs=v_w[jh][:].bitcast(FP8X4), rhs_scale=v_s[:, jh * J : (jh + 1) * J], start=True, stop=True,
+            )
+            return direct
+
         def read_out(jh):
             cols = slice(jh * J, (jh + 1) * J)
 
+            driven = {}
+
             def drive_tile(a):
                 rows = slice(a * P, (a + 1) * P)
-                shaped = psum_y.tile([P, J], F32, name="shaped")
+                shaped = bank(4 + a % 2 if jh == 0 else a % 4)
                 for g in range(GROUPS):
                     nc.tensor.matmul_mx(
                         out=shaped[:], lhsT=w3_w[g][:, rows].bitcast(FP8X4), lhsT_scale=w3_s[g][:, rows],
                         rhs=h_w[g][:, cols].bitcast(FP8X4), rhs_scale=h_s[:, g * S + jh * J : g * S + (jh + 1) * J],
                         start=(g == 0), stop=(g == GROUPS - 1),
                     )
-                nc.vector.tensor_tensor(y_t[jh][:, a, :], shaped[:], y_t[jh][:, a, :], MULT)
+                driven[a] = ring.tile([P, J], F32, name="driven")
+                nc.vector.tensor_tensor(driven[a][:], shaped[:], y_t[jh][:, a, :], MULT)
 
             def add_direct(a):
-                rows = slice(a * P, (a + 1) * P)
-                direct = psum_y.tile([P, J], F32, name="direct")
-                nc.tensor.matmul_mx(
-                    out=direct[:], lhsT=w8_w[:, rows].bitcast(FP8X4), lhsT_scale=w8_s[:, rows],
-                    rhs=v_w[jh][:].bitcast(FP8X4), rhs_scale=v_s[:, cols], start=True, stop=True,
-                )
-                nc.vector.tensor_tensor(y_t[jh][:, a, :], direct[:], y_t[jh][:, a, :], ADD)
+                direct = direct_sum(a, jh)
+                if a in GPSIMD_ADDS[jh]:
+                    parked = ring.tile([P, J], F32, name="parked", bufs=3)
+                    nc.scalar.copy(out=parked[:], in_=direct[:])
+                    nc.gpsimd.tensor_tensor(y_t[jh][:, a, :], parked[:], driven[a][:], ADD)
+                else:
+                    nc.vector.tensor_tensor(y_t[jh][:, a, :], direct[:], driven[a][:], ADD)
                 if jh == HALVES - 1:
                     nc.sync.dma_start(out=out_v[:, a, cols], in_=y_t[jh][:, a, :])
                 elif a % 2 == 1:
@@ -228,10 +245,8 @@ def tile_list_cavity_pulse_shaping_kernel(
         quantise_h(0, 1)
         quantise_h(1, 1)
         read_out(0)
-        for g in range(GROUPS):
-            nc.sync.dma_start(out=out_2[g].rearrange("p m t -> p (m t)").bitcast(I32), in_=h_w[g][:].bitcast(I32))
         for q in range(4):
-            nc.scalar.dma_start(
+            nc.sync.dma_start(
                 out=out_3[:, 4 * q : 4 * q + 4, :].rearrange("g r m -> r g m").bitcast(I32),
                 in_=h_s[32 * q : 32 * q + 4, :].bitcast(I32).rearrange("r (g m) -> r g m", g=GROUPS),
             )

@@ -26,12 +26,12 @@ J = 512
 HALVES = S // J
 NTILES = N // P
 W3_CHUNK = 256
-GPSIMD_ADDS = (range(0), range(0, 3))
+GPSIMD_ADDS = (range(0, 4), range(0, 4))
 
 
-def load_scale_rows(queues, plane, rows):
+def load_scale_rows(queue, plane, rows):
     for q in range(4):
-        queues[q].dma_start(out=plane[32 * q : 32 * q + 4, :].bitcast(I32), in_=rows[4 * q : 4 * q + 4, :].bitcast(I32))
+        queue.dma_start(out=plane[32 * q : 32 * q + 4, :].bitcast(I32), in_=rows[4 * q : 4 * q + 4, :].bitcast(I32))
 
 
 def tile_list_cavity_pulse_shaping_kernel(
@@ -40,7 +40,7 @@ def tile_list_cavity_pulse_shaping_kernel(
     nc = tc.nc
     with ExitStack() as ctx:
         held = ctx.enter_context(tc.tile_pool(name="held", bufs=1))
-        ring = ctx.enter_context(tc.tile_pool(name="ring", bufs=6))
+        ring = ctx.enter_context(tc.tile_pool(name="ring", bufs=5))
         pair = ctx.enter_context(tc.tile_pool(name="pair", bufs=2))
         psum = ctx.enter_context(tc.psum_pool(name="psum", bufs=1))
 
@@ -51,64 +51,66 @@ def tile_list_cavity_pulse_shaping_kernel(
             return held.tile(shape, dtype, name=name, tag=tag or name, align_bytes=64)
 
         offsets = held.tile([P, S // 16], U16, name="offsets")
-        tab_w = keep("tab_w", [P, T], U32, "tab_then_drive")
+        tab_w = keep("tab_w", [P, T], U32, "tab_then_parked")
+        tab_s_rows = keep("tab_s_rows", [P, T], U8)
         tab_s = keep("tab_s", [P, T], U8)
-        w4_raw = keep("w4_raw", [P, 2 * H], U8, "w4_then_floats")
-        w4_s_raw = keep("w4_s_raw", [P, H], U8, "w4s_then_w8")
+        w4_raw = keep("w4_raw", [P, 2 * H], U8)
+        w4_s_rows = keep("w4_s_rows", [P, H], U8)
+        w4_s_raw = keep("w4_s_raw", [P, H], U8)
+        w8_w = keep("w8_w", [P, N], U32)
         w8_s = keep("w8_s", [P, N], U8)
-
         cub_t = keep("cub_t", [P, GROUPS, PACK], F32)
+        w1_raw = [keep("w1_raw%d" % g, [P, PACK, PASS], F32) for g in range(GROUPS)]
+        w3_raw = [keep("w3_raw%d" % g, [P, PACK, N], F32) for g in range(GROUPS)]
+        y_rows = [keep("y_rows%d" % b, [P, NTILES // 2, S], F32) for b in range(2)]
+
+        def y_tile(a, jh):
+            return y_rows[a // 3][:, a % 3, jh * J : (jh + 1) * J]
 
         nc.vector.memset(tab_s[:].bitcast(I32), 0)
         nc.vector.memset(w4_s_raw[:].bitcast(I32), 0)
+        nc.vector.memset(w8_s[:].bitcast(I32), 0)
         nc.gpsimd.dma_start(out=cub_t[:], in_=cub.rearrange("(g p t) -> p g t", g=GROUPS, t=PACK))
-        nc.gpsimd.memset(w8_s[:].bitcast(I32), 0)
+
+        w1_rows = w1.rearrange("(p i) r -> p i r", i=PACK)
+        drive_v = drive.rearrange("(a p) j -> p a j", p=P)
+        load_scale_rows(nc.sync, tab_s_rows, tab_scales[0])
+        nc.sync.dma_start(out=w1_raw[0][:], in_=w1_rows[:, :, 0:PASS])
         nc.sync.dma_start(offsets[:], offs)
+        load_scale_rows(nc.sync, w4_s_rows, w4_scales[0])
         nc.sync.dma_start(out=w4_raw[:].bitcast(I32), in_=w4_words[0].bitcast(I32))
         nc.sync.dma_start(out=tab_w[:].bitcast(I32), in_=tab_words[0].rearrange("p n t -> p (n t)").bitcast(I32))
-        load_scale_rows([nc.scalar] * 4, tab_s, tab_scales[0])
-        load_scale_rows([nc.scalar] * 4, w4_s_raw, w4_scales[0])
-        load_scale_rows([nc.gpsimd] * 4, w8_s, w8_scales[0])
+        nc.sync.dma_start(out=w1_raw[1][:], in_=w1_rows[:, :, PASS : 2 * PASS])
+        for g in range(GROUPS):
+            nc.sync.dma_start(out=w3_raw[g][:], in_=w3[g * PASS : (g + 1) * PASS, :].rearrange("(p i) n -> p i n", i=PACK))
+        nc.sync.dma_start(out=w8_w[:].bitcast(I32), in_=w8_words[0].rearrange("p n t -> p (n t)").bitcast(I32))
+        load_scale_rows(nc.sync, w8_s, w8_scales[0])
+        for b in range(2):
+            nc.sync.dma_start(out=y_rows[b][:], in_=drive_v[:, 3 * b : 3 * b + 3, :])
+
+        def place_scale_rows(plane, rows):
+            for q in range(4):
+                nc.vector.tensor_copy(out=plane[32 * q : 32 * q + 4, :].bitcast(I32), in_=rows[32 * q : 32 * q + 4, :].bitcast(I32))
 
         w4_w = keep("w4_w", [P, 2 * H], U8)
         w4_s = keep("w4_s", [P, H], U8)
-        nc.vector.tensor_copy(
-            out=w4_w[:].bitcast(U16).rearrange("p (g t c m) -> p g c t m", g=GROUPS, t=PACK, m=8),
-            in_=w4_raw[:].bitcast(U16).rearrange("p (g c m t) -> p g c t m", g=GROUPS, t=PACK, m=8),
-        )
         v_s = keep("v_s", [P, S], U8)
         v_w = [keep("v_w%d" % jh, [P, J], U32) for jh in range(HALVES)]
 
         def gather_words(jh):
             nc.vector.tensor_copy(v_w[jh][:], tab_w[:].indirect(offsets[:, jh * (J // 16) : (jh + 1) * (J // 16)]))
 
+        place_scale_rows(tab_s, tab_s_rows)
         nc.vector.tensor_copy(v_s[:], tab_s[:].indirect(offsets[:]))
-        gather_words(0)
-        gather_words(1)
+        place_scale_rows(w4_s_raw, w4_s_rows)
         nc.vector.tensor_copy(
             out=w4_s[:].rearrange("p (g t c m) -> p g c t m", g=GROUPS, t=PACK, m=16),
             in_=w4_s_raw[:].rearrange("p (g c m t) -> p g c t m", g=GROUPS, t=PACK, m=16),
         )
-
-        floats = keep("floats", [P, PACK * H + GROUPS * PACK * N], F32, "w4_then_floats")
-        w1_raw = [floats[:, g * PACK * PASS : (g + 1) * PACK * PASS].rearrange("p (i r) -> p i r", i=PACK) for g in range(GROUPS)]
-        w3_at = PACK * H
-        w3_raw = [
-            floats[:, w3_at + g * PACK * N : w3_at + (g + 1) * PACK * N].rearrange("p (i n) -> p i n", i=PACK) for g in range(GROUPS)
-        ]
-        w1_rows = w1.rearrange("(p i) r -> p i r", i=PACK)
-        for g in range(GROUPS):
-            nc.sync.dma_start(out=w1_raw[g], in_=w1_rows[:, :, g * PASS : (g + 1) * PASS])
-        for g in range(GROUPS):
-            nc.sync.dma_start(out=w3_raw[g], in_=w3[g * PASS : (g + 1) * PASS, :].rearrange("(p i) n -> p i n", i=PACK))
-        w8_w = keep("w8_w", [P, N], U32, "w4s_then_w8")
-        nc.sync.dma_start(out=w8_w[:].bitcast(I32), in_=w8_words[0].rearrange("p n t -> p (n t)").bitcast(I32))
-        y_all = keep("y_all", [P, HALVES * NTILES, J], F32, "tab_then_drive")
-        y_t = [y_all[:, jh * NTILES : (jh + 1) * NTILES, :] for jh in range(HALVES)]
-        drive_v = drive.rearrange("(a p) j -> p a j", p=P)
-        for jh in range(HALVES):
-            for a0 in range(0, NTILES, 3):
-                nc.sync.dma_start(out=y_t[jh][:, a0 : a0 + 3, :], in_=drive_v[:, a0 : a0 + 3, jh * J : (jh + 1) * J])
+        nc.vector.tensor_copy(
+            out=w4_w[:].bitcast(U16).rearrange("p (g t c m) -> p g c t m", g=GROUPS, t=PACK, m=8),
+            in_=w4_raw[:].bitcast(U16).rearrange("p (g c m t) -> p g c t m", g=GROUPS, t=PACK, m=8),
+        )
 
         w1_w = [keep("w1_w%d" % g, [P, PASS], U32) for g in range(GROUPS)]
         w1_s = [keep("w1_s%d" % g, [P, PASS], U8) for g in range(GROUPS)]
@@ -119,7 +121,7 @@ def tile_list_cavity_pulse_shaping_kernel(
             for c, copy in enumerate(copies):
                 copy(
                     out=rounded[:].rearrange("p (t m i) -> p m t i", t=PACK, i=PACK)[:, c * share : (c + 1) * share],
-                    in_=w1_raw[g].rearrange("p i (m t) -> p m t i", t=PACK)[:, c * share : (c + 1) * share],
+                    in_=w1_raw[g][:].rearrange("p i (m t) -> p m t i", t=PACK)[:, c * share : (c + 1) * share],
                 )
             nc.vector.quantize_mx(out=w1_w[g][:].bitcast(FP8X4), scales=w1_s[g][:], in_=rounded[:])
 
@@ -133,7 +135,7 @@ def tile_list_cavity_pulse_shaping_kernel(
             h_t[g, jh] = h
             pending = []
             for t in range(PACK):
-                e = bank(g * PACK + t if jh == 0 else t)
+                e = bank(g * PACK + t)
                 m0 = t * P
                 nc.tensor.matmul_mx(
                     out=e[:], lhsT=w1_w[g][:, m0 : m0 + P].bitcast(FP8X4), lhsT_scale=w1_s[g][:, m0 : m0 + P],
@@ -159,10 +161,11 @@ def tile_list_cavity_pulse_shaping_kernel(
 
         def quantise_h(g, jh):
             rounded = pair.tile([P, J * PACK], BF16, name="h_bf", align_bytes=64)
-            nc.scalar.copy(
-                out=rounded[:].rearrange("p (c i t) -> p c t i", i=2, t=PACK),
-                in_=h_t[g, jh][:].rearrange("p t (c i) -> p c t i", i=2),
-            )
+            for c0 in range(0, J // 2, J // 4):
+                nc.scalar.copy(
+                    out=rounded[:].rearrange("p (c i t) -> p c t i", i=2, t=PACK)[:, c0 : c0 + J // 4],
+                    in_=h_t[g, jh][:].rearrange("p t (c i) -> p c t i", i=2)[:, c0 : c0 + J // 4],
+                )
             nc.vector.quantize_mx(
                 out=h_w[g][:, jh * J : (jh + 1) * J].bitcast(FP8X4),
                 scales=h_s[:, g * S + jh * J : g * S + (jh + 1) * J],
@@ -177,9 +180,10 @@ def tile_list_cavity_pulse_shaping_kernel(
         w3_s = [keep("w3_s%d" % g, [P, N], U8) for g in range(GROUPS)]
 
         def quantise_w3(g):
-            for n0, n1, copy in ((0, W3_CHUNK, nc.vector.tensor_copy), (W3_CHUNK, N, nc.scalar.copy if g else nc.vector.tensor_copy)):
+            for n0 in range(0, N, W3_CHUNK):
+                n1 = n0 + W3_CHUNK
                 rounded = keep("w3_bf%d_%d" % (g, n0), [P, (n1 - n0) * PACK], BF16)
-                copy(
+                nc.vector.tensor_copy(
                     out=rounded[:].rearrange("p (c i t) -> p c t i", i=2, t=PACK),
                     in_=w3_raw[g][:, :, n0:n1].rearrange("p t (c i) -> p c t i", i=2),
                 )
@@ -189,12 +193,18 @@ def tile_list_cavity_pulse_shaping_kernel(
 
         def direct_sum(a, jh):
             rows = slice(a * P, (a + 1) * P)
-            direct = bank(6 + a % 2 if jh == 0 else 4 + a % 4)
+            direct = bank((jh * NTILES + a) % 4)
             nc.tensor.matmul_mx(
                 out=direct[:], lhsT=w8_w[:, rows].bitcast(FP8X4), lhsT_scale=w8_s[:, rows],
                 rhs=v_w[jh][:].bitcast(FP8X4), rhs_scale=v_s[:, jh * J : (jh + 1) * J], start=True, stop=True,
             )
             return direct
+
+        parked = keep("parked", [P, NTILES, J], F32, "tab_then_parked")
+
+        def park(jh):
+            for a in GPSIMD_ADDS[jh]:
+                nc.scalar.copy(out=parked[:, a, :], in_=direct_sum(a, jh)[:])
 
         def read_out(jh):
             cols = slice(jh * J, (jh + 1) * J)
@@ -203,7 +213,7 @@ def tile_list_cavity_pulse_shaping_kernel(
 
             def drive_tile(a):
                 rows = slice(a * P, (a + 1) * P)
-                shaped = bank(4 + a % 2 if jh == 0 else a % 4)
+                shaped = bank(4 + (jh * NTILES + a) % 4)
                 for g in range(GROUPS):
                     nc.tensor.matmul_mx(
                         out=shaped[:], lhsT=w3_w[g][:, rows].bitcast(FP8X4), lhsT_scale=w3_s[g][:, rows],
@@ -211,20 +221,17 @@ def tile_list_cavity_pulse_shaping_kernel(
                         start=(g == 0), stop=(g == GROUPS - 1),
                     )
                 driven[a] = ring.tile([P, J], F32, name="driven")
-                nc.vector.tensor_tensor(driven[a][:], shaped[:], y_t[jh][:, a, :], MULT)
+                nc.vector.tensor_tensor(driven[a][:], shaped[:], y_tile(a, jh), MULT)
 
             def add_direct(a):
-                direct = direct_sum(a, jh)
                 if a in GPSIMD_ADDS[jh]:
-                    parked = ring.tile([P, J], F32, name="parked", bufs=3)
-                    nc.scalar.copy(out=parked[:], in_=direct[:])
-                    nc.gpsimd.tensor_tensor(y_t[jh][:, a, :], parked[:], driven[a][:], ADD)
+                    nc.gpsimd.tensor_tensor(y_tile(a, jh), parked[:, a, :], driven[a][:], ADD)
                 else:
-                    nc.vector.tensor_tensor(y_t[jh][:, a, :], direct[:], driven[a][:], ADD)
+                    nc.vector.tensor_tensor(y_tile(a, jh), direct_sum(a, jh)[:], driven[a][:], ADD)
                 if jh == HALVES - 1:
-                    nc.sync.dma_start(out=out_v[:, a, cols], in_=y_t[jh][:, a, :])
-                elif a % 2 == 1:
-                    nc.sync.dma_start(out=out_v[:, a - 1 : a + 1, cols], in_=y_t[jh][:, a - 1 : a + 1, :])
+                    nc.sync.dma_start(out=out_v[:, a, cols], in_=y_tile(a, jh))
+                elif a % 3 == 2:
+                    nc.sync.dma_start(out=out_v[:, a - 2 : a + 1, cols], in_=y_rows[a // 3][:, :, cols])
 
             drive_tile(0)
             for a in range(1, NTILES):
@@ -232,22 +239,26 @@ def tile_list_cavity_pulse_shaping_kernel(
                 add_direct(a - 1)
             add_direct(NTILES - 1)
 
-        quantise_w1(0, [nc.scalar.copy, nc.vector.tensor_copy])
+        quantise_w1(0, [nc.scalar.copy])
+        gather_words(0)
         shape(0, 0)
         quantise_w1(1, [nc.vector.tensor_copy])
         shape(1, 0)
+        gather_words(1)
         quantise_h(0, 0)
-        quantise_w3(0)
-        quantise_h(1, 0)
-        quantise_w3(1)
         shape(0, 1)
+        quantise_h(1, 0)
         shape(1, 1)
         quantise_h(0, 1)
+        park(0)
         quantise_h(1, 1)
+        quantise_w3(0)
+        quantise_w3(1)
         read_out(0)
         for q in range(4):
             nc.sync.dma_start(
                 out=out_3[:, 4 * q : 4 * q + 4, :].rearrange("g r m -> r g m").bitcast(I32),
                 in_=h_s[32 * q : 32 * q + 4, :].bitcast(I32).rearrange("r (g m) -> r g m", g=GROUPS),
             )
+        park(1)
         read_out(1)

@@ -26,12 +26,14 @@ J = 512
 HALVES = S // J
 NTILES = N // P
 W3_CHUNK = 256
-GPSIMD_ADDS = (range(0, 4), range(0, 4))
+FIRST_STAGE_BANKS = (((0, 1, 2, 3), (4, 5, 6, 7)), ((0, 1, 2, 3), (4, 5, 0, 1)))
+SHAPED_BANKS = ((6, 7), (4, 5, 0, 1, 6, 7))
+GPSIMD_ADDS = (range(0, 4), range(0, 3))
 
 
 def load_scale_rows(queue, plane, rows):
-    for q in range(4):
-        queue.dma_start(out=plane[32 * q : 32 * q + 4, :].bitcast(I32), in_=rows[4 * q : 4 * q + 4, :].bitcast(I32))
+    for r in range(4):
+        queue.dma_start(out=plane[r:P:32, :].bitcast(I32), in_=rows[r:16:4, :].bitcast(I32))
 
 
 def tile_list_cavity_pulse_shaping_kernel(
@@ -135,7 +137,7 @@ def tile_list_cavity_pulse_shaping_kernel(
             h_t[g, jh] = h
             pending = []
             for t in range(PACK):
-                e = bank(g * PACK + t)
+                e = bank(FIRST_STAGE_BANKS[jh][g][t])
                 m0 = t * P
                 nc.tensor.matmul_mx(
                     out=e[:], lhsT=w1_w[g][:, m0 : m0 + P].bitcast(FP8X4), lhsT_scale=w1_s[g][:, m0 : m0 + P],
@@ -179,11 +181,11 @@ def tile_list_cavity_pulse_shaping_kernel(
         w3_w = [keep("w3_w%d" % g, [P, N], U32) for g in range(GROUPS)]
         w3_s = [keep("w3_s%d" % g, [P, N], U8) for g in range(GROUPS)]
 
-        def quantise_w3(g):
-            for n0 in range(0, N, W3_CHUNK):
+        def quantise_w3(g, copies):
+            for n0, copy in zip(range(0, N, W3_CHUNK), copies):
                 n1 = n0 + W3_CHUNK
                 rounded = keep("w3_bf%d_%d" % (g, n0), [P, (n1 - n0) * PACK], BF16)
-                nc.vector.tensor_copy(
+                copy(
                     out=rounded[:].rearrange("p (c i t) -> p c t i", i=2, t=PACK),
                     in_=w3_raw[g][:, :, n0:n1].rearrange("p t (c i) -> p c t i", i=2),
                 )
@@ -193,7 +195,7 @@ def tile_list_cavity_pulse_shaping_kernel(
 
         def direct_sum(a, jh):
             rows = slice(a * P, (a + 1) * P)
-            direct = bank((jh * NTILES + a) % 4)
+            direct = bank(2 + a % 2)
             nc.tensor.matmul_mx(
                 out=direct[:], lhsT=w8_w[:, rows].bitcast(FP8X4), lhsT_scale=w8_s[:, rows],
                 rhs=v_w[jh][:].bitcast(FP8X4), rhs_scale=v_s[:, jh * J : (jh + 1) * J], start=True, stop=True,
@@ -213,7 +215,7 @@ def tile_list_cavity_pulse_shaping_kernel(
 
             def drive_tile(a):
                 rows = slice(a * P, (a + 1) * P)
-                shaped = bank(4 + (jh * NTILES + a) % 4)
+                shaped = bank(SHAPED_BANKS[jh][a % len(SHAPED_BANKS[jh])])
                 for g in range(GROUPS):
                     nc.tensor.matmul_mx(
                         out=shaped[:], lhsT=w3_w[g][:, rows].bitcast(FP8X4), lhsT_scale=w3_s[g][:, rows],
@@ -246,19 +248,19 @@ def tile_list_cavity_pulse_shaping_kernel(
         shape(1, 0)
         gather_words(1)
         quantise_h(0, 0)
-        shape(0, 1)
         quantise_h(1, 0)
+        quantise_w3(0, [nc.vector.tensor_copy] * 3)
+        quantise_w3(1, [nc.vector.tensor_copy, nc.scalar.copy, nc.scalar.copy])
+        shape(0, 1)
         shape(1, 1)
-        quantise_h(0, 1)
         park(0)
+        quantise_h(0, 1)
         quantise_h(1, 1)
-        quantise_w3(0)
-        quantise_w3(1)
         read_out(0)
-        for q in range(4):
+        for r in range(4):
             nc.sync.dma_start(
-                out=out_3[:, 4 * q : 4 * q + 4, :].rearrange("g r m -> r g m").bitcast(I32),
-                in_=h_s[32 * q : 32 * q + 4, :].bitcast(I32).rearrange("r (g m) -> r g m", g=GROUPS),
+                out=out_3[:, r:16:4, :].rearrange("g q m -> q g m").bitcast(I32),
+                in_=h_s[r:P:32, :].bitcast(I32).rearrange("q (g m) -> q g m", g=GROUPS),
             )
         park(1)
         read_out(1)

@@ -161,10 +161,10 @@ def tile_list_cavity_pulse_shaping_kernel(
                 out=out_1[g * PASS : (g + 1) * PASS, cols].rearrange("(p t) j -> p t j", t=PACK), in_=h[:]
             )
 
-        def quantise_h(g, jh):
+        def quantise_h(g, jh, copies):
             rounded = pair.tile([P, J * PACK], BF16, name="h_bf", align_bytes=64)
-            for c0 in range(0, J // 2, J // 4):
-                nc.scalar.copy(
+            for c0, copy in zip(range(0, J // 2, J // 4), copies):
+                copy(
                     out=rounded[:].rearrange("p (c i t) -> p c t i", i=2, t=PACK)[:, c0 : c0 + J // 4],
                     in_=h_t[g, jh][:].rearrange("p t (c i) -> p c t i", i=2)[:, c0 : c0 + J // 4],
                 )
@@ -182,14 +182,17 @@ def tile_list_cavity_pulse_shaping_kernel(
         w3_s = [keep("w3_s%d" % g, [P, N], U8) for g in range(GROUPS)]
 
         def quantise_w3(g, copies):
+            rounded = keep("w3_bf%d" % g, [P, N * PACK], BF16)
             for n0, copy in zip(range(0, N, W3_CHUNK), copies):
                 n1 = n0 + W3_CHUNK
-                rounded = keep("w3_bf%d_%d" % (g, n0), [P, (n1 - n0) * PACK], BF16)
                 copy(
-                    out=rounded[:].rearrange("p (c i t) -> p c t i", i=2, t=PACK),
+                    out=rounded[:, n0 * PACK : n1 * PACK].rearrange("p (c i t) -> p c t i", i=2, t=PACK),
                     in_=w3_raw[g][:, :, n0:n1].rearrange("p t (c i) -> p c t i", i=2),
                 )
-                nc.vector.quantize_mx(out=w3_w[g][:, n0:n1].bitcast(FP8X4), scales=w3_s[g][:, n0:n1], in_=rounded[:])
+            for n0, n1 in ((0, W3_CHUNK), (W3_CHUNK, N)):
+                nc.vector.quantize_mx(
+                    out=w3_w[g][:, n0:n1].bitcast(FP8X4), scales=w3_s[g][:, n0:n1], in_=rounded[:, n0 * PACK : n1 * PACK]
+                )
 
         out_v = out_0.rearrange("(a p) j -> p a j", p=P)
 
@@ -230,10 +233,7 @@ def tile_list_cavity_pulse_shaping_kernel(
                     nc.gpsimd.tensor_tensor(y_tile(a, jh), parked[:, a, :], driven[a][:], ADD)
                 else:
                     nc.vector.tensor_tensor(y_tile(a, jh), direct_sum(a, jh)[:], driven[a][:], ADD)
-                if jh == HALVES - 1:
-                    nc.sync.dma_start(out=out_v[:, a, cols], in_=y_tile(a, jh))
-                elif a % 3 == 2:
-                    nc.sync.dma_start(out=out_v[:, a - 2 : a + 1, cols], in_=y_rows[a // 3][:, :, cols])
+                nc.sync.dma_start(out=out_v[:, a, cols], in_=y_tile(a, jh))
 
             drive_tile(0)
             for a in range(1, NTILES):
@@ -243,19 +243,19 @@ def tile_list_cavity_pulse_shaping_kernel(
 
         quantise_w1(0, [nc.scalar.copy])
         gather_words(0)
-        shape(0, 0)
         quantise_w1(1, [nc.vector.tensor_copy])
+        shape(0, 0)
         shape(1, 0)
         gather_words(1)
-        quantise_h(0, 0)
-        quantise_h(1, 0)
+        quantise_h(0, 0, [nc.scalar.copy] * 2)
+        quantise_h(1, 0, [nc.scalar.copy] * 2)
         quantise_w3(0, [nc.vector.tensor_copy] * 3)
         quantise_w3(1, [nc.vector.tensor_copy, nc.scalar.copy, nc.scalar.copy])
         shape(0, 1)
         shape(1, 1)
         park(0)
-        quantise_h(0, 1)
-        quantise_h(1, 1)
+        quantise_h(0, 1, [nc.scalar.copy] * 2)
+        quantise_h(1, 1, [nc.scalar.copy, nc.vector.tensor_copy])
         read_out(0)
         for r in range(4):
             nc.sync.dma_start(

@@ -28,7 +28,7 @@ NTILES = N // P
 W3_CHUNK = 256
 FIRST_STAGE_BANKS = (((0, 1, 2, 3), (4, 5, 6, 7)), ((0, 1, 2, 3), (4, 5, 0, 1)))
 SHAPED_BANKS = ((6, 7), (4, 5, 0, 1, 6, 7))
-GPSIMD_ADDS = (range(0, 4), range(0, 3))
+GPSIMD_ADDS = (range(0, 2), range(0, 3))
 
 
 def load_scale_rows(queue, plane, rows):
@@ -62,7 +62,7 @@ def tile_list_cavity_pulse_shaping_kernel(
         w8_w = keep("w8_w", [P, N], U32)
         w8_s = keep("w8_s", [P, N], U8)
         cub_t = keep("cub_t", [P, GROUPS, PACK], F32)
-        w1_raw = [keep("w1_raw%d" % g, [P, PACK, PASS], F32) for g in range(GROUPS)]
+        w1_raw = [keep("w1_raw%d" % g, [P, PACK, PASS], F32, "w1_then_h" if g else None) for g in range(GROUPS)]
         w3_raw = [keep("w3_raw%d" % g, [P, PACK, N], F32) for g in range(GROUPS)]
         y_rows = [keep("y_rows%d" % b, [P, NTILES // 2, S], F32) for b in range(2)]
 
@@ -133,7 +133,7 @@ def tile_list_cavity_pulse_shaping_kernel(
 
         def shape(g, jh):
             cols = slice(jh * J, (jh + 1) * J)
-            h = keep("h%d%d" % (g, jh), [P, PACK, J], F32)
+            h = keep("h%d%d" % (g, jh), [P, PACK, J], F32, None if g or jh else "w1_then_h")
             h_t[g, jh] = h
             pending = []
             for t in range(PACK):
@@ -253,9 +253,9 @@ def tile_list_cavity_pulse_shaping_kernel(
         quantise_w3(1, [nc.vector.tensor_copy, nc.scalar.copy, nc.scalar.copy])
         shape(0, 1)
         shape(1, 1)
-        park(0)
         quantise_h(0, 1, [nc.scalar.copy] * 2)
-        quantise_h(1, 1, [nc.scalar.copy, nc.vector.tensor_copy])
+        park(0)
+        quantise_h(1, 1, [nc.scalar.copy] * 2)
         read_out(0)
         for r in range(4):
             nc.sync.dma_start(

@@ -16,7 +16,6 @@ FP4X4 = mybir.dt.float4_e2m1fn_x4
 MULT = mybir.AluOpType.mult
 ADD = mybir.AluOpType.add
 SQUARE = mybir.ActivationFunctionType.Square
-COPY = mybir.ActivationFunctionType.Copy
 
 P = 128
 PACK = 4
@@ -25,15 +24,25 @@ GROUPS = H // PASS
 J = 512
 HALVES = S // J
 NTILES = N // P
-W3_CHUNK = 256
-FIRST_STAGE_BANKS = (((0, 1, 2, 3), (4, 5, 6, 7)), ((0, 1, 2, 3), (4, 5, 0, 1)))
-SHAPED_BANKS = ((6, 7), (4, 5, 0, 1, 6, 7))
-GPSIMD_ADDS = (range(0, 2), range(0, 3))
+DRIVE_TILES = NTILES // 2
+QUADRANTS = 4
+SCALE_ROWS = 4
+RING = 6
+
+W3_PIECE = 256
+
+E_BANKS = (((0, 1, 2, 3), (4, 5, 6, 7)), ((0, 1, 2, 3), (4, 5, 0, 1)))
+W3_SUM_BANKS = ((6, 7, 6, 7, 6, 7), (4, 5, 0, 1, 6, 7))
+W8_SUM_BANKS = ((2, 3, 2, 3, 2, 3), (2, 4, 3, 5, 2, 0))
+
+GPSIMD_ADDS = (range(0, 2), range(0, NTILES, 2))
 
 
-def load_scale_rows(queue, plane, rows):
-    for r in range(4):
-        queue.dma_start(out=plane[r:P:32, :].bitcast(I32), in_=rows[r:16:4, :].bitcast(I32))
+def load_scale_rows(nc, plane, rows):
+    for r in range(SCALE_ROWS):
+        nc.sync.dma_start(
+            out=plane[r:P:32, :].bitcast(I32), in_=rows[r : QUADRANTS * SCALE_ROWS : SCALE_ROWS, :].bitcast(I32)
+        )
 
 
 def tile_list_cavity_pulse_shaping_kernel(
@@ -42,7 +51,7 @@ def tile_list_cavity_pulse_shaping_kernel(
     nc = tc.nc
     with ExitStack() as ctx:
         held = ctx.enter_context(tc.tile_pool(name="held", bufs=1))
-        ring = ctx.enter_context(tc.tile_pool(name="ring", bufs=5))
+        ring = ctx.enter_context(tc.tile_pool(name="ring", bufs=RING))
         pair = ctx.enter_context(tc.tile_pool(name="pair", bufs=2))
         psum = ctx.enter_context(tc.psum_pool(name="psum", bufs=1))
 
@@ -64,10 +73,10 @@ def tile_list_cavity_pulse_shaping_kernel(
         cub_t = keep("cub_t", [P, GROUPS, PACK], F32)
         w1_raw = [keep("w1_raw%d" % g, [P, PACK, PASS], F32, "w1_then_h" if g else None) for g in range(GROUPS)]
         w3_raw = [keep("w3_raw%d" % g, [P, PACK, N], F32) for g in range(GROUPS)]
-        y_rows = [keep("y_rows%d" % b, [P, NTILES // 2, S], F32) for b in range(2)]
+        y_rows = [keep("y_rows%d" % b, [P, DRIVE_TILES, S], F32) for b in range(NTILES // DRIVE_TILES)]
 
         def y_tile(a, jh):
-            return y_rows[a // 3][:, a % 3, jh * J : (jh + 1) * J]
+            return y_rows[a // DRIVE_TILES][:, a % DRIVE_TILES, jh * J : (jh + 1) * J]
 
         nc.vector.memset(tab_s[:].bitcast(I32), 0)
         nc.vector.memset(w4_s_raw[:].bitcast(I32), 0)
@@ -76,23 +85,24 @@ def tile_list_cavity_pulse_shaping_kernel(
 
         w1_rows = w1.rearrange("(p i) r -> p i r", i=PACK)
         drive_v = drive.rearrange("(a p) j -> p a j", p=P)
-        load_scale_rows(nc.sync, tab_s_rows, tab_scales[0])
+        load_scale_rows(nc, tab_s_rows, tab_scales[0])
         nc.sync.dma_start(out=w1_raw[0][:], in_=w1_rows[:, :, 0:PASS])
-        nc.sync.dma_start(offsets[:], offs)
-        load_scale_rows(nc.sync, w4_s_rows, w4_scales[0])
         nc.sync.dma_start(out=w4_raw[:].bitcast(I32), in_=w4_words[0].bitcast(I32))
+        nc.sync.dma_start(offsets[:], offs)
+        load_scale_rows(nc, w4_s_rows, w4_scales[0])
         nc.sync.dma_start(out=tab_w[:].bitcast(I32), in_=tab_words[0].rearrange("p n t -> p (n t)").bitcast(I32))
         nc.sync.dma_start(out=w1_raw[1][:], in_=w1_rows[:, :, PASS : 2 * PASS])
         for g in range(GROUPS):
             nc.sync.dma_start(out=w3_raw[g][:], in_=w3[g * PASS : (g + 1) * PASS, :].rearrange("(p i) n -> p i n", i=PACK))
         nc.sync.dma_start(out=w8_w[:].bitcast(I32), in_=w8_words[0].rearrange("p n t -> p (n t)").bitcast(I32))
-        load_scale_rows(nc.sync, w8_s, w8_scales[0])
-        for b in range(2):
-            nc.sync.dma_start(out=y_rows[b][:], in_=drive_v[:, 3 * b : 3 * b + 3, :])
+        load_scale_rows(nc, w8_s, w8_scales[0])
+        for b in range(NTILES // DRIVE_TILES):
+            nc.sync.dma_start(out=y_rows[b][:], in_=drive_v[:, DRIVE_TILES * b : DRIVE_TILES * (b + 1), :])
 
         def place_scale_rows(plane, rows):
-            for q in range(4):
-                nc.vector.tensor_copy(out=plane[32 * q : 32 * q + 4, :].bitcast(I32), in_=rows[32 * q : 32 * q + 4, :].bitcast(I32))
+            for q in range(QUADRANTS):
+                live = slice(32 * q, 32 * q + SCALE_ROWS)
+                nc.vector.tensor_copy(out=plane[live, :].bitcast(I32), in_=rows[live, :].bitcast(I32))
 
         w4_w = keep("w4_w", [P, 2 * H], U8)
         w4_s = keep("w4_s", [P, H], U8)
@@ -117,14 +127,12 @@ def tile_list_cavity_pulse_shaping_kernel(
         w1_w = [keep("w1_w%d" % g, [P, PASS], U32) for g in range(GROUPS)]
         w1_s = [keep("w1_s%d" % g, [P, PASS], U8) for g in range(GROUPS)]
 
-        def quantise_w1(g, copies):
+        def quantise_w1(g, copy):
             rounded = keep("w1_bf%d" % g, [P, PASS * PACK], BF16)
-            share = P // len(copies)
-            for c, copy in enumerate(copies):
-                copy(
-                    out=rounded[:].rearrange("p (t m i) -> p m t i", t=PACK, i=PACK)[:, c * share : (c + 1) * share],
-                    in_=w1_raw[g][:].rearrange("p i (m t) -> p m t i", t=PACK)[:, c * share : (c + 1) * share],
-                )
+            copy(
+                out=rounded[:].rearrange("p (t m i) -> p m t i", t=PACK, i=PACK),
+                in_=w1_raw[g][:].rearrange("p i (m t) -> p m t i", t=PACK),
+            )
             nc.vector.quantize_mx(out=w1_w[g][:].bitcast(FP8X4), scales=w1_s[g][:], in_=rounded[:])
 
         h_w = [keep("h_w%d" % g, [P, S], U32) for g in range(GROUPS)]
@@ -135,9 +143,10 @@ def tile_list_cavity_pulse_shaping_kernel(
             cols = slice(jh * J, (jh + 1) * J)
             h = keep("h%d%d" % (g, jh), [P, PACK, J], F32, None if g or jh else "w1_then_h")
             h_t[g, jh] = h
-            pending = []
-            for t in range(PACK):
-                e = bank(FIRST_STAGE_BANKS[jh][g][t])
+            sums, factors = {}, {}
+
+            def square(t):
+                e = bank(E_BANKS[jh][g][t])
                 m0 = t * P
                 nc.tensor.matmul_mx(
                     out=e[:], lhsT=w1_w[g][:, m0 : m0 + P].bitcast(FP8X4), lhsT_scale=w1_s[g][:, m0 : m0 + P],
@@ -152,21 +161,27 @@ def tile_list_cavity_pulse_shaping_kernel(
                 nc.scalar.activation(u[:], e[:], SQUARE)
                 factor = ring.tile([P, J], F32, name="factor")
                 nc.gpsimd.tensor_scalar(factor[:], u[:], cub_t[:, g, t : t + 1], -1.0, MULT, ADD)
-                pending.append((h[:, t, :], e, factor))
-                if len(pending) == 2 or t == PACK - 1:
-                    for row, e_done, u_done in pending[: 1 if t < PACK - 1 else 2]:
-                        nc.vector.scalar_tensor_tensor(row, e_done[:], -1.0, u_done[:], MULT, MULT)
-                    pending = pending[1:]
+                sums[t], factors[t] = e, factor
+
+            def multiply(t):
+                nc.vector.scalar_tensor_tensor(h[:, t, :], sums[t][:], -1.0, factors[t][:], MULT, MULT)
+
+            square(0)
+            for t in range(1, PACK):
+                square(t)
+                multiply(t - 1)
+            multiply(PACK - 1)
             nc.sync.dma_start(
                 out=out_1[g * PASS : (g + 1) * PASS, cols].rearrange("(p t) j -> p t j", t=PACK), in_=h[:]
             )
 
-        def quantise_h(g, jh, copies):
+        def quantise_h(g, jh):
             rounded = pair.tile([P, J * PACK], BF16, name="h_bf", align_bytes=64)
-            for c0, copy in zip(range(0, J // 2, J // 4), copies):
-                copy(
-                    out=rounded[:].rearrange("p (c i t) -> p c t i", i=2, t=PACK)[:, c0 : c0 + J // 4],
-                    in_=h_t[g, jh][:].rearrange("p t (c i) -> p c t i", i=2)[:, c0 : c0 + J // 4],
+            pairs = J // 2
+            for c0 in range(0, pairs, pairs // 2):
+                nc.scalar.copy(
+                    out=rounded[:].rearrange("p (c i t) -> p c t i", i=2, t=PACK)[:, c0 : c0 + pairs // 2],
+                    in_=h_t[g, jh][:].rearrange("p t (c i) -> p c t i", i=2)[:, c0 : c0 + pairs // 2],
                 )
             nc.vector.quantize_mx(
                 out=h_w[g][:, jh * J : (jh + 1) * J].bitcast(FP8X4),
@@ -183,22 +198,22 @@ def tile_list_cavity_pulse_shaping_kernel(
 
         def quantise_w3(g, copies):
             rounded = keep("w3_bf%d" % g, [P, N * PACK], BF16)
-            for n0, copy in zip(range(0, N, W3_CHUNK), copies):
-                n1 = n0 + W3_CHUNK
+            for n0, copy in zip(range(0, N, W3_PIECE), copies):
+                n1 = n0 + W3_PIECE
                 copy(
                     out=rounded[:, n0 * PACK : n1 * PACK].rearrange("p (c i t) -> p c t i", i=2, t=PACK),
                     in_=w3_raw[g][:, :, n0:n1].rearrange("p t (c i) -> p c t i", i=2),
                 )
-            for n0, n1 in ((0, W3_CHUNK), (W3_CHUNK, N)):
+            for n0, n1 in ((0, W3_PIECE), (W3_PIECE, N)):
                 nc.vector.quantize_mx(
                     out=w3_w[g][:, n0:n1].bitcast(FP8X4), scales=w3_s[g][:, n0:n1], in_=rounded[:, n0 * PACK : n1 * PACK]
                 )
 
         out_v = out_0.rearrange("(a p) j -> p a j", p=P)
 
-        def direct_sum(a, jh):
+        def w8_sum(a, jh):
             rows = slice(a * P, (a + 1) * P)
-            direct = bank(2 + a % 2)
+            direct = bank(W8_SUM_BANKS[jh][a])
             nc.tensor.matmul_mx(
                 out=direct[:], lhsT=w8_w[:, rows].bitcast(FP8X4), lhsT_scale=w8_s[:, rows],
                 rhs=v_w[jh][:].bitcast(FP8X4), rhs_scale=v_s[:, jh * J : (jh + 1) * J], start=True, stop=True,
@@ -209,16 +224,15 @@ def tile_list_cavity_pulse_shaping_kernel(
 
         def park(jh):
             for a in GPSIMD_ADDS[jh]:
-                nc.scalar.copy(out=parked[:, a, :], in_=direct_sum(a, jh)[:])
+                nc.scalar.copy(out=parked[:, a, :], in_=w8_sum(a, jh)[:])
 
         def read_out(jh):
             cols = slice(jh * J, (jh + 1) * J)
-
             driven = {}
 
             def drive_tile(a):
                 rows = slice(a * P, (a + 1) * P)
-                shaped = bank(SHAPED_BANKS[jh][a % len(SHAPED_BANKS[jh])])
+                shaped = bank(W3_SUM_BANKS[jh][a])
                 for g in range(GROUPS):
                     nc.tensor.matmul_mx(
                         out=shaped[:], lhsT=w3_w[g][:, rows].bitcast(FP8X4), lhsT_scale=w3_s[g][:, rows],
@@ -228,38 +242,38 @@ def tile_list_cavity_pulse_shaping_kernel(
                 driven[a] = ring.tile([P, J], F32, name="driven")
                 nc.vector.tensor_tensor(driven[a][:], shaped[:], y_tile(a, jh), MULT)
 
-            def add_direct(a):
+            def add_w8_sum(a):
                 if a in GPSIMD_ADDS[jh]:
                     nc.gpsimd.tensor_tensor(y_tile(a, jh), parked[:, a, :], driven[a][:], ADD)
                 else:
-                    nc.vector.tensor_tensor(y_tile(a, jh), direct_sum(a, jh)[:], driven[a][:], ADD)
+                    nc.vector.tensor_tensor(y_tile(a, jh), w8_sum(a, jh)[:], driven[a][:], ADD)
                 nc.sync.dma_start(out=out_v[:, a, cols], in_=y_tile(a, jh))
 
             drive_tile(0)
             for a in range(1, NTILES):
                 drive_tile(a)
-                add_direct(a - 1)
-            add_direct(NTILES - 1)
+                add_w8_sum(a - 1)
+            add_w8_sum(NTILES - 1)
 
-        quantise_w1(0, [nc.scalar.copy])
+        quantise_w1(0, nc.scalar.copy)
         gather_words(0)
-        quantise_w1(1, [nc.vector.tensor_copy])
+        quantise_w1(1, nc.vector.tensor_copy)
         shape(0, 0)
         shape(1, 0)
         gather_words(1)
-        quantise_h(0, 0, [nc.scalar.copy] * 2)
-        quantise_h(1, 0, [nc.scalar.copy] * 2)
+        quantise_h(0, 0)
+        quantise_h(1, 0)
         quantise_w3(0, [nc.vector.tensor_copy] * 3)
         quantise_w3(1, [nc.vector.tensor_copy, nc.scalar.copy, nc.scalar.copy])
         shape(0, 1)
         shape(1, 1)
-        quantise_h(0, 1, [nc.scalar.copy] * 2)
+        quantise_h(0, 1)
         park(0)
-        quantise_h(1, 1, [nc.scalar.copy] * 2)
+        quantise_h(1, 1)
         read_out(0)
-        for r in range(4):
+        for r in range(SCALE_ROWS):
             nc.sync.dma_start(
-                out=out_3[:, r:16:4, :].rearrange("g q m -> q g m").bitcast(I32),
+                out=out_3[:, r : QUADRANTS * SCALE_ROWS : SCALE_ROWS, :].rearrange("g q m -> q g m").bitcast(I32),
                 in_=h_s[r:P:32, :].bitcast(I32).rearrange("q (g m) -> q g m", g=GROUPS),
             )
         park(1)

@@ -15,6 +15,7 @@ FP8X4 = mybir.dt.float8_e4m3fn_x4
 FP4X4 = mybir.dt.float4_e2m1fn_x4
 MULT = mybir.AluOpType.mult
 ADD = mybir.AluOpType.add
+MAX = mybir.AluOpType.max
 SQUARE = mybir.ActivationFunctionType.Square
 
 P = 128
@@ -24,25 +25,25 @@ GROUPS = H // PASS
 J = 512
 HALVES = S // J
 NTILES = N // P
-DRIVE_TILES = NTILES // 2
 QUADRANTS = 4
 SCALE_ROWS = 4
+ROWS = QUADRANTS * SCALE_ROWS
+ROW0 = P - ROWS
+
+LAST_QUADRANT = P - 32
+NEIGHBOURS = 4
+
+PIECE = 256
+W3_ON_VECTOR = 4
+W3_PIECES = GROUPS * N // PIECE
+
+GPSIMD_ADDS = (range(0, 4), range(0, NTILES, 2))
+EARLY_COPIES = 2
+
+W3_BANKS = 4
+EARLY_BANKS, LATE_BANKS = (0, 1), (4, 5)
+ADD_BANKS = {(4, 0): 6, (5, 0): 7, (1, 1): 6, (3, 1): 7, (5, 1): 5}
 RING = 6
-
-W3_PIECE = 256
-
-E_BANKS = (((0, 1, 2, 3), (4, 5, 6, 7)), ((0, 1, 2, 3), (4, 5, 0, 1)))
-W3_SUM_BANKS = ((6, 7, 6, 7, 6, 7), (4, 5, 0, 1, 6, 7))
-W8_SUM_BANKS = ((2, 3, 2, 3, 2, 3), (2, 4, 3, 5, 2, 0))
-
-GPSIMD_ADDS = (range(0, 2), range(0, NTILES, 2))
-
-
-def load_scale_rows(nc, plane, rows):
-    for r in range(SCALE_ROWS):
-        nc.sync.dma_start(
-            out=plane[r:P:32, :].bitcast(I32), in_=rows[r : QUADRANTS * SCALE_ROWS : SCALE_ROWS, :].bitcast(I32)
-        )
 
 
 def tile_list_cavity_pulse_shaping_kernel(
@@ -52,7 +53,7 @@ def tile_list_cavity_pulse_shaping_kernel(
     with ExitStack() as ctx:
         held = ctx.enter_context(tc.tile_pool(name="held", bufs=1))
         ring = ctx.enter_context(tc.tile_pool(name="ring", bufs=RING))
-        pair = ctx.enter_context(tc.tile_pool(name="pair", bufs=2))
+        driven_ring = ctx.enter_context(tc.tile_pool(name="driven_ring", bufs=RING))
         psum = ctx.enter_context(tc.psum_pool(name="psum", bufs=1))
 
         def bank(b):
@@ -61,68 +62,68 @@ def tile_list_cavity_pulse_shaping_kernel(
         def keep(name, shape, dtype, tag=None):
             return held.tile(shape, dtype, name=name, tag=tag or name, align_bytes=64)
 
+        def half(jh):
+            return slice(jh * J, (jh + 1) * J)
+
         offsets = held.tile([P, S // 16], U16, name="offsets")
-        tab_w = keep("tab_w", [P, T], U32, "tab_then_parked")
         tab_s_rows = keep("tab_s_rows", [P, T], U8)
-        tab_s = keep("tab_s", [P, T], U8)
-        w4_raw = keep("w4_raw", [P, 2 * H], U8)
-        w4_s_rows = keep("w4_s_rows", [P, H], U8)
-        w4_s_raw = keep("w4_s_raw", [P, H], U8)
-        w8_w = keep("w8_w", [P, N], U32)
-        w8_s = keep("w8_s", [P, N], U8)
+        w4_s_rows = keep("w4_s_rows", [P, H], U8, "w4_s_then_w1_then_h")
+        rows = keep("rows", [P, S + H + N], U8, "rows_then_drive")
+        planes = keep("planes", [P, S + H + N], U8)
+        v_s, w4_s, w8_s = planes[:, 0:S], planes[:, S : S + H], planes[:, S + H : S + H + N]
+        tab_w = keep("tab_w", [P, T], U32)
+        w4_raw = keep("w4_raw", [P, 2 * H], U8, "w4_then_w3")
         cub_t = keep("cub_t", [P, GROUPS, PACK], F32)
-        w1_raw = [keep("w1_raw%d" % g, [P, PACK, PASS], F32, "w1_then_h" if g else None) for g in range(GROUPS)]
-        w3_raw = [keep("w3_raw%d" % g, [P, PACK, N], F32) for g in range(GROUPS)]
-        y_rows = [keep("y_rows%d" % b, [P, DRIVE_TILES, S], F32) for b in range(NTILES // DRIVE_TILES)]
 
-        def y_tile(a, jh):
-            return y_rows[a // DRIVE_TILES][:, a % DRIVE_TILES, jh * J : (jh + 1) * J]
-
-        nc.vector.memset(tab_s[:].bitcast(I32), 0)
-        nc.vector.memset(w4_s_raw[:].bitcast(I32), 0)
-        nc.vector.memset(w8_s[:].bitcast(I32), 0)
+        nc.vector.memset(tab_s_rows[0:ROW0, :].bitcast(I32), 0)
+        nc.vector.memset(w4_s_rows[0:ROW0, :].bitcast(I32), 0)
+        nc.vector.memset(planes[:].bitcast(I32), 0)
         nc.gpsimd.dma_start(out=cub_t[:], in_=cub.rearrange("(g p t) -> p g t", g=GROUPS, t=PACK))
 
         w1_rows = w1.rearrange("(p i) r -> p i r", i=PACK)
-        drive_v = drive.rearrange("(a p) j -> p a j", p=P)
-        load_scale_rows(nc, tab_s_rows, tab_scales[0])
+        nc.sync.dma_start(out=tab_s_rows[ROW0:P, :].bitcast(I32), in_=tab_scales[0].bitcast(I32))
+        nc.sync.dma_start(offsets[:], offs)
+        nc.sync.dma_start(out=w4_s_rows[ROW0:P, :].bitcast(I32), in_=w4_scales[0].bitcast(I32))
+        nc.sync.dma_start(out=rows[ROW0:P, S + H : S + H + N].bitcast(I32), in_=w8_scales[0].bitcast(I32))
+        w1_raw = [keep("w1_raw0", [P, PACK, PASS], F32, "w1_then_w3")]
         nc.sync.dma_start(out=w1_raw[0][:], in_=w1_rows[:, :, 0:PASS])
         nc.sync.dma_start(out=w4_raw[:].bitcast(I32), in_=w4_words[0].bitcast(I32))
-        nc.sync.dma_start(offsets[:], offs)
-        load_scale_rows(nc, w4_s_rows, w4_scales[0])
         nc.sync.dma_start(out=tab_w[:].bitcast(I32), in_=tab_words[0].rearrange("p n t -> p (n t)").bitcast(I32))
-        nc.sync.dma_start(out=w1_raw[1][:], in_=w1_rows[:, :, PASS : 2 * PASS])
-        for g in range(GROUPS):
-            nc.sync.dma_start(out=w3_raw[g][:], in_=w3[g * PASS : (g + 1) * PASS, :].rearrange("(p i) n -> p i n", i=PACK))
-        nc.sync.dma_start(out=w8_w[:].bitcast(I32), in_=w8_words[0].rearrange("p n t -> p (n t)").bitcast(I32))
-        load_scale_rows(nc, w8_s, w8_scales[0])
-        for b in range(NTILES // DRIVE_TILES):
-            nc.sync.dma_start(out=y_rows[b][:], in_=drive_v[:, DRIVE_TILES * b : DRIVE_TILES * (b + 1), :])
 
-        def place_scale_rows(plane, rows):
-            for q in range(QUADRANTS):
-                live = slice(32 * q, 32 * q + SCALE_ROWS)
-                nc.vector.tensor_copy(out=plane[live, :].bitcast(I32), in_=rows[live, :].bitcast(I32))
-
-        w4_w = keep("w4_w", [P, 2 * H], U8)
-        w4_s = keep("w4_s", [P, H], U8)
-        v_s = keep("v_s", [P, S], U8)
-        v_w = [keep("v_w%d" % jh, [P, J], U32) for jh in range(HALVES)]
-
-        def gather_words(jh):
-            nc.vector.tensor_copy(v_w[jh][:], tab_w[:].indirect(offsets[:, jh * (J // 16) : (jh + 1) * (J // 16)]))
-
-        place_scale_rows(tab_s, tab_s_rows)
-        nc.vector.tensor_copy(v_s[:], tab_s[:].indirect(offsets[:]))
-        place_scale_rows(w4_s_raw, w4_s_rows)
+        v_s_rows = keep("v_s_rows", [P, S], U8)
+        nc.vector.tensor_copy(v_s_rows[:], tab_s_rows[:].indirect(offsets[:]))
+        nc.vector.tensor_copy(out=rows[LAST_QUADRANT:P, 0:S].bitcast(I32), in_=v_s_rows[LAST_QUADRANT:P, :].bitcast(I32))
         nc.vector.tensor_copy(
-            out=w4_s[:].rearrange("p (g t c m) -> p g c t m", g=GROUPS, t=PACK, m=16),
-            in_=w4_s_raw[:].rearrange("p (g c m t) -> p g c t m", g=GROUPS, t=PACK, m=16),
+            out=rows[:, S : S + H].rearrange("p (g t c m) -> p g c t m", g=GROUPS, t=PACK, m=16),
+            in_=w4_s_rows[:].rearrange("p (g c m t) -> p g c t m", g=GROUPS, t=PACK, m=16),
         )
+        for r in range(SCALE_ROWS):
+            nc.sync.dma_start(out=planes[r:P:32, :].bitcast(I32), in_=rows[ROW0 + r : P : SCALE_ROWS, :].bitcast(I32))
+        w1_raw.append(keep("w1_raw1", [P, PACK, PASS], F32, "w4_s_then_w1_then_h"))
+        nc.sync.dma_start(out=w1_raw[1][:], in_=w1_rows[:, :, PASS : 2 * PASS])
+
+        v_w = [keep("v_w%d" % jh, [P, J], U32) for jh in range(HALVES)]
+        w4_w = keep("w4_w", [P, 2 * H], U8)
         nc.vector.tensor_copy(
             out=w4_w[:].bitcast(U16).rearrange("p (g t c m) -> p g c t m", g=GROUPS, t=PACK, m=8),
             in_=w4_raw[:].bitcast(U16).rearrange("p (g c m t) -> p g c t m", g=GROUPS, t=PACK, m=8),
         )
+
+        def w8_sum(a, jh, b):
+            tile_cols = slice(a * P, (a + 1) * P)
+            direct = bank(b)
+            nc.tensor.matmul_mx(
+                out=direct[:], lhsT=w8_w[:, tile_cols].bitcast(FP8X4), lhsT_scale=w8_s[:, tile_cols],
+                rhs=v_w[jh][:].bitcast(FP8X4), rhs_scale=v_s[:, half(jh)], start=True, stop=True,
+            )
+            return direct
+
+        parked = {}
+
+        def park(jh, tiles, banks):
+            for n, a in enumerate(tiles):
+                parked[a, jh] = keep("parked%d%d" % (jh, a), [P, J], F32)
+                nc.scalar.copy(out=parked[a, jh][:], in_=w8_sum(a, jh, banks[n % len(banks)])[:])
 
         w1_w = [keep("w1_w%d" % g, [P, PASS], U32) for g in range(GROUPS)]
         w1_s = [keep("w1_s%d" % g, [P, PASS], U8) for g in range(GROUPS)]
@@ -135,119 +136,113 @@ def tile_list_cavity_pulse_shaping_kernel(
             )
             nc.vector.quantize_mx(out=w1_w[g][:].bitcast(FP8X4), scales=w1_s[g][:], in_=rounded[:])
 
-        h_w = [keep("h_w%d" % g, [P, S], U32) for g in range(GROUPS)]
-        h_s = keep("h_s", [P, GROUPS * S], U8)
-        h_t = {}
+        h_w = [keep("h_w%d" % jh, [P, GROUPS * J], U32) for jh in range(HALVES)]
+        h_s = [keep("h_s%d" % jh, [P, GROUPS * J], U8) for jh in range(HALVES)]
+        h = {}
 
-        def shape(g, jh):
-            cols = slice(jh * J, (jh + 1) * J)
-            h = keep("h%d%d" % (g, jh), [P, PACK, J], F32, None if g or jh else "w1_then_h")
-            h_t[g, jh] = h
+        def in_ring(name, t):
+            return ring.tile([P, J], F32, name=name)
+
+        def in_own_buffer(name, t):
+            return keep("%s%d" % (name, t), [P, J], F32)
+
+        def shape(g, jh, out, stage):
+            h[g, jh] = out
             sums, factors = {}, {}
 
             def square(t):
-                e = bank(E_BANKS[jh][g][t])
+                e = bank(PACK * jh + t)
                 m0 = t * P
-                nc.tensor.matmul_mx(
-                    out=e[:], lhsT=w1_w[g][:, m0 : m0 + P].bitcast(FP8X4), lhsT_scale=w1_s[g][:, m0 : m0 + P],
-                    rhs=v_w[jh][:].bitcast(FP8X4), rhs_scale=v_s[:, cols], start=True, stop=False,
-                )
                 c0 = g * PASS + m0
-                nc.tensor.matmul_mx(
-                    out=e[:], lhsT=w4_w[:, 2 * c0 : 2 * (c0 + P)].bitcast(FP4X4), lhsT_scale=w4_s[:, c0 : c0 + P],
-                    rhs=v_w[jh][:].bitcast(FP8X4), rhs_scale=v_s[:, cols], start=False, stop=True,
-                )
-                u = ring.tile([P, J], F32, name="u")
+                weights = [
+                    (w1_w[g][:, m0 : m0 + P].bitcast(FP8X4), w1_s[g][:, m0 : m0 + P]),
+                    (w4_w[:, 2 * c0 : 2 * (c0 + P)].bitcast(FP4X4), w4_s[:, c0 : c0 + P]),
+                ]
+                for n, (words, scales) in enumerate(weights if g or jh else reversed(weights)):
+                    nc.tensor.matmul_mx(
+                        out=e[:], lhsT=words, lhsT_scale=scales,
+                        rhs=v_w[jh][:].bitcast(FP8X4), rhs_scale=v_s[:, half(jh)], start=(n == 0), stop=(n == 1),
+                    )
+                u = stage("u", t)
                 nc.scalar.activation(u[:], e[:], SQUARE)
-                factor = ring.tile([P, J], F32, name="factor")
-                nc.gpsimd.tensor_scalar(factor[:], u[:], cub_t[:, g, t : t + 1], -1.0, MULT, ADD)
-                sums[t], factors[t] = e, factor
+                factors[t] = stage("factor", t)
+                nc.gpsimd.tensor_scalar(factors[t][:], u[:], cub_t[:, g, t : t + 1], -1.0, MULT, ADD)
+                sums[t] = e
 
             def multiply(t):
-                nc.vector.scalar_tensor_tensor(h[:, t, :], sums[t][:], -1.0, factors[t][:], MULT, MULT)
+                nc.vector.scalar_tensor_tensor(out[:, t, :], sums[t][:], -1.0, factors[t][:], MULT, MULT)
 
             square(0)
             for t in range(1, PACK):
                 square(t)
                 multiply(t - 1)
             multiply(PACK - 1)
+
+        def store_h(g, cols, tile):
+            nc.sync.dma_start(out=out_1[g * PASS : (g + 1) * PASS, cols].rearrange("(p t) j -> p t j", t=PACK), in_=tile)
+
+        def interleave(copy, out, in_):
+            copy(
+                out=out.rearrange("p (c i t) -> p c t i", i=NEIGHBOURS, t=PACK),
+                in_=in_.rearrange("p t (c i) -> p c t i", i=NEIGHBOURS),
+            )
+
+        def quantise_h(jh, groups, tag=None):
+            rounded = keep("h_bf%d%d" % (jh, groups[0]), [P, len(groups) * J * PACK], BF16, tag)
+            for n, g in enumerate(groups):
+                for x in range(0, J, PIECE):
+                    x0 = (n * J + x) * PACK
+                    interleave(nc.scalar.copy, rounded[:, x0 : x0 + PIECE * PACK], h[g, jh][:, :, x : x + PIECE])
+            cols = slice(groups[0] * J, (groups[-1] + 1) * J)
+            nc.vector.quantize_mx(out=h_w[jh][:, cols].bitcast(FP8X4), scales=h_s[jh][:, cols], in_=rounded[:])
+
+        def store_planes(jh):
             nc.sync.dma_start(
-                out=out_1[g * PASS : (g + 1) * PASS, cols].rearrange("(p t) j -> p t j", t=PACK), in_=h[:]
+                out=out_2.rearrange("g p m t -> p g (m t)").bitcast(I32)[:, :, half(jh)],
+                in_=h_w[jh][:].bitcast(I32).rearrange("p (g m) -> p g m", g=GROUPS),
             )
-
-        def quantise_h(g, jh):
-            rounded = pair.tile([P, J * PACK], BF16, name="h_bf", align_bytes=64)
-            pairs = J // 2
-            for c0 in range(0, pairs, pairs // 2):
-                nc.scalar.copy(
-                    out=rounded[:].rearrange("p (c i t) -> p c t i", i=2, t=PACK)[:, c0 : c0 + pairs // 2],
-                    in_=h_t[g, jh][:].rearrange("p t (c i) -> p c t i", i=2)[:, c0 : c0 + pairs // 2],
+            for r in range(SCALE_ROWS):
+                nc.sync.dma_start(
+                    out=out_3[:, r:ROWS:SCALE_ROWS, half(jh)].rearrange("g q m -> q g m").bitcast(I32),
+                    in_=h_s[jh][r:P:32, :].bitcast(I32).rearrange("q (g m) -> q g m", g=GROUPS),
                 )
-            nc.vector.quantize_mx(
-                out=h_w[g][:, jh * J : (jh + 1) * J].bitcast(FP8X4),
-                scales=h_s[:, g * S + jh * J : g * S + (jh + 1) * J],
-                in_=rounded[:],
-            )
-            nc.sync.dma_start(
-                out=out_2[g].rearrange("p m t -> p (m t)").bitcast(I32)[:, jh * J : (jh + 1) * J],
-                in_=h_w[g][:, jh * J : (jh + 1) * J].bitcast(I32),
-            )
 
-        w3_w = [keep("w3_w%d" % g, [P, N], U32) for g in range(GROUPS)]
-        w3_s = [keep("w3_s%d" % g, [P, N], U8) for g in range(GROUPS)]
+        w3_w = keep("w3_w", [P, GROUPS * N], U32)
+        w3_s = keep("w3_s", [P, GROUPS * N], U8)
 
-        def quantise_w3(g, copies):
-            rounded = keep("w3_bf%d" % g, [P, N * PACK], BF16)
-            for n0, copy in zip(range(0, N, W3_PIECE), copies):
-                n1 = n0 + W3_PIECE
-                copy(
-                    out=rounded[:, n0 * PACK : n1 * PACK].rearrange("p (c i t) -> p c t i", i=2, t=PACK),
-                    in_=w3_raw[g][:, :, n0:n1].rearrange("p t (c i) -> p c t i", i=2),
-                )
-            for n0, n1 in ((0, W3_PIECE), (W3_PIECE, N)):
-                nc.vector.quantize_mx(
-                    out=w3_w[g][:, n0:n1].bitcast(FP8X4), scales=w3_s[g][:, n0:n1], in_=rounded[:, n0 * PACK : n1 * PACK]
-                )
+        def quantise_w3(pieces, copy, tag):
+            rounded = keep("w3_bf%d" % pieces.start, [P, len(pieces) * PIECE * PACK], BF16, tag)
+            for x, piece in enumerate(pieces):
+                g, n0 = divmod(piece * PIECE, N)
+                interleave(copy, rounded[:, x * PIECE * PACK : (x + 1) * PIECE * PACK], w3_raw[g][:, :, n0 : n0 + PIECE])
+            cols = slice(pieces.start * PIECE, pieces.stop * PIECE)
+            nc.vector.quantize_mx(out=w3_w[:, cols].bitcast(FP8X4), scales=w3_s[:, cols], in_=rounded[:])
 
         out_v = out_0.rearrange("(a p) j -> p a j", p=P)
 
-        def w8_sum(a, jh):
-            rows = slice(a * P, (a + 1) * P)
-            direct = bank(W8_SUM_BANKS[jh][a])
-            nc.tensor.matmul_mx(
-                out=direct[:], lhsT=w8_w[:, rows].bitcast(FP8X4), lhsT_scale=w8_s[:, rows],
-                rhs=v_w[jh][:].bitcast(FP8X4), rhs_scale=v_s[:, jh * J : (jh + 1) * J], start=True, stop=True,
-            )
-            return direct
-
-        parked = keep("parked", [P, NTILES, J], F32, "tab_then_parked")
-
-        def park(jh):
-            for a in GPSIMD_ADDS[jh]:
-                nc.scalar.copy(out=parked[:, a, :], in_=w8_sum(a, jh)[:])
-
         def read_out(jh):
-            cols = slice(jh * J, (jh + 1) * J)
             driven = {}
 
             def drive_tile(a):
-                rows = slice(a * P, (a + 1) * P)
-                shaped = bank(W3_SUM_BANKS[jh][a])
+                shaped = bank((len(EARLY_BANKS) + jh * NTILES + a) % W3_BANKS)
                 for g in range(GROUPS):
+                    tile_cols = slice(g * N + a * P, g * N + (a + 1) * P)
+                    group_cols = slice(g * J, (g + 1) * J)
                     nc.tensor.matmul_mx(
-                        out=shaped[:], lhsT=w3_w[g][:, rows].bitcast(FP8X4), lhsT_scale=w3_s[g][:, rows],
-                        rhs=h_w[g][:, cols].bitcast(FP8X4), rhs_scale=h_s[:, g * S + jh * J : g * S + (jh + 1) * J],
+                        out=shaped[:], lhsT=w3_w[:, tile_cols].bitcast(FP8X4), lhsT_scale=w3_s[:, tile_cols],
+                        rhs=h_w[jh][:, group_cols].bitcast(FP8X4), rhs_scale=h_s[jh][:, group_cols],
                         start=(g == 0), stop=(g == GROUPS - 1),
                     )
-                driven[a] = ring.tile([P, J], F32, name="driven")
-                nc.vector.tensor_tensor(driven[a][:], shaped[:], y_tile(a, jh), MULT)
+                driven[a] = driven_ring.tile([P, J], F32, name="driven")
+                nc.vector.tensor_tensor(driven[a][:], shaped[:], y_rows[:, a, half(jh)], MULT)
 
             def add_w8_sum(a):
+                y = y_rows[:, a, half(jh)]
                 if a in GPSIMD_ADDS[jh]:
-                    nc.gpsimd.tensor_tensor(y_tile(a, jh), parked[:, a, :], driven[a][:], ADD)
+                    nc.gpsimd.tensor_tensor(y, parked[a, jh][:], driven[a][:], ADD)
                 else:
-                    nc.vector.tensor_tensor(y_tile(a, jh), w8_sum(a, jh)[:], driven[a][:], ADD)
-                nc.sync.dma_start(out=out_v[:, a, cols], in_=y_tile(a, jh))
+                    nc.vector.tensor_tensor(y, w8_sum(a, jh, ADD_BANKS[a, jh])[:], driven[a][:], ADD)
+                nc.sync.dma_start(out=out_v[:, a, half(jh)], in_=y)
 
             drive_tile(0)
             for a in range(1, NTILES):
@@ -255,26 +250,43 @@ def tile_list_cavity_pulse_shaping_kernel(
                 add_w8_sum(a - 1)
             add_w8_sum(NTILES - 1)
 
+        unread = keep("unread", [P, 1], F32)
+
+        def round_beside_gpsimd(out, in_):
+            nc.vector.tensor_scalar(out, in_, 1.0, None, MULT, MAX, accum_out=unread[:])
+
         quantise_w1(0, nc.scalar.copy)
-        gather_words(0)
-        quantise_w1(1, nc.vector.tensor_copy)
-        shape(0, 0)
-        shape(1, 0)
-        gather_words(1)
-        quantise_h(0, 0)
-        quantise_h(1, 0)
-        quantise_w3(0, [nc.vector.tensor_copy] * 3)
-        quantise_w3(1, [nc.vector.tensor_copy, nc.scalar.copy, nc.scalar.copy])
-        shape(0, 1)
-        shape(1, 1)
-        quantise_h(0, 1)
-        park(0)
-        quantise_h(1, 1)
+        w3_raw = [keep("w3_raw0", [P, PACK, N], F32, "w4_then_w3"), keep("w3_raw1", [P, PACK, N], F32, "w1_then_w3")]
+        for g in range(GROUPS):
+            nc.sync.dma_start(out=w3_raw[g][:], in_=w3[g * PASS : (g + 1) * PASS, :].rearrange("(p i) n -> p i n", i=PACK))
+        w8_w = keep("w8_w", [P, N], U32, "w1_bf0")
+        nc.sync.dma_start(out=w8_w[:].bitcast(I32), in_=w8_words[0].rearrange("p n t -> p (n t)").bitcast(I32))
+        for jh in range(HALVES):
+            nc.vector.tensor_copy(v_w[jh][:], tab_w[:].indirect(offsets[:, jh * (J // 16) : (jh + 1) * (J // 16)]))
+        y_rows = keep("y_rows", [P, NTILES, S], F32, "rows_then_drive")
+        nc.sync.dma_start(out=y_rows[:], in_=drive.rearrange("(a p) j -> p a j", p=P))
+        quantise_w1(1, round_beside_gpsimd)
+
+        h_first = keep("h0", [P, PACK, S], F32, "w4_s_then_w1_then_h")
+        for jh in range(HALVES):
+            shape(0, jh, h_first[:, :, half(jh)], in_ring)
+        store_h(0, slice(0, S), h_first[:])
+        h_second = [keep("h1%d" % jh, [P, PACK, J], F32)[:] for jh in range(HALVES)]
+        shape(1, 0, h_second[0], in_own_buffer)
+        store_h(1, half(0), h_second[0])
+
+        quantise_h(0, [0])
+        quantise_w3(range(W3_ON_VECTOR, W3_PIECES), nc.scalar.copy, "u1")
+        quantise_w3(range(0, W3_ON_VECTOR), nc.vector.tensor_copy, "u3")
+        quantise_h(0, [1])
+        store_planes(0)
+        park(0, GPSIMD_ADDS[0][:EARLY_COPIES], EARLY_BANKS)
+
+        shape(1, 1, h_second[1], in_ring)
+        store_h(1, half(1), h_second[1])
+        quantise_h(1, [0, 1], "factor3")
+        park(0, GPSIMD_ADDS[0][EARLY_COPIES:], LATE_BANKS)
         read_out(0)
-        for r in range(SCALE_ROWS):
-            nc.sync.dma_start(
-                out=out_3[:, r : QUADRANTS * SCALE_ROWS : SCALE_ROWS, :].rearrange("g q m -> q g m").bitcast(I32),
-                in_=h_s[r:P:32, :].bitcast(I32).rearrange("q (g m) -> q g m", g=GROUPS),
-            )
-        park(1)
+        store_planes(1)
+        park(1, GPSIMD_ADDS[1], LATE_BANKS)
         read_out(1)

@@ -37,12 +37,12 @@ PIECE = 256
 W3_ON_VECTOR = 4
 W3_PIECES = GROUPS * N // PIECE
 
-GPSIMD_ADDS = (range(0, 4), range(0, NTILES, 2))
+GPSIMD_ADDS = ((0, 1, 2, 5), (0, 2, 4))
 EARLY_COPIES = 2
 
 W3_BANKS = 4
 EARLY_BANKS, LATE_BANKS = (0, 1), (4, 5)
-ADD_BANKS = {(4, 0): 6, (5, 0): 7, (1, 1): 6, (3, 1): 7, (5, 1): 5}
+ADD_BANKS = {(3, 0): 6, (4, 0): 7, (1, 1): 6, (3, 1): 7, (5, 1): 5}
 RING = 6
 
 
@@ -128,12 +128,15 @@ def tile_list_cavity_pulse_shaping_kernel(
         w1_w = [keep("w1_w%d" % g, [P, PASS], U32) for g in range(GROUPS)]
         w1_s = [keep("w1_s%d" % g, [P, PASS], U8) for g in range(GROUPS)]
 
-        def quantise_w1(g, copy):
+        def round_w1(g, copy):
             rounded = keep("w1_bf%d" % g, [P, PASS * PACK], BF16)
             copy(
                 out=rounded[:].rearrange("p (t m i) -> p m t i", t=PACK, i=PACK),
                 in_=w1_raw[g][:].rearrange("p i (m t) -> p m t i", t=PACK),
             )
+            return rounded
+
+        def quantise_w1(g, rounded):
             nc.vector.quantize_mx(out=w1_w[g][:].bitcast(FP8X4), scales=w1_s[g][:], in_=rounded[:])
 
         h_w = [keep("h_w%d" % jh, [P, GROUPS * J], U32) for jh in range(HALVES)]
@@ -146,7 +149,7 @@ def tile_list_cavity_pulse_shaping_kernel(
         def in_own_buffer(name, t):
             return keep("%s%d" % (name, t), [P, J], F32)
 
-        def shape(g, jh, out, stage):
+        def shape(g, jh, out, stage, after_first_product=None):
             h[g, jh] = out
             sums, factors = {}, {}
 
@@ -158,7 +161,7 @@ def tile_list_cavity_pulse_shaping_kernel(
                     (w1_w[g][:, m0 : m0 + P].bitcast(FP8X4), w1_s[g][:, m0 : m0 + P]),
                     (w4_w[:, 2 * c0 : 2 * (c0 + P)].bitcast(FP4X4), w4_s[:, c0 : c0 + P]),
                 ]
-                for n, (words, scales) in enumerate(weights if g or jh else reversed(weights)):
+                for n, (words, scales) in enumerate(weights if jh else reversed(weights)):
                     nc.tensor.matmul_mx(
                         out=e[:], lhsT=words, lhsT_scale=scales,
                         rhs=v_w[jh][:].bitcast(FP8X4), rhs_scale=v_s[:, half(jh)], start=(n == 0), stop=(n == 1),
@@ -176,10 +179,13 @@ def tile_list_cavity_pulse_shaping_kernel(
             for t in range(1, PACK):
                 square(t)
                 multiply(t - 1)
+                if after_first_product and t == 1:
+                    after_first_product()
             multiply(PACK - 1)
 
-        def store_h(g, cols, tile):
-            nc.sync.dma_start(out=out_1[g * PASS : (g + 1) * PASS, cols].rearrange("(p t) j -> p t j", t=PACK), in_=tile)
+        def store_h(g, tile, sums):
+            rows_of_h = out_1[g * PASS : (g + 1) * PASS, :].rearrange("(p t) j -> p t j", t=PACK)
+            nc.sync.dma_start(out=rows_of_h[:, sums, :], in_=tile[:, sums, :])
 
         def interleave(copy, out, in_):
             copy(
@@ -255,7 +261,7 @@ def tile_list_cavity_pulse_shaping_kernel(
         def round_beside_gpsimd(out, in_):
             nc.vector.tensor_scalar(out, in_, 1.0, None, MULT, MAX, accum_out=unread[:])
 
-        quantise_w1(0, nc.scalar.copy)
+        quantise_w1(0, round_w1(0, nc.scalar.copy))
         w3_raw = [keep("w3_raw0", [P, PACK, N], F32, "w4_then_w3"), keep("w3_raw1", [P, PACK, N], F32, "w1_then_w3")]
         for g in range(GROUPS):
             nc.sync.dma_start(out=w3_raw[g][:], in_=w3[g * PASS : (g + 1) * PASS, :].rearrange("(p i) n -> p i n", i=PACK))
@@ -265,15 +271,14 @@ def tile_list_cavity_pulse_shaping_kernel(
             nc.vector.tensor_copy(v_w[jh][:], tab_w[:].indirect(offsets[:, jh * (J // 16) : (jh + 1) * (J // 16)]))
         y_rows = keep("y_rows", [P, NTILES, S], F32, "rows_then_drive")
         nc.sync.dma_start(out=y_rows[:], in_=drive.rearrange("(a p) j -> p a j", p=P))
-        quantise_w1(1, round_beside_gpsimd)
+        w1_second = round_w1(1, round_beside_gpsimd)
 
         h_first = keep("h0", [P, PACK, S], F32, "w4_s_then_w1_then_h")
-        for jh in range(HALVES):
-            shape(0, jh, h_first[:, :, half(jh)], in_ring)
-        store_h(0, slice(0, S), h_first[:])
-        h_second = [keep("h1%d" % jh, [P, PACK, J], F32)[:] for jh in range(HALVES)]
-        shape(1, 0, h_second[0], in_own_buffer)
-        store_h(1, half(0), h_second[0])
+        shape(0, 0, h_first[:, :, half(0)], in_ring, lambda: quantise_w1(1, w1_second))
+        shape(0, 1, h_first[:, :, half(1)], in_ring)
+        store_h(0, h_first, slice(0, PACK))
+        h_second = keep("h1", [P, PACK, S], F32)
+        shape(1, 0, h_second[:, :, half(0)], in_own_buffer)
 
         quantise_h(0, [0])
         quantise_w3(range(W3_ON_VECTOR, W3_PIECES), nc.scalar.copy, "u1")
@@ -282,8 +287,9 @@ def tile_list_cavity_pulse_shaping_kernel(
         store_planes(0)
         park(0, GPSIMD_ADDS[0][:EARLY_COPIES], EARLY_BANKS)
 
-        shape(1, 1, h_second[1], in_ring)
-        store_h(1, half(1), h_second[1])
+        shape(1, 1, h_second[:, :, half(1)], in_ring)
+        for t in range(0, PACK, 2):
+            store_h(1, h_second, slice(t, t + 2))
         quantise_h(1, [0, 1], "factor3")
         park(0, GPSIMD_ADDS[0][EARLY_COPIES:], LATE_BANKS)
         read_out(0)

@@ -16,7 +16,10 @@ FP4X4 = mybir.dt.float4_e2m1fn_x4
 MULT = mybir.AluOpType.mult
 ADD = mybir.AluOpType.add
 MAX = mybir.AluOpType.max
+SUB = mybir.AluOpType.subtract
+IS_GE = mybir.AluOpType.is_ge
 SQUARE = mybir.ActivationFunctionType.Square
+POW = mybir.AluOpType.pow
 
 P = 128
 PACK = 4
@@ -34,15 +37,9 @@ LAST_QUADRANT = P - 32
 NEIGHBOURS = 4
 
 PIECE = 256
-W3_ON_VECTOR = 4
 W3_PIECES = GROUPS * N // PIECE
-
-GPSIMD_ADDS = ((0, 1, 2, 5), (0, 2, 4))
-EARLY_COPIES = 2
-
-W3_BANKS = 4
-EARLY_BANKS, LATE_BANKS = (0, 1), (4, 5)
-ADD_BANKS = {(3, 0): 6, (4, 0): 7, (1, 1): 6, (3, 1): 7, (5, 1): 5}
+BY_GPSIMD = (0, 2, 4, 5, 6, 8, 10)
+TURNS_ON_VECTOR = 2
 RING = 6
 
 
@@ -53,7 +50,6 @@ def tile_list_cavity_pulse_shaping_kernel(
     with ExitStack() as ctx:
         held = ctx.enter_context(tc.tile_pool(name="held", bufs=1))
         ring = ctx.enter_context(tc.tile_pool(name="ring", bufs=RING))
-        driven_ring = ctx.enter_context(tc.tile_pool(name="driven_ring", bufs=RING))
         psum = ctx.enter_context(tc.psum_pool(name="psum", bufs=1))
 
         def bank(b):
@@ -67,28 +63,30 @@ def tile_list_cavity_pulse_shaping_kernel(
 
         offsets = held.tile([P, S // 16], U16, name="offsets")
         tab_s_rows = keep("tab_s_rows", [P, T], U8)
-        w4_s_rows = keep("w4_s_rows", [P, H], U8, "w4_s_then_w1_then_h")
-        rows = keep("rows", [P, S + H + N], U8, "rows_then_drive")
+        w4_s_rows = keep("w4_s_rows", [P, H], U8)
+        rows = keep("rows", [P, S + H + N], U8, "rows_then_w3")
         planes = keep("planes", [P, S + H + N], U8)
         v_s, w4_s, w8_s = planes[:, 0:S], planes[:, S : S + H], planes[:, S + H : S + H + N]
-        tab_w = keep("tab_w", [P, T], U32)
-        w4_raw = keep("w4_raw", [P, 2 * H], U8, "w4_then_w3")
-        cub_t = keep("cub_t", [P, GROUPS, PACK], F32)
+        tab_w = keep("tab_w", [P, T], U32, "table_then_w3")
+        w4_raw = keep("w4_raw", [P, 2 * H], U8, "w4_then_w1")
+        cub_t = keep("cub_t", [P, GROUPS * PACK], F32)
 
         nc.vector.memset(tab_s_rows[0:ROW0, :].bitcast(I32), 0)
         nc.vector.memset(w4_s_rows[0:ROW0, :].bitcast(I32), 0)
         nc.vector.memset(planes[:].bitcast(I32), 0)
-        nc.gpsimd.dma_start(out=cub_t[:], in_=cub.rearrange("(g p t) -> p g t", g=GROUPS, t=PACK))
 
         w1_rows = w1.rearrange("(p i) r -> p i r", i=PACK)
         nc.sync.dma_start(out=tab_s_rows[ROW0:P, :].bitcast(I32), in_=tab_scales[0].bitcast(I32))
         nc.sync.dma_start(offsets[:], offs)
         nc.sync.dma_start(out=w4_s_rows[ROW0:P, :].bitcast(I32), in_=w4_scales[0].bitcast(I32))
         nc.sync.dma_start(out=rows[ROW0:P, S + H : S + H + N].bitcast(I32), in_=w8_scales[0].bitcast(I32))
-        w1_raw = [keep("w1_raw0", [P, PACK, PASS], F32, "w1_then_w3")]
-        nc.sync.dma_start(out=w1_raw[0][:], in_=w1_rows[:, :, 0:PASS])
+        nc.sync.dma_start(
+            out=cub_t[:].rearrange("p (g t) -> p g t", t=PACK), in_=cub.rearrange("(g p t) -> p g t", g=GROUPS, t=PACK)
+        )
         nc.sync.dma_start(out=w4_raw[:].bitcast(I32), in_=w4_words[0].bitcast(I32))
         nc.sync.dma_start(out=tab_w[:].bitcast(I32), in_=tab_words[0].rearrange("p n t -> p (n t)").bitcast(I32))
+        w1_raw = [keep("w1_raw0", [P, PACK, PASS], F32)]
+        nc.sync.dma_start(out=w1_raw[0][:], in_=w1_rows[:, :, 0:PASS])
 
         v_s_rows = keep("v_s_rows", [P, S], U8)
         nc.vector.tensor_copy(v_s_rows[:], tab_s_rows[:].indirect(offsets[:]))
@@ -98,16 +96,144 @@ def tile_list_cavity_pulse_shaping_kernel(
             in_=w4_s_rows[:].rearrange("p (g c m t) -> p g c t m", g=GROUPS, t=PACK, m=16),
         )
         for r in range(SCALE_ROWS):
-            nc.sync.dma_start(out=planes[r:P:32, :].bitcast(I32), in_=rows[ROW0 + r : P : SCALE_ROWS, :].bitcast(I32))
-        w1_raw.append(keep("w1_raw1", [P, PACK, PASS], F32, "w4_s_then_w1_then_h"))
-        nc.sync.dma_start(out=w1_raw[1][:], in_=w1_rows[:, :, PASS : 2 * PASS])
+            nc.scalar.dma_start(out=planes[r:P:32, :].bitcast(I32), in_=rows[ROW0 + r : P : SCALE_ROWS, :].bitcast(I32))
 
         v_w = [keep("v_w%d" % jh, [P, J], U32) for jh in range(HALVES)]
         w4_w = keep("w4_w", [P, 2 * H], U8)
+
+        def gather_words(jh):
+            nc.vector.tensor_copy(v_w[jh][:], tab_w[:].indirect(offsets[:, jh * (J // 16) : (jh + 1) * (J // 16)]))
+
         nc.vector.tensor_copy(
             out=w4_w[:].bitcast(U16).rearrange("p (g t c m) -> p g c t m", g=GROUPS, t=PACK, m=8),
             in_=w4_raw[:].bitcast(U16).rearrange("p (g c m t) -> p g c t m", g=GROUPS, t=PACK, m=8),
         )
+        w1_raw.append(keep("w1_raw1", [P, PACK, PASS], F32, "w4_then_w1"))
+        nc.sync.dma_start(out=w1_raw[1][:], in_=w1_rows[:, :, PASS : 2 * PASS])
+        for jh in range(HALVES):
+            gather_words(jh)
+
+        twice, size, halves, root, sign, flip = [
+            keep(n, [P, GROUPS * PACK], F32) for n in ("twice", "size", "halves", "root", "sign", "flip")
+        ]
+        nc.gpsimd.memset(halves[:], 0.5)
+        nc.gpsimd.tensor_scalar(twice[:], cub_t[:], 0.0, 2.0, IS_GE, MULT)
+        nc.gpsimd.tensor_scalar(sign[:], twice[:], 1.0, -1.0, MULT, ADD)
+        nc.gpsimd.tensor_scalar(flip[:], twice[:], -1.0, 1.0, MULT, ADD)
+        nc.gpsimd.tensor_tensor(size[:], cub_t[:], sign[:], MULT)
+        nc.gpsimd.tensor_tensor(root[:], size[:], halves[:], POW)
+
+        w1_w = [keep("w1_w%d" % g, [P, PASS], U32) for g in range(GROUPS)]
+        w1_s = [keep("w1_s%d" % g, [P, PASS], U8) for g in range(GROUPS)]
+
+        def round_w1(g, pair, rounded, copy):
+            copy(
+                out=rounded.rearrange("p (u m i) -> p m i u", u=2, i=PACK),
+                in_=w1_raw[g][:].rearrange("p i (m x u) -> p x m i u", x=2, u=2)[:, pair],
+            )
+
+        def quantise_w1(g, cols, rounded):
+            nc.vector.quantize_mx(out=w1_w[g][:, cols].bitcast(FP8X4), scales=w1_s[g][:, cols], in_=rounded)
+
+        first = [keep("w1_bf0%d" % pair, [P, 2 * PASS], BF16, "w1_bf_then_drive" if pair else "table_then_w3") for pair in range(2)]
+        round_w1(0, 0, first[0][:], nc.vector.tensor_copy)
+        round_w1(0, 1, first[1][:], nc.scalar.copy)
+        for pair in range(2):
+            quantise_w1(0, slice(pair * 2 * P, (pair + 1) * 2 * P), first[pair][:])
+
+        w3_raw = [keep("w3_raw0", [P, PACK, N], F32, "rows_then_w3"), keep("w3_raw1", [P, PACK, N], F32, "table_then_w3")]
+        for g in range(GROUPS):
+            nc.sync.dma_start(out=w3_raw[g][:], in_=w3[g * PASS : (g + 1) * PASS, :].rearrange("(p i) n -> p i n", i=PACK))
+        y_rows = keep("y_rows", [P, NTILES, S], F32, "w1_bf_then_drive")
+        nc.sync.dma_start(out=y_rows[:], in_=drive.rearrange("(a p) j -> p a j", p=P))
+
+        h = [keep("h%d" % g, [P, PACK, S], F32) for g in range(GROUPS)]
+        h_w = [keep("h_w%d" % g, [P, S], U32) for g in range(GROUPS)]
+        h_s = keep("h_s", [P, GROUPS, S], U8)
+
+        def shape(g, t, jh):
+            e = bank(HALVES * t + jh)
+            m0 = t * P
+            c0 = g * PASS + m0
+            weights = [
+                (w4_w[:, 2 * c0 : 2 * (c0 + P)].bitcast(FP4X4), w4_s[:, c0 : c0 + P]),
+                (w1_w[g][:, m0 : m0 + P].bitcast(FP8X4), w1_s[g][:, m0 : m0 + P]),
+            ]
+            for n, (words, scales) in enumerate(weights):
+                nc.tensor.matmul_mx(
+                    out=e[:], lhsT=words, lhsT_scale=scales,
+                    rhs=v_w[jh][:].bitcast(FP8X4), rhs_scale=v_s[:, half(jh)], start=(n == 0), stop=(n == 1),
+                )
+            c = slice(g * PACK + t, g * PACK + t + 1)
+            tag = {(GROUPS - 1, PACK - 1, HALVES - 1): "u_then_w3"}.get((g, t, jh))
+            u = keep("u_own", [P, J], F32, tag) if tag else ring.tile([P, J], F32, name="u")
+            nc.scalar.activation(u[:], e[:], SQUARE, scale=root[:, c])
+            nc.vector.scalar_tensor_tensor(h[g][:, t, half(jh)], u[:], sign[:, c], e[:], SUB, MULT)
+
+        def turn(g, t, engine):
+            c = slice(g * PACK + t, g * PACK + t + 1)
+            engine.tensor_scalar(h[g][:, t, :], h[g][:, t, :], flip[:, c], 0.0, MULT, ADD)
+
+        def store_h(g):
+            rows_of_h = out_1[g * PASS : (g + 1) * PASS, :].rearrange("(p t) j -> p t j", t=PACK)
+            nc.sync.dma_start(out=rows_of_h, in_=h[g][:])
+
+        sums = [(g, t, jh) for g in range(GROUPS) for t in range(PACK) for jh in range(HALVES)]
+        second = keep("w1_bf1", [P, PACK * PASS], BF16)
+        for pair in range(2):
+            round_w1(1, pair, second[:, pair * 2 * PASS : (pair + 1) * 2 * PASS], nc.vector.tensor_copy)
+        w8_w = keep("w8_w", [P, N], U32, "w4_then_w1")
+        nc.sync.dma_start(out=w8_w[:].bitcast(I32), in_=w8_words[0].rearrange("p n t -> p (n t)").bitcast(I32))
+        shape(*sums[0])
+        quantise_w1(1, slice(0, PASS), second[:])
+        for g, t, jh in sums[1:]:
+            shape(g, t, jh)
+            if jh == HALVES - 1 and g * PACK + t < GROUPS * PACK - TURNS_ON_VECTOR:
+                turn(g, t, nc.gpsimd)
+                if t == PACK - 1:
+                    store_h(g)
+        for t in range(PACK - TURNS_ON_VECTOR, PACK):
+            turn(GROUPS - 1, t, nc.vector)
+        store_h(GROUPS - 1)
+
+        def interleave(copy, out, in_):
+            copy(
+                out=out.rearrange("p (c i t) -> p c t i", i=NEIGHBOURS, t=PACK),
+                in_=in_.rearrange("p t (c i) -> p c t i", i=NEIGHBOURS),
+            )
+
+        def round_h(g, cols, copy):
+            rounded = keep("h_bf%d%d" % (g, cols.start), [P, (cols.stop - cols.start) * PACK], BF16)
+            for x in range(cols.start, cols.stop, PIECE):
+                x0 = (x - cols.start) * PACK
+                interleave(copy if x >= J else nc.scalar.copy, rounded[:, x0 : x0 + PIECE * PACK], h[g][:, :, x : x + PIECE])
+            return rounded
+
+        def quantise_h(g, cols, rounded):
+            nc.vector.quantize_mx(out=h_w[g][:, cols].bitcast(FP8X4), scales=h_s[:, g, cols], in_=rounded[:])
+
+        def store_words(g):
+            nc.sync.dma_start(out=out_2[g].rearrange("p m t -> p (m t)").bitcast(I32), in_=h_w[g][:].bitcast(I32))
+
+        def store_scales():
+            for r in range(SCALE_ROWS):
+                nc.sync.dma_start(
+                    out=out_3[:, r:ROWS:SCALE_ROWS, :].rearrange("g q m -> q g m").bitcast(I32), in_=h_s[r:P:32].bitcast(I32)
+                )
+
+        w3_w = keep("w3_w", [P, GROUPS * N], U32)
+        w3_s = keep("w3_s", [P, GROUPS * N], U8)
+
+        def round_w3(pieces, copy, tag):
+            rounded = keep("w3_bf%d" % pieces.start, [P, len(pieces) * PIECE * PACK], BF16, tag)
+            for x, piece in enumerate(pieces):
+                n0, g = piece // GROUPS * PIECE, piece % GROUPS
+                interleave(copy, rounded[:, x * PIECE * PACK : (x + 1) * PIECE * PACK], w3_raw[g][:, :, n0 : n0 + PIECE])
+            return rounded
+
+        def quantise_w3(pieces, rounded):
+            cols = slice(pieces.start * PIECE, pieces.stop * PIECE)
+            nc.vector.quantize_mx(out=w3_w[:, cols].bitcast(FP8X4), scales=w3_s[:, cols], in_=rounded[:])
 
         def w8_sum(a, jh, b):
             tile_cols = slice(a * P, (a + 1) * P)
@@ -118,181 +244,65 @@ def tile_list_cavity_pulse_shaping_kernel(
             )
             return direct
 
+        w8_banks = {4: [], 6: []}
+
+        def next_w8_bank(b0):
+            w8_banks[b0].append(b0 + len(w8_banks[b0]) % 2)
+            return w8_banks[b0][-1]
+
+        steps = [(a, jh) for a in range(NTILES) for jh in range(HALVES)]
+        by_gpsimd = [steps[n] for n in BY_GPSIMD]
         parked = {}
 
-        def park(jh, tiles, banks):
-            for n, a in enumerate(tiles):
+        def park(some):
+            for a, jh in some:
                 parked[a, jh] = keep("parked%d%d" % (jh, a), [P, J], F32)
-                nc.scalar.copy(out=parked[a, jh][:], in_=w8_sum(a, jh, banks[n % len(banks)])[:])
-
-        w1_w = [keep("w1_w%d" % g, [P, PASS], U32) for g in range(GROUPS)]
-        w1_s = [keep("w1_s%d" % g, [P, PASS], U8) for g in range(GROUPS)]
-
-        def round_w1(g, copy):
-            rounded = keep("w1_bf%d" % g, [P, PASS * PACK], BF16)
-            copy(
-                out=rounded[:].rearrange("p (t m i) -> p m t i", t=PACK, i=PACK),
-                in_=w1_raw[g][:].rearrange("p i (m t) -> p m t i", t=PACK),
-            )
-            return rounded
-
-        def quantise_w1(g, rounded):
-            nc.vector.quantize_mx(out=w1_w[g][:].bitcast(FP8X4), scales=w1_s[g][:], in_=rounded[:])
-
-        h_w = [keep("h_w%d" % jh, [P, GROUPS * J], U32) for jh in range(HALVES)]
-        h_s = [keep("h_s%d" % jh, [P, GROUPS * J], U8) for jh in range(HALVES)]
-        h = {}
-
-        def in_ring(name, t):
-            return ring.tile([P, J], F32, name=name)
-
-        def in_own_buffer(name, t):
-            return keep("%s%d" % (name, t), [P, J], F32)
-
-        def shape(g, jh, out, stage, after_first_product=None):
-            h[g, jh] = out
-            sums, factors = {}, {}
-
-            def square(t):
-                e = bank(PACK * jh + t)
-                m0 = t * P
-                c0 = g * PASS + m0
-                weights = [
-                    (w1_w[g][:, m0 : m0 + P].bitcast(FP8X4), w1_s[g][:, m0 : m0 + P]),
-                    (w4_w[:, 2 * c0 : 2 * (c0 + P)].bitcast(FP4X4), w4_s[:, c0 : c0 + P]),
-                ]
-                for n, (words, scales) in enumerate(weights if jh else reversed(weights)):
-                    nc.tensor.matmul_mx(
-                        out=e[:], lhsT=words, lhsT_scale=scales,
-                        rhs=v_w[jh][:].bitcast(FP8X4), rhs_scale=v_s[:, half(jh)], start=(n == 0), stop=(n == 1),
-                    )
-                u = stage("u", t)
-                nc.scalar.activation(u[:], e[:], SQUARE)
-                factors[t] = stage("factor", t)
-                nc.gpsimd.tensor_scalar(factors[t][:], u[:], cub_t[:, g, t : t + 1], -1.0, MULT, ADD)
-                sums[t] = e
-
-            def multiply(t):
-                nc.vector.scalar_tensor_tensor(out[:, t, :], sums[t][:], -1.0, factors[t][:], MULT, MULT)
-
-            square(0)
-            for t in range(1, PACK):
-                square(t)
-                multiply(t - 1)
-                if after_first_product and t == 1:
-                    after_first_product()
-            multiply(PACK - 1)
-
-        def store_h(g, tile, sums):
-            rows_of_h = out_1[g * PASS : (g + 1) * PASS, :].rearrange("(p t) j -> p t j", t=PACK)
-            nc.sync.dma_start(out=rows_of_h[:, sums, :], in_=tile[:, sums, :])
-
-        def interleave(copy, out, in_):
-            copy(
-                out=out.rearrange("p (c i t) -> p c t i", i=NEIGHBOURS, t=PACK),
-                in_=in_.rearrange("p t (c i) -> p c t i", i=NEIGHBOURS),
-            )
-
-        def quantise_h(jh, groups, tag=None):
-            rounded = keep("h_bf%d%d" % (jh, groups[0]), [P, len(groups) * J * PACK], BF16, tag)
-            for n, g in enumerate(groups):
-                for x in range(0, J, PIECE):
-                    x0 = (n * J + x) * PACK
-                    interleave(nc.scalar.copy, rounded[:, x0 : x0 + PIECE * PACK], h[g, jh][:, :, x : x + PIECE])
-            cols = slice(groups[0] * J, (groups[-1] + 1) * J)
-            nc.vector.quantize_mx(out=h_w[jh][:, cols].bitcast(FP8X4), scales=h_s[jh][:, cols], in_=rounded[:])
-
-        def store_planes(jh):
-            nc.sync.dma_start(
-                out=out_2.rearrange("g p m t -> p g (m t)").bitcast(I32)[:, :, half(jh)],
-                in_=h_w[jh][:].bitcast(I32).rearrange("p (g m) -> p g m", g=GROUPS),
-            )
-            for r in range(SCALE_ROWS):
-                nc.sync.dma_start(
-                    out=out_3[:, r:ROWS:SCALE_ROWS, half(jh)].rearrange("g q m -> q g m").bitcast(I32),
-                    in_=h_s[jh][r:P:32, :].bitcast(I32).rearrange("q (g m) -> q g m", g=GROUPS),
-                )
-
-        w3_w = keep("w3_w", [P, GROUPS * N], U32)
-        w3_s = keep("w3_s", [P, GROUPS * N], U8)
-
-        def quantise_w3(pieces, copy, tag):
-            rounded = keep("w3_bf%d" % pieces.start, [P, len(pieces) * PIECE * PACK], BF16, tag)
-            for x, piece in enumerate(pieces):
-                g, n0 = divmod(piece * PIECE, N)
-                interleave(copy, rounded[:, x * PIECE * PACK : (x + 1) * PIECE * PACK], w3_raw[g][:, :, n0 : n0 + PIECE])
-            cols = slice(pieces.start * PIECE, pieces.stop * PIECE)
-            nc.vector.quantize_mx(out=w3_w[:, cols].bitcast(FP8X4), scales=w3_s[:, cols], in_=rounded[:])
+                nc.scalar.copy(out=parked[a, jh][:], in_=w8_sum(a, jh, next_w8_bank(4))[:])
 
         out_v = out_0.rearrange("(a p) j -> p a j", p=P)
+        driven = {}
 
-        def read_out(jh):
-            driven = {}
+        def drive_tile(n):
+            a, jh = steps[n]
+            shaped = bank(n % 4)
+            for g in range(GROUPS):
+                c0 = (a * P // PIECE * GROUPS + g) * PIECE + a * P % PIECE
+                tile_cols = slice(c0, c0 + P)
+                nc.tensor.matmul_mx(
+                    out=shaped[:], lhsT=w3_w[:, tile_cols].bitcast(FP8X4), lhsT_scale=w3_s[:, tile_cols],
+                    rhs=h_w[g][:, half(jh)].bitcast(FP8X4), rhs_scale=h_s[:, g, half(jh)],
+                    start=(g == 0), stop=(g == GROUPS - 1),
+                )
+            driven[n] = ring.tile([P, J], F32, name="driven")
+            nc.vector.tensor_tensor(driven[n][:], shaped[:], y_rows[:, a, half(jh)], MULT)
 
-            def drive_tile(a):
-                shaped = bank((len(EARLY_BANKS) + jh * NTILES + a) % W3_BANKS)
-                for g in range(GROUPS):
-                    tile_cols = slice(g * N + a * P, g * N + (a + 1) * P)
-                    group_cols = slice(g * J, (g + 1) * J)
-                    nc.tensor.matmul_mx(
-                        out=shaped[:], lhsT=w3_w[:, tile_cols].bitcast(FP8X4), lhsT_scale=w3_s[:, tile_cols],
-                        rhs=h_w[jh][:, group_cols].bitcast(FP8X4), rhs_scale=h_s[jh][:, group_cols],
-                        start=(g == 0), stop=(g == GROUPS - 1),
-                    )
-                driven[a] = driven_ring.tile([P, J], F32, name="driven")
-                nc.vector.tensor_tensor(driven[a][:], shaped[:], y_rows[:, a, half(jh)], MULT)
-
-            def add_w8_sum(a):
-                y = y_rows[:, a, half(jh)]
-                if a in GPSIMD_ADDS[jh]:
-                    nc.gpsimd.tensor_tensor(y, parked[a, jh][:], driven[a][:], ADD)
-                else:
-                    nc.vector.tensor_tensor(y, w8_sum(a, jh, ADD_BANKS[a, jh])[:], driven[a][:], ADD)
+        def add_w8_sum(n):
+            a, jh = steps[n]
+            y = y_rows[:, a, half(jh)]
+            if (a, jh) in by_gpsimd:
+                nc.gpsimd.tensor_tensor(y, parked[a, jh][:], driven[n][:], ADD)
+            else:
+                nc.vector.tensor_tensor(y, w8_sum(a, jh, next_w8_bank(6))[:], driven[n][:], ADD)
+            if a == NTILES - 1:
                 nc.sync.dma_start(out=out_v[:, a, half(jh)], in_=y)
+            elif jh == HALVES - 1:
+                nc.sync.dma_start(out=out_v[:, a, :], in_=y_rows[:, a, :])
 
-            drive_tile(0)
-            for a in range(1, NTILES):
-                drive_tile(a)
-                add_w8_sum(a - 1)
-            add_w8_sum(NTILES - 1)
-
-        unread = keep("unread", [P, 1], F32)
-
-        def round_beside_gpsimd(out, in_):
-            nc.vector.tensor_scalar(out, in_, 1.0, None, MULT, MAX, accum_out=unread[:])
-
-        quantise_w1(0, round_w1(0, nc.scalar.copy))
-        w3_raw = [keep("w3_raw0", [P, PACK, N], F32, "w4_then_w3"), keep("w3_raw1", [P, PACK, N], F32, "w1_then_w3")]
+        h0 = round_h(0, slice(0, S), nc.scalar.copy)
+        w3_first = round_w3(range(0, 2), nc.vector.tensor_copy, "u_then_w3")
+        h1 = round_h(1, slice(0, S), nc.vector.tensor_copy)
+        quantise_h(0, slice(0, S), h0)
+        quantise_w3(range(0, 2), w3_first)
+        quantise_h(1, slice(0, S), h1)
         for g in range(GROUPS):
-            nc.sync.dma_start(out=w3_raw[g][:], in_=w3[g * PASS : (g + 1) * PASS, :].rearrange("(p i) n -> p i n", i=PACK))
-        w8_w = keep("w8_w", [P, N], U32, "w1_bf0")
-        nc.sync.dma_start(out=w8_w[:].bitcast(I32), in_=w8_words[0].rearrange("p n t -> p (n t)").bitcast(I32))
-        for jh in range(HALVES):
-            nc.vector.tensor_copy(v_w[jh][:], tab_w[:].indirect(offsets[:, jh * (J // 16) : (jh + 1) * (J // 16)]))
-        y_rows = keep("y_rows", [P, NTILES, S], F32, "rows_then_drive")
-        nc.sync.dma_start(out=y_rows[:], in_=drive.rearrange("(a p) j -> p a j", p=P))
-        w1_second = round_w1(1, round_beside_gpsimd)
-
-        h_first = keep("h0", [P, PACK, S], F32, "w4_s_then_w1_then_h")
-        shape(0, 0, h_first[:, :, half(0)], in_ring, lambda: quantise_w1(1, w1_second))
-        shape(0, 1, h_first[:, :, half(1)], in_ring)
-        store_h(0, h_first, slice(0, PACK))
-        h_second = keep("h1", [P, PACK, S], F32)
-        shape(1, 0, h_second[:, :, half(0)], in_own_buffer)
-
-        quantise_h(0, [0])
-        quantise_w3(range(W3_ON_VECTOR, W3_PIECES), nc.scalar.copy, "u1")
-        quantise_w3(range(0, W3_ON_VECTOR), nc.vector.tensor_copy, "u3")
-        quantise_h(0, [1])
-        store_planes(0)
-        park(0, GPSIMD_ADDS[0][:EARLY_COPIES], EARLY_BANKS)
-
-        shape(1, 1, h_second[:, :, half(1)], in_ring)
-        for t in range(0, PACK, 2):
-            store_h(1, h_second, slice(t, t + 2))
-        quantise_h(1, [0, 1], "factor3")
-        park(0, GPSIMD_ADDS[0][EARLY_COPIES:], LATE_BANKS)
-        read_out(0)
-        store_planes(1)
-        park(1, GPSIMD_ADDS[1], LATE_BANKS)
-        read_out(1)
+            store_words(g)
+        store_scales()
+        quantise_w3(range(2, 4), round_w3(range(2, 4), nc.scalar.copy, None))
+        park(by_gpsimd[:2])
+        quantise_w3(range(4, 6), round_w3(range(4, 6), nc.scalar.copy, None))
+        park(by_gpsimd[2:])
+        drive_tile(0)
+        for n in range(1, len(steps)):
+            drive_tile(n)
+            add_w8_sum(n - 1)
+        add_w8_sum(len(steps) - 1)

@@ -38,8 +38,8 @@ NEIGHBOURS = 4
 
 PIECE = 256
 W3_PIECES = GROUPS * N // PIECE
-BY_GPSIMD = (0, 2, 4, 5, 6, 8, 10)
-TURNS_ON_VECTOR = 2
+BY_GPSIMD = (2, 3, 4, 6, 8, 10)
+TURNS_ON_VECTOR = 3
 RING = 6
 
 
@@ -144,8 +144,8 @@ def tile_list_cavity_pulse_shaping_kernel(
         w3_raw = [keep("w3_raw0", [P, PACK, N], F32, "rows_then_w3"), keep("w3_raw1", [P, PACK, N], F32, "table_then_w3")]
         for g in range(GROUPS):
             nc.sync.dma_start(out=w3_raw[g][:], in_=w3[g * PASS : (g + 1) * PASS, :].rearrange("(p i) n -> p i n", i=PACK))
-        y_rows = keep("y_rows", [P, NTILES, S], F32, "w1_bf_then_drive")
-        nc.sync.dma_start(out=y_rows[:], in_=drive.rearrange("(a p) j -> p a j", p=P))
+        w8_w = keep("w8_w", [P, N], U32, "w1_bf_then_drive")
+        nc.sync.dma_start(out=w8_w[:].bitcast(I32), in_=w8_words[0].rearrange("p n t -> p (n t)").bitcast(I32))
 
         h = [keep("h%d" % g, [P, PACK, S], F32) for g in range(GROUPS)]
         h_w = [keep("h_w%d" % g, [P, S], U32) for g in range(GROUPS)]
@@ -182,8 +182,8 @@ def tile_list_cavity_pulse_shaping_kernel(
         second = keep("w1_bf1", [P, PACK * PASS], BF16)
         for pair in range(2):
             round_w1(1, pair, second[:, pair * 2 * PASS : (pair + 1) * 2 * PASS], nc.vector.tensor_copy)
-        w8_w = keep("w8_w", [P, N], U32, "w4_then_w1")
-        nc.sync.dma_start(out=w8_w[:].bitcast(I32), in_=w8_words[0].rearrange("p n t -> p (n t)").bitcast(I32))
+        y_rows = keep("y_rows", [P, NTILES, S], F32, "w4_then_w1")
+        nc.sync.dma_start(out=y_rows[:], in_=drive.rearrange("(a p) j -> p a j", p=P))
         shape(*sums[0])
         quantise_w1(1, slice(0, PASS), second[:])
         for g, t, jh in sums[1:]:
@@ -206,7 +206,7 @@ def tile_list_cavity_pulse_shaping_kernel(
             rounded = keep("h_bf%d%d" % (g, cols.start), [P, (cols.stop - cols.start) * PACK], BF16)
             for x in range(cols.start, cols.stop, PIECE):
                 x0 = (x - cols.start) * PACK
-                interleave(copy if x >= J else nc.scalar.copy, rounded[:, x0 : x0 + PIECE * PACK], h[g][:, :, x : x + PIECE])
+                interleave(copy, rounded[:, x0 : x0 + PIECE * PACK], h[g][:, :, x : x + PIECE])
             return rounded
 
         def quantise_h(g, cols, rounded):
@@ -288,19 +288,20 @@ def tile_list_cavity_pulse_shaping_kernel(
             elif jh == HALVES - 1:
                 nc.sync.dma_start(out=out_v[:, a, :], in_=y_rows[:, a, :])
 
-        h0 = round_h(0, slice(0, S), nc.scalar.copy)
+        h00, h01, h10 = [round_h(g, half(jh), nc.scalar.copy) for g, jh in ((0, 0), (0, 1), (1, 0))]
         w3_first = round_w3(range(0, 2), nc.vector.tensor_copy, "u_then_w3")
-        h1 = round_h(1, slice(0, S), nc.vector.tensor_copy)
-        quantise_h(0, slice(0, S), h0)
+        quantise_h(0, half(0), h00)
         quantise_w3(range(0, 2), w3_first)
-        quantise_h(1, slice(0, S), h1)
+        quantise_h(0, half(1), h01)
+        h11 = round_h(1, half(1), nc.vector.tensor_copy)
+        quantise_h(1, half(0), h10)
+        quantise_h(1, half(1), h11)
         for g in range(GROUPS):
             store_words(g)
         store_scales()
         quantise_w3(range(2, 4), round_w3(range(2, 4), nc.scalar.copy, None))
-        park(by_gpsimd[:2])
         quantise_w3(range(4, 6), round_w3(range(4, 6), nc.scalar.copy, None))
-        park(by_gpsimd[2:])
+        park(by_gpsimd)
         drive_tile(0)
         for n in range(1, len(steps)):
             drive_tile(n)

@@ -85,8 +85,6 @@ def tile_list_cavity_pulse_shaping_kernel(
         )
         nc.sync.dma_start(out=w4_raw[:].bitcast(I32), in_=w4_words[0].bitcast(I32))
         nc.sync.dma_start(out=tab_w[:].bitcast(I32), in_=tab_words[0].rearrange("p n t -> p (n t)").bitcast(I32))
-        w1_raw = [keep("w1_raw0", [P, PACK, PASS], F32)]
-        nc.sync.dma_start(out=w1_raw[0][:], in_=w1_rows[:, :, 0:PASS])
 
         v_s_rows = keep("v_s_rows", [P, S], U8)
         nc.vector.tensor_copy(v_s_rows[:], tab_s_rows[:].indirect(offsets[:]))
@@ -96,7 +94,9 @@ def tile_list_cavity_pulse_shaping_kernel(
             in_=w4_s_rows[:].rearrange("p (g c m t) -> p g c t m", g=GROUPS, t=PACK, m=16),
         )
         for r in range(SCALE_ROWS):
-            nc.scalar.dma_start(out=planes[r:P:32, :].bitcast(I32), in_=rows[ROW0 + r : P : SCALE_ROWS, :].bitcast(I32))
+            nc.sync.dma_start(out=planes[r:P:32, :].bitcast(I32), in_=rows[ROW0 + r : P : SCALE_ROWS, :].bitcast(I32))
+        w1_raw = [keep("w1_raw0", [P, PACK, PASS], F32, "w4_s_rows")]
+        nc.sync.dma_start(out=w1_raw[0][:], in_=w1_rows[:, :, 0:PASS])
 
         v_w = [keep("v_w%d" % jh, [P, J], U32) for jh in range(HALVES)]
         w4_w = keep("w4_w", [P, 2 * H], U8)
@@ -203,10 +203,8 @@ def tile_list_cavity_pulse_shaping_kernel(
             )
 
         def round_h(g, cols, copy):
-            rounded = keep("h_bf%d%d" % (g, cols.start), [P, (cols.stop - cols.start) * PACK], BF16)
-            for x in range(cols.start, cols.stop, PIECE):
-                x0 = (x - cols.start) * PACK
-                interleave(copy, rounded[:, x0 : x0 + PIECE * PACK], h[g][:, :, x : x + PIECE])
+            rounded = keep("h_bf%d%d" % (g, cols.start), [P, J * PACK], BF16)
+            interleave(copy, rounded[:], h[g][:, :, cols])
             return rounded
 
         def quantise_h(g, cols, rounded):

@@ -41,6 +41,7 @@ W3_PIECES = GROUPS * N // PIECE
 BY_GPSIMD = (2, 3, 4, 6, 8, 10)
 TURNS_ON_VECTOR = 3
 RING = 6
+W4_FIRST = 4
 
 
 def tile_list_cavity_pulse_shaping_kernel(
@@ -159,7 +160,8 @@ def tile_list_cavity_pulse_shaping_kernel(
                 (w4_w[:, 2 * c0 : 2 * (c0 + P)].bitcast(FP4X4), w4_s[:, c0 : c0 + P]),
                 (w1_w[g][:, m0 : m0 + P].bitcast(FP8X4), w1_s[g][:, m0 : m0 + P]),
             ]
-            for n, (words, scales) in enumerate(weights):
+            early = g > 0 or HALVES * t + jh < W4_FIRST
+            for n, (words, scales) in enumerate(weights if early else reversed(weights)):
                 nc.tensor.matmul_mx(
                     out=e[:], lhsT=words, lhsT_scale=scales,
                     rhs=v_w[jh][:].bitcast(FP8X4), rhs_scale=v_s[:, half(jh)], start=(n == 0), stop=(n == 1),
@@ -291,7 +293,9 @@ def tile_list_cavity_pulse_shaping_kernel(
         quantise_h(0, half(0), h00)
         quantise_w3(range(0, 2), w3_first)
         quantise_h(0, half(1), h01)
-        h11 = round_h(1, half(1), nc.vector.tensor_copy)
+        h11 = keep("h_bf_last", [P, J * PACK], BF16)
+        for x, copy in ((0, nc.scalar.copy), (PIECE, nc.vector.tensor_copy)):
+            interleave(copy, h11[:, x * PACK : (x + PIECE) * PACK], h[1][:, :, J + x : J + x + PIECE])
         quantise_h(1, half(0), h10)
         quantise_h(1, half(1), h11)
         for g in range(GROUPS):

@@ -15,11 +15,10 @@ FP8X4 = mybir.dt.float8_e4m3fn_x4
 FP4X4 = mybir.dt.float4_e2m1fn_x4
 MULT = mybir.AluOpType.mult
 ADD = mybir.AluOpType.add
-MAX = mybir.AluOpType.max
 SUB = mybir.AluOpType.subtract
+POW = mybir.AluOpType.pow
 IS_GE = mybir.AluOpType.is_ge
 SQUARE = mybir.ActivationFunctionType.Square
-POW = mybir.AluOpType.pow
 
 P = 128
 PACK = 4
@@ -32,16 +31,17 @@ QUADRANTS = 4
 SCALE_ROWS = 4
 ROWS = QUADRANTS * SCALE_ROWS
 ROW0 = P - ROWS
-
 LAST_QUADRANT = P - 32
 NEIGHBOURS = 4
+PAIR = 2 * P
 
-PIECE = 256
-W3_PIECES = GROUPS * N // PIECE
-BY_GPSIMD = (2, 3, 4, 6, 8, 10)
-TURNS_ON_VECTOR = 3
-RING = 6
 W4_FIRST = 4
+TURNS_ON_VECTOR = 3
+LAST_ON_SCALAR = 128
+BY_GPSIMD = (2, 3, 4, 6, 8, 10)
+LAST_ON_GPSIMD = 256
+W3_BANKS, PARK_BANK, ADD_BANK = 4, 4, 6
+RING = 6
 
 
 def tile_list_cavity_pulse_shaping_kernel(
@@ -63,23 +63,22 @@ def tile_list_cavity_pulse_shaping_kernel(
             return slice(jh * J, (jh + 1) * J)
 
         offsets = held.tile([P, S // 16], U16, name="offsets")
-        tab_s_rows = keep("tab_s_rows", [P, T], U8)
+        tab_s_rows = keep("tab_s_rows", [P, T], U8, "tab_s_then_w4")
         w4_s_rows = keep("w4_s_rows", [P, H], U8)
         rows = keep("rows", [P, S + H + N], U8, "rows_then_w3")
         planes = keep("planes", [P, S + H + N], U8)
         v_s, w4_s, w8_s = planes[:, 0:S], planes[:, S : S + H], planes[:, S + H : S + H + N]
-        tab_w = keep("tab_w", [P, T], U32, "table_then_w3")
-        w4_raw = keep("w4_raw", [P, 2 * H], U8, "w4_then_w1")
+        tab_w = keep("tab_w", [P, T], U32, "table_then_w1_then_w3")
+        w4_raw = keep("w4_raw", [P, 2 * H], U8, "w4_then_w1_then_drive")
         cub_t = keep("cub_t", [P, GROUPS * PACK], F32)
 
         nc.vector.memset(tab_s_rows[0:ROW0, :].bitcast(I32), 0)
         nc.vector.memset(w4_s_rows[0:ROW0, :].bitcast(I32), 0)
         nc.vector.memset(planes[:].bitcast(I32), 0)
 
-        w1_rows = w1.rearrange("(p i) r -> p i r", i=PACK)
+        nc.sync.dma_start(out=w4_s_rows[ROW0:P, :].bitcast(I32), in_=w4_scales[0].bitcast(I32))
         nc.sync.dma_start(out=tab_s_rows[ROW0:P, :].bitcast(I32), in_=tab_scales[0].bitcast(I32))
         nc.sync.dma_start(offsets[:], offs)
-        nc.sync.dma_start(out=w4_s_rows[ROW0:P, :].bitcast(I32), in_=w4_scales[0].bitcast(I32))
         nc.sync.dma_start(out=rows[ROW0:P, S + H : S + H + N].bitcast(I32), in_=w8_scales[0].bitcast(I32))
         nc.sync.dma_start(
             out=cub_t[:].rearrange("p (g t) -> p g t", t=PACK), in_=cub.rearrange("(g p t) -> p g t", g=GROUPS, t=PACK)
@@ -87,36 +86,28 @@ def tile_list_cavity_pulse_shaping_kernel(
         nc.sync.dma_start(out=w4_raw[:].bitcast(I32), in_=w4_words[0].bitcast(I32))
         nc.sync.dma_start(out=tab_w[:].bitcast(I32), in_=tab_words[0].rearrange("p n t -> p (n t)").bitcast(I32))
 
-        v_s_rows = keep("v_s_rows", [P, S], U8)
-        nc.vector.tensor_copy(v_s_rows[:], tab_s_rows[:].indirect(offsets[:]))
-        nc.vector.tensor_copy(out=rows[LAST_QUADRANT:P, 0:S].bitcast(I32), in_=v_s_rows[LAST_QUADRANT:P, :].bitcast(I32))
         nc.vector.tensor_copy(
             out=rows[:, S : S + H].rearrange("p (g t c m) -> p g c t m", g=GROUPS, t=PACK, m=16),
             in_=w4_s_rows[:].rearrange("p (g c m t) -> p g c t m", g=GROUPS, t=PACK, m=16),
         )
+        v_s_rows = keep("v_s_rows", [P, S], U8, "v_s_then_w1")
+        nc.vector.tensor_copy(v_s_rows[:], tab_s_rows[:].indirect(offsets[:]))
+        nc.vector.tensor_copy(out=rows[LAST_QUADRANT:P, 0:S].bitcast(I32), in_=v_s_rows[LAST_QUADRANT:P, :].bitcast(I32))
         for r in range(SCALE_ROWS):
             nc.sync.dma_start(out=planes[r:P:32, :].bitcast(I32), in_=rows[ROW0 + r : P : SCALE_ROWS, :].bitcast(I32))
-        w1_raw = [keep("w1_raw0", [P, PACK, PASS], F32, "w4_s_rows")]
+
+        w1_rows = w1.rearrange("(p i) r -> p i r", i=PACK)
+        w1_raw = [keep("w1_raw0", [P, PACK, PASS], F32, "v_s_then_w1")]
         nc.sync.dma_start(out=w1_raw[0][:], in_=w1_rows[:, :, 0:PASS])
 
-        v_w = [keep("v_w%d" % jh, [P, J], U32) for jh in range(HALVES)]
-        w4_w = keep("w4_w", [P, 2 * H], U8)
-
-        def gather_words(jh):
-            nc.vector.tensor_copy(v_w[jh][:], tab_w[:].indirect(offsets[:, jh * (J // 16) : (jh + 1) * (J // 16)]))
-
+        w4_w = keep("w4_w", [P, 2 * H], U8, "tab_s_then_w4")
         nc.vector.tensor_copy(
             out=w4_w[:].bitcast(U16).rearrange("p (g t c m) -> p g c t m", g=GROUPS, t=PACK, m=8),
             in_=w4_raw[:].bitcast(U16).rearrange("p (g c m t) -> p g c t m", g=GROUPS, t=PACK, m=8),
         )
-        w1_raw.append(keep("w1_raw1", [P, PACK, PASS], F32, "w4_then_w1"))
-        nc.sync.dma_start(out=w1_raw[1][:], in_=w1_rows[:, :, PASS : 2 * PASS])
-        for jh in range(HALVES):
-            gather_words(jh)
 
-        twice, size, halves, root, sign, flip = [
-            keep(n, [P, GROUPS * PACK], F32) for n in ("twice", "size", "halves", "root", "sign", "flip")
-        ]
+        twice = keep("twice", [P, GROUPS * PACK], F32, "w4_then_w1_then_drive")
+        size, halves, root, sign, flip = [keep(n, [P, GROUPS * PACK], F32) for n in ("size", "halves", "root", "sign", "flip")]
         nc.gpsimd.memset(halves[:], 0.5)
         nc.gpsimd.tensor_scalar(twice[:], cub_t[:], 0.0, 2.0, IS_GE, MULT)
         nc.gpsimd.tensor_scalar(sign[:], twice[:], 1.0, -1.0, MULT, ADD)
@@ -124,33 +115,40 @@ def tile_list_cavity_pulse_shaping_kernel(
         nc.gpsimd.tensor_tensor(size[:], cub_t[:], sign[:], MULT)
         nc.gpsimd.tensor_tensor(root[:], size[:], halves[:], POW)
 
+        w1_raw.append(keep("w1_raw1", [P, PACK, PASS], F32, "w4_then_w1_then_drive"))
+        nc.sync.dma_start(out=w1_raw[1][:], in_=w1_rows[:, :, PASS : 2 * PASS])
+        v_w = [keep("v_w%d" % jh, [P, J], U32) for jh in range(HALVES)]
+        for jh in range(HALVES):
+            nc.vector.tensor_copy(v_w[jh][:], tab_w[:].indirect(offsets[:, jh * (J // 16) : (jh + 1) * (J // 16)]))
+
         w1_w = [keep("w1_w%d" % g, [P, PASS], U32) for g in range(GROUPS)]
         w1_s = [keep("w1_s%d" % g, [P, PASS], U8) for g in range(GROUPS)]
 
-        def round_w1(g, pair, rounded, copy):
+        def round_w1(g, x, rounded, copy):
             copy(
-                out=rounded.rearrange("p (u m i) -> p m i u", u=2, i=PACK),
-                in_=w1_raw[g][:].rearrange("p i (m x u) -> p x m i u", x=2, u=2)[:, pair],
+                out=rounded.rearrange("p (y m i) -> p m i y", y=2, i=PACK),
+                in_=w1_raw[g][:].rearrange("p i (m x y) -> p x m i y", x=2, y=2)[:, x],
             )
 
         def quantise_w1(g, cols, rounded):
             nc.vector.quantize_mx(out=w1_w[g][:, cols].bitcast(FP8X4), scales=w1_s[g][:, cols], in_=rounded)
 
-        first = [keep("w1_bf0%d" % pair, [P, 2 * PASS], BF16, "w1_bf_then_drive" if pair else "table_then_w3") for pair in range(2)]
-        round_w1(0, 0, first[0][:], nc.vector.tensor_copy)
-        round_w1(0, 1, first[1][:], nc.scalar.copy)
-        for pair in range(2):
-            quantise_w1(0, slice(pair * 2 * P, (pair + 1) * 2 * P), first[pair][:])
+        w1_first = [keep("w1_bf00", [P, 2 * PASS], BF16, "table_then_w1_then_w3"), keep("w1_bf01", [P, 2 * PASS], BF16, "w1_then_w8")]
+        round_w1(0, 0, w1_first[0][:], nc.vector.tensor_copy)
+        round_w1(0, 1, w1_first[1][:], nc.scalar.copy)
+        for x in range(2):
+            quantise_w1(0, slice(x * 2 * P, (x + 1) * 2 * P), w1_first[x][:])
 
-        w3_raw = [keep("w3_raw0", [P, PACK, N], F32, "rows_then_w3"), keep("w3_raw1", [P, PACK, N], F32, "table_then_w3")]
+        w3_raw = [keep("w3_raw0", [P, PACK, N], F32, "rows_then_w3"), keep("w3_raw1", [P, PACK, N], F32, "table_then_w1_then_w3")]
         for g in range(GROUPS):
             nc.sync.dma_start(out=w3_raw[g][:], in_=w3[g * PASS : (g + 1) * PASS, :].rearrange("(p i) n -> p i n", i=PACK))
-        w8_w = keep("w8_w", [P, N], U32, "w1_bf_then_drive")
+        w8_w = keep("w8_w", [P, N], U32, "w1_then_w8")
         nc.sync.dma_start(out=w8_w[:].bitcast(I32), in_=w8_words[0].rearrange("p n t -> p (n t)").bitcast(I32))
 
         h = [keep("h%d" % g, [P, PACK, S], F32) for g in range(GROUPS)]
         h_w = [keep("h_w%d" % g, [P, S], U32) for g in range(GROUPS)]
         h_s = keep("h_s", [P, GROUPS, S], U8)
+        sums = [(g, t, jh) for g in range(GROUPS) for t in range(PACK) for jh in range(HALVES)]
 
         def shape(g, t, jh):
             e = bank(HALVES * t + jh)
@@ -160,15 +158,14 @@ def tile_list_cavity_pulse_shaping_kernel(
                 (w4_w[:, 2 * c0 : 2 * (c0 + P)].bitcast(FP4X4), w4_s[:, c0 : c0 + P]),
                 (w1_w[g][:, m0 : m0 + P].bitcast(FP8X4), w1_s[g][:, m0 : m0 + P]),
             ]
-            early = g > 0 or HALVES * t + jh < W4_FIRST
-            for n, (words, scales) in enumerate(weights if early else reversed(weights)):
+            opens_with_w4 = g > 0 or HALVES * t + jh < W4_FIRST
+            for n, (words, scales) in enumerate(weights if opens_with_w4 else reversed(weights)):
                 nc.tensor.matmul_mx(
                     out=e[:], lhsT=words, lhsT_scale=scales,
                     rhs=v_w[jh][:].bitcast(FP8X4), rhs_scale=v_s[:, half(jh)], start=(n == 0), stop=(n == 1),
                 )
             c = slice(g * PACK + t, g * PACK + t + 1)
-            tag = {(GROUPS - 1, PACK - 1, HALVES - 1): "u_then_w3"}.get((g, t, jh))
-            u = keep("u_own", [P, J], F32, tag) if tag else ring.tile([P, J], F32, name="u")
+            u = keep("u_last", [P, J], F32, "u_then_w3") if (g, t, jh) == sums[-1] else ring.tile([P, J], F32, name="u")
             nc.scalar.activation(u[:], e[:], SQUARE, scale=root[:, c])
             nc.vector.scalar_tensor_tensor(h[g][:, t, half(jh)], u[:], sign[:, c], e[:], SUB, MULT)
 
@@ -180,14 +177,13 @@ def tile_list_cavity_pulse_shaping_kernel(
             rows_of_h = out_1[g * PASS : (g + 1) * PASS, :].rearrange("(p t) j -> p t j", t=PACK)
             nc.sync.dma_start(out=rows_of_h, in_=h[g][:])
 
-        sums = [(g, t, jh) for g in range(GROUPS) for t in range(PACK) for jh in range(HALVES)]
-        second = keep("w1_bf1", [P, PACK * PASS], BF16)
-        for pair in range(2):
-            round_w1(1, pair, second[:, pair * 2 * PASS : (pair + 1) * 2 * PASS], nc.vector.tensor_copy)
-        y_rows = keep("y_rows", [P, NTILES, S], F32, "w4_then_w1")
+        w1_second = keep("w1_bf1", [P, PACK * PASS], BF16)
+        for x in range(2):
+            round_w1(1, x, w1_second[:, x * 2 * PASS : (x + 1) * 2 * PASS], nc.vector.tensor_copy)
+        y_rows = keep("y_rows", [P, NTILES, S], F32, "w4_then_w1_then_drive")
         nc.sync.dma_start(out=y_rows[:], in_=drive.rearrange("(a p) j -> p a j", p=P))
         shape(*sums[0])
-        quantise_w1(1, slice(0, PASS), second[:])
+        quantise_w1(1, slice(0, PASS), w1_second[:])
         for g, t, jh in sums[1:]:
             shape(g, t, jh)
             if jh == HALVES - 1 and g * PACK + t < GROUPS * PACK - TURNS_ON_VECTOR:
@@ -204,108 +200,100 @@ def tile_list_cavity_pulse_shaping_kernel(
                 in_=in_.rearrange("p t (c i) -> p c t i", i=NEIGHBOURS),
             )
 
-        def round_h(g, cols, copy):
-            rounded = keep("h_bf%d%d" % (g, cols.start), [P, J * PACK], BF16)
-            interleave(copy, rounded[:], h[g][:, :, cols])
+        def round_h(g, jh, on_scalar):
+            rounded = keep("h_bf%d%d" % (g, jh), [P, J * PACK], BF16)
+            interleave(nc.scalar.copy, rounded[:, 0 : on_scalar * PACK], h[g][:, :, jh * J : jh * J + on_scalar])
+            if on_scalar < J:
+                interleave(nc.vector.tensor_copy, rounded[:, on_scalar * PACK :], h[g][:, :, jh * J + on_scalar : (jh + 1) * J])
             return rounded
 
-        def quantise_h(g, cols, rounded):
-            nc.vector.quantize_mx(out=h_w[g][:, cols].bitcast(FP8X4), scales=h_s[:, g, cols], in_=rounded[:])
-
-        def store_words(g):
-            nc.sync.dma_start(out=out_2[g].rearrange("p m t -> p (m t)").bitcast(I32), in_=h_w[g][:].bitcast(I32))
-
-        def store_scales():
-            for r in range(SCALE_ROWS):
-                nc.sync.dma_start(
-                    out=out_3[:, r:ROWS:SCALE_ROWS, :].rearrange("g q m -> q g m").bitcast(I32), in_=h_s[r:P:32].bitcast(I32)
-                )
+        def quantise_h(g, jh, rounded):
+            nc.vector.quantize_mx(out=h_w[g][:, half(jh)].bitcast(FP8X4), scales=h_s[:, g, half(jh)], in_=rounded[:])
 
         w3_w = keep("w3_w", [P, GROUPS * N], U32)
         w3_s = keep("w3_s", [P, GROUPS * N], U8)
 
-        def round_w3(pieces, copy, tag):
-            rounded = keep("w3_bf%d" % pieces.start, [P, len(pieces) * PIECE * PACK], BF16, tag)
-            for x, piece in enumerate(pieces):
-                n0, g = piece // GROUPS * PIECE, piece % GROUPS
-                interleave(copy, rounded[:, x * PIECE * PACK : (x + 1) * PIECE * PACK], w3_raw[g][:, :, n0 : n0 + PIECE])
+        def round_w3(pair, copy, tag=None):
+            rounded = keep("w3_bf%d" % pair, [P, GROUPS * PAIR * PACK], BF16, tag)
+            for g in range(GROUPS):
+                interleave(copy, rounded[:, g * PAIR * PACK : (g + 1) * PAIR * PACK], w3_raw[g][:, :, pair * PAIR : (pair + 1) * PAIR])
             return rounded
 
-        def quantise_w3(pieces, rounded):
-            cols = slice(pieces.start * PIECE, pieces.stop * PIECE)
+        def quantise_w3(pair, rounded):
+            cols = slice(pair * GROUPS * PAIR, (pair + 1) * GROUPS * PAIR)
             nc.vector.quantize_mx(out=w3_w[:, cols].bitcast(FP8X4), scales=w3_s[:, cols], in_=rounded[:])
 
-        def w8_sum(a, jh, b):
-            tile_cols = slice(a * P, (a + 1) * P)
-            direct = bank(b)
-            nc.tensor.matmul_mx(
-                out=direct[:], lhsT=w8_w[:, tile_cols].bitcast(FP8X4), lhsT_scale=w8_s[:, tile_cols],
-                rhs=v_w[jh][:].bitcast(FP8X4), rhs_scale=v_s[:, half(jh)], start=True, stop=True,
+        h_rounded = {(g, jh): round_h(g, jh, J) for g, jh in ((0, 0), (0, 1), (1, 0))}
+        w3_first = round_w3(0, nc.vector.tensor_copy, "u_then_w3")
+        quantise_h(0, 0, h_rounded[0, 0])
+        quantise_w3(0, w3_first)
+        quantise_h(0, 1, h_rounded[0, 1])
+        h_rounded[1, 1] = round_h(1, 1, LAST_ON_SCALAR)
+        for jh in range(HALVES):
+            quantise_h(1, jh, h_rounded[1, jh])
+        for g in range(GROUPS):
+            nc.sync.dma_start(out=out_2[g].rearrange("p m t -> p (m t)").bitcast(I32), in_=h_w[g][:].bitcast(I32))
+        for r in range(SCALE_ROWS):
+            nc.sync.dma_start(
+                out=out_3[:, r:ROWS:SCALE_ROWS, :].rearrange("g q m -> q g m").bitcast(I32), in_=h_s[r:P:32].bitcast(I32)
             )
-            return direct
-
-        w8_banks = {4: [], 6: []}
-
-        def next_w8_bank(b0):
-            w8_banks[b0].append(b0 + len(w8_banks[b0]) % 2)
-            return w8_banks[b0][-1]
+        for pair in range(1, N // PAIR):
+            quantise_w3(pair, round_w3(pair, nc.scalar.copy))
 
         steps = [(a, jh) for a in range(NTILES) for jh in range(HALVES)]
-        by_gpsimd = [steps[n] for n in BY_GPSIMD]
-        parked = {}
 
-        def park(some):
-            for a, jh in some:
-                parked[a, jh] = keep("parked%d%d" % (jh, a), [P, J], F32)
-                nc.scalar.copy(out=parked[a, jh][:], in_=w8_sum(a, jh, next_w8_bank(4))[:])
+        def w8_sum(n, b):
+            a, jh = steps[n]
+            tile_cols = slice(a * P, (a + 1) * P)
+            total = bank(b)
+            nc.tensor.matmul_mx(
+                out=total[:], lhsT=w8_w[:, tile_cols].bitcast(FP8X4), lhsT_scale=w8_s[:, tile_cols],
+                rhs=v_w[jh][:].bitcast(FP8X4), rhs_scale=v_s[:, half(jh)], start=True, stop=True,
+            )
+            return total
+
+        direct, parked = {}, {}
+        for x, n in enumerate(BY_GPSIMD):
+            width = LAST_ON_GPSIMD if n == BY_GPSIMD[-1] else J
+            direct[n] = w8_sum(n, PARK_BANK + x % 2)
+            parked[n] = keep("parked%d" % n, [P, width], F32)
+            nc.scalar.copy(out=parked[n][:], in_=direct[n][:, 0:width])
+        by_vector = [n for n in range(len(steps)) if n not in BY_GPSIMD]
 
         out_v = out_0.rearrange("(a p) j -> p a j", p=P)
         driven = {}
 
-        def drive_tile(n):
+        def drive_step(n):
             a, jh = steps[n]
-            shaped = bank(n % 4)
+            shaped = bank(n % W3_BANKS)
             for g in range(GROUPS):
-                c0 = (a * P // PIECE * GROUPS + g) * PIECE + a * P % PIECE
-                tile_cols = slice(c0, c0 + P)
+                c0 = (a // 2 * GROUPS + g) * PAIR + a % 2 * P
                 nc.tensor.matmul_mx(
-                    out=shaped[:], lhsT=w3_w[:, tile_cols].bitcast(FP8X4), lhsT_scale=w3_s[:, tile_cols],
+                    out=shaped[:], lhsT=w3_w[:, c0 : c0 + P].bitcast(FP8X4), lhsT_scale=w3_s[:, c0 : c0 + P],
                     rhs=h_w[g][:, half(jh)].bitcast(FP8X4), rhs_scale=h_s[:, g, half(jh)],
                     start=(g == 0), stop=(g == GROUPS - 1),
                 )
             driven[n] = ring.tile([P, J], F32, name="driven")
             nc.vector.tensor_tensor(driven[n][:], shaped[:], y_rows[:, a, half(jh)], MULT)
 
-        def add_w8_sum(n):
+        def add_step(n):
             a, jh = steps[n]
             y = y_rows[:, a, half(jh)]
-            if (a, jh) in by_gpsimd:
-                nc.gpsimd.tensor_tensor(y, parked[a, jh][:], driven[n][:], ADD)
+            if n in by_vector:
+                nc.vector.tensor_tensor(y, w8_sum(n, ADD_BANK + by_vector.index(n) % 2)[:], driven[n][:], ADD)
+            elif n == BY_GPSIMD[-1]:
+                x = LAST_ON_GPSIMD
+                nc.gpsimd.tensor_tensor(y[:, 0:x], parked[n][:], driven[n][:, 0:x], ADD)
+                nc.vector.tensor_tensor(y[:, x:J], direct[n][:, x:J], driven[n][:, x:J], ADD)
             else:
-                nc.vector.tensor_tensor(y, w8_sum(a, jh, next_w8_bank(6))[:], driven[n][:], ADD)
+                nc.gpsimd.tensor_tensor(y, parked[n][:], driven[n][:], ADD)
             if a == NTILES - 1:
                 nc.sync.dma_start(out=out_v[:, a, half(jh)], in_=y)
             elif jh == HALVES - 1:
                 nc.sync.dma_start(out=out_v[:, a, :], in_=y_rows[:, a, :])
 
-        h00, h01, h10 = [round_h(g, half(jh), nc.scalar.copy) for g, jh in ((0, 0), (0, 1), (1, 0))]
-        w3_first = round_w3(range(0, 2), nc.vector.tensor_copy, "u_then_w3")
-        quantise_h(0, half(0), h00)
-        quantise_w3(range(0, 2), w3_first)
-        quantise_h(0, half(1), h01)
-        h11 = keep("h_bf_last", [P, J * PACK], BF16)
-        for x, copy in ((0, nc.scalar.copy), (PIECE, nc.vector.tensor_copy)):
-            interleave(copy, h11[:, x * PACK : (x + PIECE) * PACK], h[1][:, :, J + x : J + x + PIECE])
-        quantise_h(1, half(0), h10)
-        quantise_h(1, half(1), h11)
-        for g in range(GROUPS):
-            store_words(g)
-        store_scales()
-        quantise_w3(range(2, 4), round_w3(range(2, 4), nc.scalar.copy, None))
-        quantise_w3(range(4, 6), round_w3(range(4, 6), nc.scalar.copy, None))
-        park(by_gpsimd)
-        drive_tile(0)
+        drive_step(0)
         for n in range(1, len(steps)):
-            drive_tile(n)
-            add_w8_sum(n - 1)
-        add_w8_sum(len(steps) - 1)
+            drive_step(n)
+            add_step(n - 1)
+        add_step(len(steps) - 1)

@@ -38,8 +38,7 @@ PAIR = 2 * P
 W4_FIRST = 4
 TURNS_ON_VECTOR = 3
 LAST_ON_SCALAR = 128
-BY_GPSIMD = (2, 3, 4, 6, 8, 10)
-LAST_ON_GPSIMD = 256
+BY_GPSIMD = (2, 3, 6, 8, 10)
 W3_BANKS, PARK_BANK, ADD_BANK = 4, 4, 6
 RING = 6
 
@@ -237,8 +236,7 @@ def tile_list_cavity_pulse_shaping_kernel(
             nc.sync.dma_start(
                 out=out_3[:, r:ROWS:SCALE_ROWS, :].rearrange("g q m -> q g m").bitcast(I32), in_=h_s[r:P:32].bitcast(I32)
             )
-        for pair in range(1, N // PAIR):
-            quantise_w3(pair, round_w3(pair, nc.scalar.copy))
+        w3_late = {1: round_w3(1, nc.scalar.copy), 2: round_w3(2, nc.scalar.copy, "w3_then_y")}
 
         steps = [(a, jh) for a in range(NTILES) for jh in range(HALVES)]
 
@@ -252,12 +250,10 @@ def tile_list_cavity_pulse_shaping_kernel(
             )
             return total
 
-        direct, parked = {}, {}
+        parked = {}
         for x, n in enumerate(BY_GPSIMD):
-            width = LAST_ON_GPSIMD if n == BY_GPSIMD[-1] else J
-            direct[n] = w8_sum(n, PARK_BANK + x % 2)
-            parked[n] = keep("parked%d" % n, [P, width], F32)
-            nc.scalar.copy(out=parked[n][:], in_=direct[n][:, 0:width])
+            parked[n] = keep("parked%d" % n, [P, J], F32)
+            nc.scalar.copy(out=parked[n][:], in_=w8_sum(n, PARK_BANK + x % 2)[:])
         by_vector = [n for n in range(len(steps)) if n not in BY_GPSIMD]
 
         out_v = out_0.rearrange("(a p) j -> p a j", p=P)
@@ -278,22 +274,28 @@ def tile_list_cavity_pulse_shaping_kernel(
 
         def add_step(n):
             a, jh = steps[n]
-            y = y_rows[:, a, half(jh)]
+            y_tile = y_second[:] if a == 1 else y_rows[:, a, :]
+            y = y_tile[:, half(jh)]
             if n in by_vector:
                 nc.vector.tensor_tensor(y, w8_sum(n, ADD_BANK + by_vector.index(n) % 2)[:], driven[n][:], ADD)
-            elif n == BY_GPSIMD[-1]:
-                x = LAST_ON_GPSIMD
-                nc.gpsimd.tensor_tensor(y[:, 0:x], parked[n][:], driven[n][:, 0:x], ADD)
-                nc.vector.tensor_tensor(y[:, x:J], direct[n][:, x:J], driven[n][:, x:J], ADD)
             else:
                 nc.gpsimd.tensor_tensor(y, parked[n][:], driven[n][:], ADD)
             if a == NTILES - 1:
                 nc.sync.dma_start(out=out_v[:, a, half(jh)], in_=y)
             elif jh == HALVES - 1:
-                nc.sync.dma_start(out=out_v[:, a, :], in_=y_rows[:, a, :])
+                nc.sync.dma_start(out=out_v[:, a, :], in_=y_tile)
 
         drive_step(0)
-        for n in range(1, len(steps)):
+        drive_step(1)
+        add_step(0)
+        quantise_w3(1, w3_late[1])
+        drive_step(2)
+        add_step(1)
+        drive_step(3)
+        quantise_w3(2, w3_late[2])
+        y_second = keep("y_second", [P, S], F32, "w3_then_y")
+        add_step(2)
+        for n in range(4, len(steps)):
             drive_step(n)
             add_step(n - 1)
         add_step(len(steps) - 1)

from contextlib import ExitStack

import concourse.mybir as mybir

K, H, N, T, S = 512, 1024, 768, 4096, 1024
FLOPS = 2 * S * (2 * K * H + H * N + K * N)

F32 = mybir.dt.float32
BF16 = mybir.dt.bfloat16
I32 = mybir.dt.int32
U32 = mybir.dt.uint32
U16 = mybir.dt.uint16
U8 = mybir.dt.uint8
FP8X4 = mybir.dt.float8_e4m3fn_x4
FP4X4 = mybir.dt.float4_e2m1fn_x4
MULT = mybir.AluOpType.mult
ADD = mybir.AluOpType.add
SUB = mybir.AluOpType.subtract
POW = mybir.AluOpType.pow
IS_GE = mybir.AluOpType.is_ge
SQUARE = mybir.ActivationFunctionType.Square

P = 128
PACK = 4
PASS = P * PACK
GROUPS = H // PASS
J = 512
HALVES = S // J
NTILES = N // P
QUADRANTS = 4
SCALE_ROWS = 4
ROWS = QUADRANTS * SCALE_ROWS
ROW0 = P - ROWS
LAST_QUADRANT = P - 32
NEIGHBOURS = 4
PAIR = 2 * P

W4_FIRST = 4
TURNS_ON_VECTOR = 3
LAST_ON_SCALAR = 128
BY_GPSIMD = (2, 3, 6, 8, 10)
W3_BANKS, PARK_BANK, ADD_BANK = 4, 4, 6
RING = 6


def tile_list_cavity_pulse_shaping_kernel(
    tc, tab_words, tab_scales, offs, w1, w4_words, w4_scales, cub, w3, drive, w8_words, w8_scales, out_0, out_1, out_2, out_3
):
    nc = tc.nc
    with ExitStack() as ctx:
        held = ctx.enter_context(tc.tile_pool(name="held", bufs=1))
        ring = ctx.enter_context(tc.tile_pool(name="ring", bufs=RING))
        psum = ctx.enter_context(tc.psum_pool(name="psum", bufs=1))

        def bank(b):
            return psum.tile([P, J], F32, name="bank%d" % b)

        def keep(name, shape, dtype, tag=None):
            return held.tile(shape, dtype, name=name, tag=tag or name, align_bytes=64)

        def half(jh):
            return slice(jh * J, (jh + 1) * J)

        offsets = held.tile([P, S // 16], U16, name="offsets")
        tab_s_rows = keep("tab_s_rows", [P, T], U8, "tab_s_then_w4")
        w4_s_rows = keep("w4_s_rows", [P, H], U8)
        rows = keep("rows", [P, S + H + N], U8, "rows_then_w3")
        planes = keep("planes", [P, S + H + N], U8)
        v_s, w4_s, w8_s = planes[:, 0:S], planes[:, S : S + H], planes[:, S + H : S + H + N]
        tab_w = keep("tab_w", [P, T], U32, "table_then_w1_then_w3")
        w4_raw = keep("w4_raw", [P, 2 * H], U8, "w4_then_w1_then_drive")
        cub_t = keep("cub_t", [P, GROUPS * PACK], F32)

        nc.vector.memset(tab_s_rows[0:ROW0, :].bitcast(I32), 0)
        nc.vector.memset(w4_s_rows[0:ROW0, :].bitcast(I32), 0)
        nc.vector.memset(planes[:].bitcast(I32), 0)

        nc.sync.dma_start(out=w4_s_rows[ROW0:P, :].bitcast(I32), in_=w4_scales[0].bitcast(I32))
        nc.sync.dma_start(out=tab_s_rows[ROW0:P, :].bitcast(I32), in_=tab_scales[0].bitcast(I32))
        nc.sync.dma_start(offsets[:], offs)
        nc.sync.dma_start(out=rows[ROW0:P, S + H : S + H + N].bitcast(I32), in_=w8_scales[0].bitcast(I32))
        nc.sync.dma_start(
            out=cub_t[:].rearrange("p (g t) -> p g t", t=PACK), in_=cub.rearrange("(g p t) -> p g t", g=GROUPS, t=PACK)
        )
        nc.sync.dma_start(out=w4_raw[:].bitcast(I32), in_=w4_words[0].bitcast(I32))
        nc.sync.dma_start(out=tab_w[:].bitcast(I32), in_=tab_words[0].rearrange("p n t -> p (n t)").bitcast(I32))

        nc.vector.tensor_copy(
            out=rows[:, S : S + H].rearrange("p (g t c m) -> p g c t m", g=GROUPS, t=PACK, m=16),
            in_=w4_s_rows[:].rearrange("p (g c m t) -> p g c t m", g=GROUPS, t=PACK, m=16),
        )
        v_s_rows = keep("v_s_rows", [P, S], U8, "v_s_then_w1")
        nc.vector.tensor_copy(v_s_rows[:], tab_s_rows[:].indirect(offsets[:]))
        nc.vector.tensor_copy(out=rows[LAST_QUADRANT:P, 0:S].bitcast(I32), in_=v_s_rows[LAST_QUADRANT:P, :].bitcast(I32))
        for r in range(SCALE_ROWS):
            nc.sync.dma_start(out=planes[r:P:32, :].bitcast(I32), in_=rows[ROW0 + r : P : SCALE_ROWS, :].bitcast(I32))

        w1_rows = w1.rearrange("(p i) r -> p i r", i=PACK)
        w1_raw = [keep("w1_raw0", [P, PACK, PASS], F32, "v_s_then_w1")]
        nc.sync.dma_start(out=w1_raw[0][:], in_=w1_rows[:, :, 0:PASS])

        w4_w = keep("w4_w", [P, 2 * H], U8, "tab_s_then_w4")
        nc.vector.tensor_copy(
            out=w4_w[:].bitcast(U16).rearrange("p (g t c m) -> p g c t m", g=GROUPS, t=PACK, m=8),
            in_=w4_raw[:].bitcast(U16).rearrange("p (g c m t) -> p g c t m", g=GROUPS, t=PACK, m=8),
        )

        twice = keep("twice", [P, GROUPS * PACK], F32, "w4_then_w1_then_drive")
        size, halves, root, sign, flip = [keep(n, [P, GROUPS * PACK], F32) for n in ("size", "halves", "root", "sign", "flip")]
        nc.gpsimd.memset(halves[:], 0.5)
        nc.gpsimd.tensor_scalar(twice[:], cub_t[:], 0.0, 2.0, IS_GE, MULT)
        nc.gpsimd.tensor_scalar(sign[:], twice[:], 1.0, -1.0, MULT, ADD)
        nc.gpsimd.tensor_scalar(flip[:], twice[:], -1.0, 1.0, MULT, ADD)
        nc.gpsimd.tensor_tensor(size[:], cub_t[:], sign[:], MULT)
        nc.gpsimd.tensor_tensor(root[:], size[:], halves[:], POW)

        w1_raw.append(keep("w1_raw1", [P, PACK, PASS], F32, "w4_then_w1_then_drive"))
        nc.sync.dma_start(out=w1_raw[1][:], in_=w1_rows[:, :, PASS : 2 * PASS])
        v_w = [keep("v_w%d" % jh, [P, J], U32) for jh in range(HALVES)]
        for jh in range(HALVES):
            nc.vector.tensor_copy(v_w[jh][:], tab_w[:].indirect(offsets[:, jh * (J // 16) : (jh + 1) * (J // 16)]))

        w1_w = [keep("w1_w%d" % g, [P, PASS], U32) for g in range(GROUPS)]
        w1_s = [keep("w1_s%d" % g, [P, PASS], U8) for g in range(GROUPS)]

        def round_w1(g, x, rounded, copy):
            copy(
                out=rounded.rearrange("p (y m i) -> p m i y", y=2, i=PACK),
                in_=w1_raw[g][:].rearrange("p i (m x y) -> p x m i y", x=2, y=2)[:, x],
            )

        def quantise_w1(g, cols, rounded):
            nc.vector.quantize_mx(out=w1_w[g][:, cols].bitcast(FP8X4), scales=w1_s[g][:, cols], in_=rounded)

        w1_first = [keep("w1_bf00", [P, 2 * PASS], BF16, "table_then_w1_then_w3"), keep("w1_bf01", [P, 2 * PASS], BF16, "w1_then_w8")]
        round_w1(0, 0, w1_first[0][:], nc.vector.tensor_copy)
        round_w1(0, 1, w1_first[1][:], nc.scalar.copy)
        for x in range(2):
            quantise_w1(0, slice(x * 2 * P, (x + 1) * 2 * P), w1_first[x][:])

        w3_raw = [keep("w3_raw0", [P, PACK, N], F32, "rows_then_w3"), keep("w3_raw1", [P, PACK, N], F32, "table_then_w1_then_w3")]
        for g in range(GROUPS):
            nc.sync.dma_start(out=w3_raw[g][:], in_=w3[g * PASS : (g + 1) * PASS, :].rearrange("(p i) n -> p i n", i=PACK))
        w8_w = keep("w8_w", [P, N], U32, "w1_then_w8")
        nc.sync.dma_start(out=w8_w[:].bitcast(I32), in_=w8_words[0].rearrange("p n t -> p (n t)").bitcast(I32))

        h = [keep("h%d" % g, [P, PACK, S], F32) for g in range(GROUPS)]
        h_w = [keep("h_w%d" % g, [P, S], U32) for g in range(GROUPS)]
        h_s = keep("h_s", [P, GROUPS, S], U8)
        sums = [(g, t, jh) for g in range(GROUPS) for t in range(PACK) for jh in range(HALVES)]

        def shape(g, t, jh):
            e = bank(HALVES * t + jh)
            m0 = t * P
            c0 = g * PASS + m0
            weights = [
                (w4_w[:, 2 * c0 : 2 * (c0 + P)].bitcast(FP4X4), w4_s[:, c0 : c0 + P]),
                (w1_w[g][:, m0 : m0 + P].bitcast(FP8X4), w1_s[g][:, m0 : m0 + P]),
            ]
            opens_with_w4 = g > 0 or HALVES * t + jh < W4_FIRST
            for n, (words, scales) in enumerate(weights if opens_with_w4 else reversed(weights)):
                nc.tensor.matmul_mx(
                    out=e[:], lhsT=words, lhsT_scale=scales,
                    rhs=v_w[jh][:].bitcast(FP8X4), rhs_scale=v_s[:, half(jh)], start=(n == 0), stop=(n == 1),
                )
            c = slice(g * PACK + t, g * PACK + t + 1)
            u = keep("u_last", [P, J], F32, "u_then_w3") if (g, t, jh) == sums[-1] else ring.tile([P, J], F32, name="u")
            nc.scalar.activation(u[:], e[:], SQUARE, scale=root[:, c])
            nc.vector.scalar_tensor_tensor(h[g][:, t, half(jh)], u[:], sign[:, c], e[:], SUB, MULT)

        def turn(g, t, engine):
            c = slice(g * PACK + t, g * PACK + t + 1)
            engine.tensor_scalar(h[g][:, t, :], h[g][:, t, :], flip[:, c], 0.0, MULT, ADD)

        def store_h(g):
            rows_of_h = out_1[g * PASS : (g + 1) * PASS, :].rearrange("(p t) j -> p t j", t=PACK)
            nc.sync.dma_start(out=rows_of_h, in_=h[g][:])

        w1_second = keep("w1_bf1", [P, PACK * PASS], BF16)
        for x in range(2):
            round_w1(1, x, w1_second[:, x * 2 * PASS : (x + 1) * 2 * PASS], nc.vector.tensor_copy)
        y_rows = keep("y_rows", [P, NTILES, S], F32, "w4_then_w1_then_drive")
        nc.sync.dma_start(out=y_rows[:], in_=drive.rearrange("(a p) j -> p a j", p=P))
        shape(*sums[0])
        quantise_w1(1, slice(0, PASS), w1_second[:])
        for g, t, jh in sums[1:]:
            shape(g, t, jh)
            if jh == HALVES - 1 and g * PACK + t < GROUPS * PACK - TURNS_ON_VECTOR:
                turn(g, t, nc.gpsimd)
                if t == PACK - 1:
                    store_h(g)
        for t in range(PACK - TURNS_ON_VECTOR, PACK):
            turn(GROUPS - 1, t, nc.vector)
        store_h(GROUPS - 1)

        def interleave(copy, out, in_):
            copy(
                out=out.rearrange("p (c i t) -> p c t i", i=NEIGHBOURS, t=PACK),
                in_=in_.rearrange("p t (c i) -> p c t i", i=NEIGHBOURS),
            )

        def round_h(g, jh, on_scalar):
            rounded = keep("h_bf%d%d" % (g, jh), [P, J * PACK], BF16)
            interleave(nc.scalar.copy, rounded[:, 0 : on_scalar * PACK], h[g][:, :, jh * J : jh * J + on_scalar])
            if on_scalar < J:
                interleave(nc.vector.tensor_copy, rounded[:, on_scalar * PACK :], h[g][:, :, jh * J + on_scalar : (jh + 1) * J])
            return rounded

        def quantise_h(g, jh, rounded):
            nc.vector.quantize_mx(out=h_w[g][:, half(jh)].bitcast(FP8X4), scales=h_s[:, g, half(jh)], in_=rounded[:])

        w3_w = keep("w3_w", [P, GROUPS * N], U32)
        w3_s = keep("w3_s", [P, GROUPS * N], U8)

        def round_w3(pair, copy, tag=None):
            rounded = keep("w3_bf%d" % pair, [P, GROUPS * PAIR * PACK], BF16, tag)
            for g in range(GROUPS):
                interleave(copy, rounded[:, g * PAIR * PACK : (g + 1) * PAIR * PACK], w3_raw[g][:, :, pair * PAIR : (pair + 1) * PAIR])
            return rounded

        def quantise_w3(pair, rounded):
            cols = slice(pair * GROUPS * PAIR, (pair + 1) * GROUPS * PAIR)
            nc.vector.quantize_mx(out=w3_w[:, cols].bitcast(FP8X4), scales=w3_s[:, cols], in_=rounded[:])

        h_rounded = {(g, jh): round_h(g, jh, J) for g, jh in ((0, 0), (0, 1), (1, 0))}
        w3_first = round_w3(0, nc.vector.tensor_copy, "u_then_w3")
        quantise_h(0, 0, h_rounded[0, 0])
        quantise_w3(0, w3_first)
        quantise_h(0, 1, h_rounded[0, 1])
        h_rounded[1, 1] = round_h(1, 1, LAST_ON_SCALAR)
        for jh in range(HALVES):
            quantise_h(1, jh, h_rounded[1, jh])
        for g in range(GROUPS):
            nc.sync.dma_start(out=out_2[g].rearrange("p m t -> p (m t)").bitcast(I32), in_=h_w[g][:].bitcast(I32))
        for r in range(SCALE_ROWS):
            nc.sync.dma_start(
                out=out_3[:, r:ROWS:SCALE_ROWS, :].rearrange("g q m -> q g m").bitcast(I32), in_=h_s[r:P:32].bitcast(I32)
            )
        w3_late = {1: round_w3(1, nc.scalar.copy), 2: round_w3(2, nc.scalar.copy, "w3_then_y")}

        steps = [(a, jh) for a in range(NTILES) for jh in range(HALVES)]

        def w8_sum(n, b):
            a, jh = steps[n]
            tile_cols = slice(a * P, (a + 1) * P)
            total = bank(b)
            nc.tensor.matmul_mx(
                out=total[:], lhsT=w8_w[:, tile_cols].bitcast(FP8X4), lhsT_scale=w8_s[:, tile_cols],
                rhs=v_w[jh][:].bitcast(FP8X4), rhs_scale=v_s[:, half(jh)], start=True, stop=True,
            )
            return total

        parked = {}
        for x, n in enumerate(BY_GPSIMD):
            parked[n] = keep("parked%d" % n, [P, J], F32)
            nc.scalar.copy(out=parked[n][:], in_=w8_sum(n, PARK_BANK + x % 2)[:])
        by_vector = [n for n in range(len(steps)) if n not in BY_GPSIMD]

        out_v = out_0.rearrange("(a p) j -> p a j", p=P)
        driven = {}

        def drive_step(n):
            a, jh = steps[n]
            shaped = bank(n % W3_BANKS)
            for g in range(GROUPS):
                c0 = (a // 2 * GROUPS + g) * PAIR + a % 2 * P
                nc.tensor.matmul_mx(
                    out=shaped[:], lhsT=w3_w[:, c0 : c0 + P].bitcast(FP8X4), lhsT_scale=w3_s[:, c0 : c0 + P],
                    rhs=h_w[g][:, half(jh)].bitcast(FP8X4), rhs_scale=h_s[:, g, half(jh)],
                    start=(g == 0), stop=(g == GROUPS - 1),
                )
            driven[n] = ring.tile([P, J], F32, name="driven")
            nc.vector.tensor_tensor(driven[n][:], shaped[:], y_rows[:, a, half(jh)], MULT)

        def add_step(n):
            a, jh = steps[n]
            y_tile = y_second[:] if a == 1 else y_rows[:, a, :]
            y = y_tile[:, half(jh)]
            if n in by_vector:
                nc.vector.tensor_tensor(y, w8_sum(n, ADD_BANK + by_vector.index(n) % 2)[:], driven[n][:], ADD)
            else:
                nc.gpsimd.tensor_tensor(y, parked[n][:], driven[n][:], ADD)
            if a == NTILES - 1:
                nc.sync.dma_start(out=out_v[:, a, half(jh)], in_=y)
            elif jh == HALVES - 1:
                nc.sync.dma_start(out=out_v[:, a, :], in_=y_tile)

        drive_step(0)
        drive_step(1)
        add_step(0)
        quantise_w3(1, w3_late[1])
        drive_step(2)
        add_step(1)
        drive_step(3)
        quantise_w3(2, w3_late[2])
        y_second = keep("y_second", [P, S], F32, "w3_then_y")
        add_step(2)
        for n in range(4, len(steps)):
            drive_step(n)
            add_step(n - 1)
        add_step(len(steps) - 1)
